import numpy as np, ml_dtypes
CORES = [5,29,101,125,133,157,229,253]
N = 8
BF = ml_dtypes.bfloat16
def gentries(a):
    return np.ascontiguousarray(a.reshape(8, 16, -1).transpose(0, 2, 1)).reshape(8, -1)
def gtable(e):
    e = np.asarray(e); return np.ascontiguousarray(e.reshape(8, -1, 16).transpose(0, 2, 1)).reshape(128, -1).astype(np.int32)
W, M, L, D, S = 2048, 4096, 128, 16, 4
K = L * D
def cols(rng, n):
    base = rng.integers(0, 256, (N, 8, 1, n)); amp = rng.integers(0, 129, (N, 8, 1, n))
    return np.clip(np.rint(base + amp * (2.0 * rng.random((N, 8, 16, n)) - 1.0)), 0, 255).astype(np.int64)
def parts(rng):
    X, Z = cols(rng, W), cols(rng, L)
    P = rng.integers(0, W, (N, 8, M)); V = rng.integers(0, W, (N, 8, K)); pool = rng.integers(0, M, (N, 8, 256))
    O = np.where(rng.random((N, 8, K)) < 0.5, rng.integers(0, M, (N, 8, K)), np.take_along_axis(pool, rng.integers(0, 256, (N, 8, K)), 2))
    c = rng.random((N, 8, K)); T = np.where(c < 0.45, rng.integers(0, S + 2, (N, 8, K)), np.where(c < 0.85, 99, rng.integers(0, 99, (N, 8, K))))
    return X, Z, P, O, V, T, rng.integers(200, 3400, (N, 8, S))
def pack(X, Z, P, O, V, T, th):
    return {"x": np.ascontiguousarray(X).reshape(N, 128, W).astype(np.float32).astype(BF), "z": np.ascontiguousarray(Z).reshape(N, 128, L).astype(np.float32).astype(BF), "px": P.astype(np.int32),
            "ol": np.stack([gtable(a) for a in O]), "nl": np.stack([gtable(a) for a in V]), "tl": np.stack([gtable(a) for a in T]), "th": th.astype(np.int32)}
def setup_inputs(rng):
    return pack(*parts(rng))
def setup_inputs_spread(rng):
    X = (np.exp2(8 * rng.random((N, 8, 1, W))) * rng.random((N, 8, 16, W))).astype(np.int64); Z = (np.exp2(8 * rng.random((N, 8, 1, L))) * rng.random((N, 8, 16, L))).astype(np.int64)
    e = rng.integers(1, 5, (3, N, 8, 1))
    P = (W * rng.random((N, 8, M)) ** e[0]).astype(np.int64); O = (M * rng.random((N, 8, K)) ** e[1]).astype(np.int64); V = (W * rng.random((N, 8, K)) ** e[2]).astype(np.int64)
    T = np.where(rng.random((N, 8, K)) < 0.3, 99, (100 * rng.random((N, 8, K)) ** 4).astype(np.int64)); th = (4081 * rng.random((N, 8, S)) ** 2).astype(np.int64)
    return pack(X, Z, P, O, V, T, th)
def setup_inputs_ends(rng):
    def ends(n):
        m = rng.integers(0, 3, (N, 8, 1, n)); return np.where(m == 2, 255 * rng.integers(0, 2, (N, 8, 16, n)), 255 * np.minimum(m, 1)) + np.zeros((N, 8, 16, n), np.int64)
    X, Z = ends(W), ends(L); X[..., 0] = 0; X[..., W - 1] = 255
    P = (W - 1) * rng.integers(0, 2, (N, 8, M)); O = (M - 1) * rng.integers(0, 2, (N, 8, K)); V = (W - 1) * rng.integers(0, 2, (N, 8, K)); T = 99 * rng.integers(0, 2, (N, 8, K))
    th = 4080 * rng.integers(0, 2, (N, 8, S)); th[:, 0, 0] = 0; th[:, 1, 0] = 4080; th[0, 7, 0] = 0; th[N - 1, 7, 0] = 4080
    star = int(np.argmax(((37 * np.arange(M)) & (W - 1)) == W - 1))
    for pair, v, n, o, ks in (((0, L - 1), 0, 0, star, (0, 1, D - 1)), ((1, L - 2), 255, W - 1, star, (0, 1, D - 1)), ((2, L - 3), 0, W - 1, M - 1, (0, 3, D - 1))):
        for l in pair:
            Z[..., l] = v
            for k in ks: V[..., k * L + l] = n; T[..., k * L + l] = 0; O[..., k * L + l] = o
    return pack(X, Z, P, O, V, T, th)
def setup_inputs_corners(rng):
    X, Z, P, O, V, T, th = parts(rng)
    th = np.where(rng.random((N, 8, S)) < 0.5, 4080 * rng.integers(0, 2, (N, 8, S)), th)
    for a in range(N):
        ct, cp, co, cv, cz = [rng.permutation(8) for i in range(5)]
        for g in range(8):
            T[a, g] = rng.choice(np.array(((0,), (99,), (98,), (S,), (S - 1,), (0, 98), (1, 2, 99), (0, 1, 2, S - 1, S, S + 1, 98, 99))[ct[g]]), K)
            if cp[g] < 5: P[a, g] = (np.arange(M) & (W - 1), np.zeros(M, np.int64), np.full(M, W - 1), W - 1 - (np.arange(M) & (W - 1)), rng.choice(np.array([0, W - 1]), M))[cp[g]]
            if co[g] < 4: O[a, g] = (np.zeros(K, np.int64), np.full(K, M - 1), rng.choice(np.array([0, M - 1]), K), np.arange(K))[co[g]]
            if cv[g] < 4: V[a, g] = (np.zeros(K, np.int64), np.full(K, W - 1), rng.choice(np.array([0, W - 1]), K), np.arange(K) & (W - 1))[cv[g]]
            if cz[g] < 2: Z[a, g] = 255 * cz[g]
    e = int(rng.integers(0, 8)); X[:, e] = 255; Z[:, e] = 0; Z[:, e, 0, 1::2] = 1; th[:, e, 0] = 4079
    O[:, e, 1::2] = 32 * (M // 32 - 1 - rng.integers(0, 8, (N, K // 2))) + 17
    return pack(X, Z, P, O, V, T, th)
def setup_inputs_crowd(rng):
    X, Z, P, O, V, T, th = parts(rng); pm = rng.permutation(8)
    for g in range(8):
        c = int(pm[g])
        if c < 2: th[:, g] = 4080; T[:, g] = 99
        if c == 2 or c == 3: th[:, g] = 0
        if c == 4 or c == 5: X[:, g, :, 0] = 0; th[:, g] = rng.integers(100, 1500, (N, S))
        for a in range(N):
            one = int(rng.integers(1, L)); p = int(rng.integers(0, M))
            if c == 1: T[a, g, int(rng.integers(0, K))] = 98
            if 2 <= c < 6: O[a, g] = p
            if c == 4 or c == 5:
                V[a, g] = 0; T[a, g] = 0; v = rng.integers(0, 256, 16); v[0] = 255; v[1] = 0
                Z[a, g] = v[np.argsort(rng.random((16, L)), axis=0)]
            if c == 3 or c == 5: O[a, g, one::L] = (p + 1 + int(rng.integers(0, M - 1))) % M
            if c == 5: Z[a, g, :, one] = rng.integers(0, 256, 16)
            if c == 6:
                l = np.arange(K) % L; w = rng.integers(0, M, L); n = int(rng.integers(0, W)); O[a, g] = w[np.minimum(l, L - 1 - l)]; V[a, g] = n; T[a, g] = 0; X[a, g, :, n] = 0
                Z[a, g, 0] = 255; Z[a, g, 15] = 0; v = Z[a, g][:, np.minimum(np.arange(L), L - 1 - np.arange(L))]
                Z[a, g] = np.where(np.arange(L) < L // 2, v, v[::-1])
            if c == 7: O[a, g] = rng.choice(rng.integers(0, M, 4), K)
    return pack(X, Z, P, O, V, T, th)
def setup_inputs_ties(rng):
    X, Z, P, O, V, T, th = parts(rng)
    pat = 64 * rng.integers(0, 4, (N, 8, 16, 8)); X = np.take_along_axis(pat, rng.integers(0, 8, (N, 8, 1, W)), 3)
    Z = np.where(rng.random((N, 8, 1, L)) < 0.5, np.take_along_axis(np.roll(pat, -1, axis=0), rng.integers(0, 8, (N, 8, 1, L)), 3), 64 * rng.integers(0, 4, (N, 8, 16, L)))
    T = np.where(rng.random((N, 8, K)) < 0.7, rng.integers(0, S + 1, (N, 8, K)), 99); th = 64 * rng.integers(0, 40, (N, 8, S)); th[:, ::3, 1] = 0; th[:, 1::3, 0] = 0
    return pack(X, Z, P, O, V, T, th)
def check_inputs(d):
    bad = []
    for k, lo, hi in (("x", 0, 255), ("z", 0, 255), ("px", 0, W - 1), ("ol", 0, M - 1), ("nl", 0, W - 1), ("tl", 0, 99), ("th", 0, 4080)):
        v = np.asarray(d[k]).astype(np.float64)
        if not (np.min(v) >= lo and np.max(v) <= hi): bad.append("range of " + k)
        elif np.any(v != np.floor(v)): bad.append("whole numbers in " + k)
    return bad
def reference(x, z, px, ol, nl, tl, th):
    X = x.astype(np.float32).astype(np.int64).reshape(N, 8, 16, W); Z = z.astype(np.float32).astype(np.int64).reshape(N, 8, 16, L); P = px.astype(np.int64)
    O, V, T = [np.stack([gentries(a) for a in b]).astype(np.int64) for b in (ol, nl, tl)]
    lower = np.tri(L, L, -1, dtype=bool); lane = np.arange(L); A = np.zeros((N, 8, 1), np.int64)
    for s in range(S):
        R = np.where(T <= s, V, np.take_along_axis(P, O, 2))
        y = np.take_along_axis(X, R[:, :, None, :], 3); u = np.add.reduce(np.abs(y - np.tile(Z, (1, 1, 1, D))), axis=2)
        h = (((u * O) >> 5) + u + 37 * O + A) & (W - 1)
        h, O, V, T, Z = [np.roll(a, 1, axis=0) for a in (h, O, V, T, Z)]
        G = np.take_along_axis(X, h[:, :, None, :], 3); d = np.add.reduce(np.abs(G - np.tile(Z, (1, 1, 1, D))), axis=2)
        lim = th[:, :, s:s + 1].astype(np.int64)
        red = (d <= lim) & ~((T > s) & (T < 99))
        V = np.where(red, h, V); T = np.where(red, s + 2, T); A = np.sum(red.astype(np.int64), axis=2, keepdims=True)
        by = d.reshape(N, 8, D, L); j = np.argmax(by, axis=2) * L + lane; b = np.argmin(by, axis=2) * L + lane
        go = np.take_along_axis(d, j, 2) > lim
        np.put_along_axis(T, j, np.where(go, 99, np.take_along_axis(T, j, 2)), 2)
        oj = np.take_along_axis(O, j, 2); hj = np.take_along_axis(h, j, 2); hb = np.take_along_axis(h, b, 2)
        win = go & ~np.any((oj[..., :, None] == oj[..., None, :]) & lower & go[..., None, :], axis=3)
        q, g, l = np.nonzero(win); P[q, g, oj[q, g, l]] = hj[q, g, l]
        Z = (Z + np.take_along_axis(G, b[:, :, None, :], 3)) >> 1
        win = ~np.any((hb[..., :, None] == hb[..., None, :]) & lower, axis=3)
        q, g, l = np.nonzero(win); X[q, g, :, hb[q, g, l]] = Z[q, g, :, l]
    return {"yx": X.reshape(N, 128, W).astype(np.float32).astype(BF), "yp": P.astype(np.float32), "yz": Z.reshape(N, 128, L).astype(np.float32).astype(BF),
            "yn": np.stack([gtable(a) for a in V]).astype(np.float32), "yt": np.stack([gtable(a) for a in T]).astype(np.float32)}

@@ -1,0 +1,606 @@
+from concourse.bass import DstId, RemoteDMATransfer
+from concourse.mybir import AluOpType as OP, ActivationFunctionType as AF
+
+N, S = 8, 4
+X0 = 528
+XE, XD = X0 + 2048, X0 + 4096
+SEGO = [8 * a * (a + 1) for a in range(9)]
+BF, F, I, U = "bfloat16", "float32", "int32", "uint16"
+
+
+def _sb(cols, dt):
+    return ("sbuf", [128] + (list(cols) if isinstance(cols, tuple) else [cols]), dt)
+
+
+SCRATCH = {
+    "TB0": _sb(XE, BF), "TB1": _sb(XD, BF), "TB2": _sb(XD, BF), "TB3": _sb(XD, BF), "TB4": _sb(XD, BF),
+    "PWa": _sb(8192, BF), "PWb": _sb(8192, BF), "PWF": _sb(8192, F),
+    "D": _sb(2048, BF), "AB": _sb(2048, BF), "PG": _sb(2048, BF),
+    "PXI": _sb(256, I), "OLI": _sb(128, I), "NLI": _sb(128, I), "TLI": _sb(128, I), "THI": _sb(8, I),
+    "J": _sb(144, I), "PID": _sb(8, I), "PI2": _sb(8, I), "PF": _sb(8, F), "JG": _sb(128, I), "JM": _sb(128, I),
+    "ZC": _sb(144, BF), "SF1": _sb(128, F), "S01": _sb(128, BF), "NID": _sb(128, BF),
+    "BD": _sb(128, F), "BDb": _sb(128, BF), "DM2": _sb(256, F), "SEG2": _sb(256, F), "KC": _sb(128, BF),
+    "KC2": _sb(128, F), "KN": _sb(128, F), "E2": _sb(128, F),
+    "DK0": _sb(8, F), "LN": _sb(8, F), "DU": _sb(16, F), "TILE": _sb(8, U), "ENDS": _sb(8, U), "EN": _sb(8, F),
+    "CS": _sb(1152, BF), "M2K": _sb(64, BF),
+    "OW": _sb(136, F), "OW4": _sb(136, F), "OU": _sb(128, U), "O32": _sb(128, F), "CI": _sb(128, I), "CI2": _sb(128, I),
+    "CO": _sb(128, F), "CA": _sb(128, F), "ST": _sb(256, F), "ST4": _sb(256, F), "ZT": _sb(512, BF), "ZT4": _sb(512, BF),
+    "HI": _sb(136, I), "HI4": _sb(136, I), "HU": _sb(128, U), "VI": _sb(128, I), "RF": _sb(128, F), "RU": _sb(128, U),
+    "D1": _sb(128, BF), "NM": _sb(128, F), "KS": _sb(128, F), "H1": _sb(64, F), "H2": _sb(64, F),
+    "TR": _sb((2, 32), F), "TR2": _sb((2, 16), F), "MM": _sb((2, 8), I), "MA": _sb((2, 8), I), "CU": _sb((3, 8), U),
+    "VV": _sb(384, F), "SC": _sb(256, F), "EQ": _sb(1152, BF), "SP": _sb(1152, BF), "OF": _sb(32, F),
+    "VHH": _sb(128, BF), "ZI": _sb(128, I), "E": _sb(128, F), "LT": _sb(128, F), "DT": _sb(128, F), "HN": _sb(128, F),
+    "NE": _sb(128, F), "JK": _sb(128, BF), "RS": _sb(8, F), "A32": _sb(8, F), "L1": _sb(8, F), "DK": _sb(32, F), "YT": _sb(128, F),
+    "XM0": _sb(144, U), "XM1": _sb(144, U), "XM2": _sb(144, U), "XM3": _sb(144, U),
+    "XL0": _sb(144, U), "XL1": _sb(144, U), "XL2": _sb(144, U),
+    "PV": _sb(128, BF), "PF3": _sb(128, F), "PFC": _sb(256, F), "EA": _sb(1152, BF),
+}
+for _b in range(8):
+    SCRATCH["B%d" % _b] = ("psum", [128, 512], F)
+
+CY = 1.0
+GA, SCA, FIX, LAT = 1.6, 3.8, 60.0, 90.0
+HOP1, HOP2 = 2600.0, 3200.0
+PEC, BW, AFIX = 0.5, 45.0, 70.0
+EQA, PGV = [(6, 5)] * 3 + [(6, 2)], [(0, 1, 0, 0)] * 4
+CUT = ((0, 0, 0, 0), (0, 0, 0, 256))
+GRP = [((0, 2), (2, 4))] * 3 + [((0, 1), (1, 2), (2, 4))]
+NUDGE = [35284, 30127, 49224, 37915, 30834, 1134, 2644, 46312, 28536, 46491, 47782, 51847, 37148, 29294, 39564, 27028, 39567, 28893,
+         3605, 5432, 6773, 32940, 22553, 43315, 45610, 44686, 18948, 16961]
+EPS = 2.0 ** -10
+
+
+def v(name, lo, hi, step=1, rows=None):
+    r = slice(None) if rows is None else slice(rows, None, 16)
+    return ("v", name, (r, slice(lo, hi, step)), lo, hi, len(range(lo, hi, step)))
+
+
+def v3(name, w, j0, j1, lo, hi):
+    idx = (slice(None), j0, slice(lo, hi)) if j1 == j0 + 1 else (slice(None), slice(j0, j1), slice(lo, hi))
+    return ("v", name, idx, j0 * w + lo, (j1 - 1) * w + hi, (j1 - j0) * (hi - lo))
+
+
+def hbm(name, lo=None, hi=None):
+    return ("h", name, lo, hi)
+
+
+def ind(win, off):
+    return ("i", win, off)
+
+
+def _isv(a):
+    return isinstance(a, tuple) and len(a) > 0 and a[0] in ("v", "i", "h")
+
+
+def build():
+    ops = []
+
+    def two(a):
+        return SCRATCH[a[1]][2] in (BF, U)
+
+    def op(eng, meth, out, *args, **kw):
+        rd, wr = [], []
+        for a in list(args) + [x for k, x in kw.items() if k != "accum_out"]:
+            if _isv(a):
+                rd += [a[1], a[2]] if a[0] == "i" else ([a] if a[0] == "v" else [])
+        if out[0] == "i":
+            wr.append(out[1]); rd.append(out[2])
+        elif out[0] == "v":
+            wr.append(out)
+        if "accum_out" in kw:
+            wr.append(kw["accum_out"])
+        kind, lat = "c", 0.0
+        if meth == "dma_start":
+            kind = "d"
+            a = out if out[0] == "v" else args[0]
+            by = a[5] * (2 if two(a) else 4) * (8 if a[2][0] != slice(None) else 128)
+            cost, lat = 100.0, 2000.0 + by / 180.0
+        elif out[0] == "i":
+            cost = FIX + SCA * 16 * out[2][5]
+        elif args and _isv(args[0]) and args[0][0] == "i":
+            cost = FIX + GA * out[5]
+        elif meth == "tensor_tensor":
+            ps = SCRATCH[args[0][1]][0] == "psum" or SCRATCH[args[1][1]][0] == "psum"
+            cost = max(64, out[5] * (1 if ps else 2))
+        elif meth == "activation":
+            cost = AFIX + out[5]
+        elif meth == "iota":
+            cost = 150 + 2 * out[5]
+        else:
+            big = [a for a in rd + wr if a[5] > 1]
+            cost = max(64, out[5] * (0.5 if all(two(a) for a in big) else 1))
+        ops.append(dict(eng=eng, kind=kind, meth=meth, out=out, args=args, kw=kw, rd=rd, wr=wr, cost=cost * CY, lat=lat, after=[]))
+        return len(ops) - 1
+
+    def mm(out, pairs):
+        rd = [a for p in pairs for a in p]
+        cost = sum(PEC * max(64, p[1][5]) * (1 if two(p[0]) else 4) for p in pairs)
+        ops.append(dict(eng="P", kind="m", out=out, pairs=pairs, rd=rd, wr=[out], cost=cost + 60, lat=0.0, after=[]))
+
+    def send(name, parts, to, relays=None, eng="all", after=(), arr=None):
+        by = sum(p[0][5] * (2 if two(p[0]) else 4) * 128 for p in parts)
+        lat = HOP2 + by / BW if relays is None else HOP1 + by / 150.0 + HOP2 + by / (BW * min(2, len(parts)))
+        ops.append(dict(eng="G", kind="r", name=name, parts=parts, to=to, relays=relays, sel=eng, arr=arr or name,
+                        rd=[p[0] for p in parts], wr=[], cost=900.0, lat=lat, after=list(after)))
+        return len(ops) - 1
+
+    def arrive(name, sends):
+        wr = [p[1] for s in sends for p in ops[s]["parts"]]
+        ops.append(dict(eng="X", kind="a", name=name, rd=[], wr=wr, cost=0.0, lat=0.0, after=list(sends), n=len(wr)))
+        return len(ops) - 1
+
+    def tt(out, a, b, o): return op("V", "tensor_tensor", out, a, b, o)
+    def ts(out, a, s1, o0, s2=None, o1=None):
+        return op("V", "tensor_scalar", out, a, s1, s2, o0, o1) if o1 is not None else op("V", "tensor_scalar", out, a, s1, None, o0)
+    def cp(out, a): return op("V", "tensor_copy", out, a)
+    def ms(out, c): return op("V", "memset", out, c)
+    def act(out, a, f=AF.Copy, **kw): return op("A", "activation", out, a, f, **kw)
+    def dma(q, out, a, **kw): return op(q, "dma_start", out, a, **kw)
+    def sel(p): return v("ZC", 15 - p, 143 - p)
+
+    def group_sums(bank, const, src, h0, h1=None):
+        lo, hi = int(1024 * h0), int(1024 * (h0 + 1 if h1 is None else h1))
+        mm(v(bank, 0, (hi - lo) // 16), [(v("NID", 0, 128), const)] + [(sel(p), v(src, lo + p, hi, 16)) for p in range(16)])
+
+    def stage_to(pw, tb, q2="S"):
+        dma("S", v(pw, 0, 4096, rows=0), v(tb, 0, 256))
+        dma(q2, v(pw, 0, 4096, rows=1), v(tb, 256, 512))
+
+    def stage_from(pw, tb):
+        dma("S", v(tb, 0, 256), v(pw, 0, 4096, rows=0))
+        dma("S", v(tb, 256, 512), v(pw, 0, 4096, rows=1))
+
+    dma("S", v("PXI", 0, 256), hbm("px"))
+    dma("A", v("TB0", X0, X0 + 1024), hbm("x", 0, 1024))
+    dma("S", v("TB0", X0 + 1024, XE), hbm("x", 1024, 2048))
+    dma("A", v("OLI", 0, 128), hbm("ol"))
+    dma("A", v("TLI", 0, 128), hbm("tl"))
+    dma("S", v("NLI", 0, 128), hbm("nl"))
+    dma("A", v("ZT", 0, 128), hbm("z"))
+    ms(v("THI", 0, 8), 0)
+    dma("S", v("THI", 0, 4, rows=0), hbm("th"))
+    ms(v("PWa", 0, 4096), 0.0)
+    op("G", "iota", v("J", 0, 144), [[1, 144]], 0, 0)
+    op("G", "iota", v("PID", 0, 1), [[1, 1]], 0, 1)
+    xa = send("xa", [(v("TB0", X0 + 512 * c, X0 + 512 * c + 512), v("TB1", X0 + 512 * c, X0 + 512 * c + 512)) for c in (0, 1)], -1, [0, 2], arr="x1")
+    xb = send("xb", [(v("TB0", X0 + 512 * c, X0 + 512 * c + 512), v("TB1", X0 + 512 * c, X0 + 512 * c + 512)) for c in (2, 3)], -1, [1, 3], arr="x1")
+    x1 = arrive("x1", [xa, xb])
+    cp(v("TB0", 0, 256), v("PXI", 0, 256))
+    tt(v("TB0", 256, 512), v("PXI", 0, 256), v("TB0", 0, 256), OP.subtract)
+    stage_to("PWa", "TB0")
+    cp(v("TB0", 512, 520), v("THI", 0, 8))
+    tt(v("TB0", 520, 528), v("THI", 0, 8), v("TB0", 512, 520), OP.subtract)
+    arrive("p1", [send("p1", [(v("TB0", 0, X0), v("TB1", 0, X0))], -1, [0], after=[xb])])
+    ts(v("PI2", 0, 1), v("PID", 0, 1), 112, OP.bitwise_and)
+    ts(v("PI2", 1, 2), v("PID", 0, 1), 15, OP.bitwise_and)
+    ts(v("PI2", 2, 3), v("PID", 0, 1), 7, OP.bitwise_and)
+    cp(v("PF", 0, 3), v("PI2", 0, 3))
+    cp(v("PF", 3, 4), v("PID", 0, 1))
+    g16, pm, p8, pid = [v("PF", j, j + 1) for j in range(4)]
+    ts(v("ZC", 0, 144), v("J", 0, 144), 15.0, OP.subtract, g16, OP.is_equal)
+    ts(v("NID", 0, 128), v("J", 0, 128), pid, OP.is_equal, -1.0, OP.mult)
+    ms(v("M2K", 0, 64), 2048.0)
+    cp(v("OU", 0, 128), v("OLI", 0, 128))
+    cp(v("OW", 0, 128), v("OLI", 0, 128))
+    act(v("O32", 0, 128), v("OW", 0, 128), AF.Identity, bias=32.0)
+    ts(v("CI", 0, 128), v("OLI", 0, 128), 3232.0, OP.mult)
+    ts(v("CI2", 0, 128), v("CI", 0, 128), 65535, OP.bitwise_and)
+    cp(v("B7", 128, 256), v("NLI", 0, 128))
+    ts(v("ST", 128, 256), v("TLI", 0, 128), -1.0, OP.mult, 99.0, OP.add)
+    cp(v("CO", 0, 128), v("CI2", 0, 128))
+    act(v("SF1", 0, 128), sel(1))
+    tt(v("S01", 0, 128), sel(0), sel(1), OP.subtract)
+    ts(v("JG", 0, 128), v("J", 0, 128), 112, OP.bitwise_and)
+    ts(v("JM", 0, 128), v("J", 0, 128), 15, OP.bitwise_and)
+    ts(v("BD", 0, 128), v("JG", 0, 128), g16, OP.is_equal)
+    act(v("BDb", 0, 128), v("BD", 0, 128))
+    ts(v("DM2", 0, 128), v("JM", 0, 128), pm, OP.is_equal)
+    act(v("DM2", 128, 256), v("DM2", 0, 128))
+    ts(v("SEG2", 0, 128), v("JM", 0, 128), 1.0, OP.min)
+    act(v("SEG2", 128, 256), v("SEG2", 0, 128))
+    ts(v("KC", 0, 128), v("J", 0, 128), 255.0, OP.subtract)
+    act(v("KC2", 0, 128), v("KC", 0, 128), scale=-2.0)
+    ts(v("DK0", 0, 8), v("J", 0, 8), -1.0, OP.mult, 127.0, OP.add)
+    ts(v("LN", 0, 8), v("J", 0, 8), 16.0, OP.mult, pm, OP.add)
+    act(v("OW", 128, 136), v("LN", 0, 8), AF.Identity, scale=32.0, bias=4096.0)
+    act(v("DU", 0, 8), v("LN", 0, 8), AF.Identity, scale=16 / EPS, bias=2048 / EPS - 1)
+    act(v("DU", 8, 16), v("LN", 0, 8), AF.Identity, scale=32 / EPS, bias=4096 / EPS - 1)
+    ts(v("TILE", 0, 8), v("DK0", 0, 8), 0.0, OP.mult, p8, OP.add)
+    ts(v("EN", 0, 1), p8, 1.0, OP.add, 8.0, OP.mult)
+    ts(v("EN", 1, 2), p8, 2.0, OP.add, v("EN", 0, 1), OP.mult)
+    ts(v("ENDS", 0, 1), v("EN", 1, 2), 1.0, OP.subtract)
+    act(v("PF", 4, 5), pm, AF.Identity, bias=4080.0)
+    act(v("CS", 0, 1152), v("TB0", X0, X0 + 1152), AF.Identity, scale=0.0, bias=1.0)
+    for j in range(2):
+        for a in range(8):
+            lo = 576 * j
+            act(v("CS", lo + SEGO[a + 1] - 16, lo + SEGO[a + 1]), v("DM2", 0, 16), AF.Identity, scale=v("DU", 8 * j + a, 8 * j + a + 1), bias=1.0)
+            act(v("CS", lo + SEGO[a], lo + SEGO[a] + 1), v("DM2", 0, 1), scale=0.0)
+    ms(v("HI", 128, 136), 0)
+    ms(v("HI4", 128, 136), 0)
+    ms(v("PWb", 0, 2048), 0.0)
+    ms(v("PWb", 2048, 4096), 0.0)
+    o4 = send("o4", [(v("OW", 0, 136), v("OW4", 0, 136))], 4, after=[x1])
+    arrive("o4", [o4])
+    arrive("t2", [send("t2", [(v("TB0", 512, XE), v("TB2", 512, XE))], -2, after=[o4])])
+    stage_to("PWb", "TB1")
+
+    def tile_z(zt):
+        act(v(zt, 128, 256), v(zt, 0, 128))
+        act(v(zt, 256, 512), v(zt, 0, 256))
+
+    def limits(s, tb):
+        mm(v("B5", 256, 264), [(v("BDb", 0, 128), v(tb, 512, 520)), (v("BDb", 0, 128), v(tb, 520, 528))])
+        act(v("L1", s, s + 1), v("B5", 256 + s, 257 + s), AF.Identity, scale=256.0, bias=256.0)
+        act(v("DK", 8 * s, 8 * s + 8), v("DK0", 0, 8), AF.Identity, bias=v("L1", s, s + 1))
+
+    def distances(tb, offs, zt, scale, c):
+        cut = CUT[scale > 1][c]
+        for lo, hi in (((0, cut), (cut, 512)) if cut else ((0, 512),)):
+            a, b = 512 * c + lo, 512 * c + hi
+            tt(v("D", a, b), ind(v(tb, X0, XE), v(offs, a // 16, b // 16)), v(zt, 0, b - a), OP.subtract)
+            act(v("AB", a, b), v("D", a, b), AF.Abs, scale=scale)
+
+    def part_a(s, tb, pw):
+        sends = []
+        act(v("D1", 0, 128), v("ST", 128, 256), AF.Relu, scale=4096.0, bias=-4096.0 * (98 - s))
+        tt(v("NM", 0, 128), v("B7", 128, 256), v("D1", 0, 128), OP.min)
+        for c in range(4):
+            o, w = v("PG", 512 * c, 512 * c + 512), ind(v(pw, 0, 4096), v("OU", 32 * c, 32 * c + 32))
+            if (c % 2 == 0 if s == 0 else PGV[s][c]): cp(o, w)
+            else: act(o, w)
+        for hh, (c0, c1) in enumerate(GRP[s]):
+            b, lo, hi = "B%d" % ((2 + hh) % 4), 32 * c0, 32 * c1
+            group_sums(b, v("D1", lo, hi), "PG", c0 / 2, c1 / 2)
+            tt(v("RF", lo, hi), v(b, 0, hi - lo), v("NM", lo, hi), OP.max)
+            cp(v("RU", lo, hi), v("RF", lo, hi))
+        for hh, (c0, c1) in enumerate(GRP[s]):
+            b, lo, hi = "B%d" % ((2 + hh) % 4), 32 * c0, 32 * c1
+            for c in range(c0, c1):
+                distances(tb, "RU", "ZT", 1.0, c)
+            group_sums(b, v("M2K", 0, hi - lo), "AB", c0 / 2, c1 / 2)
+            tt(v("B7", 384 + lo, 384 + hi), v(b, 0, hi - lo), v("O32", lo, hi), OP.mult)
+            tt(v("VI", lo, hi), v("B7", 384 + lo, 384 + hi), v("CO" if s == 0 else "CA", lo, hi), OP.add)
+            ts(v("HI", lo, hi), v("VI", lo, hi), 5, OP.arith_shift_right, 2047, OP.bitwise_and)
+            if s == S - 1:
+                sends.append(send("h%d" % hh, [(v("HI", lo, hi), v("HI4", lo, hi))], 4, after=sends[-1:]))
+                arrive("h%d" % hh, sends[-1:])
+
+    def part_c(s, tb, pw, hi, ow, st, zt):
+        last = s == S - 1
+        n_, t_ = (v(st, 0, 128) if last else v("B7", 128, 256)), v(st, 128, 256)
+        half = (99.0 - s) / 2
+        act(v("E", 0, 128), t_, AF.Abs, bias=-half)
+        act(v("DT", 0, 128), t_, AF.Identity, scale=-1.0, bias=97.0 - s)
+        act(v("E2", 0, 128), v("E", 0, 128), AF.Relu, scale=-2.0 ** 21, bias=half * 2.0 ** 21)
+        act(v("LT", 0, 128), v("E2", 0, 128), AF.Identity, scale=-1.0, bias=v("L1", s, s + 1))
+        for hh in range(2):
+            lo = 64 * hh
+            for c in (2 * hh, 2 * hh + 1):
+                for c0, c1 in GRP[s]:
+                    if c0 == c: cp(v("HU", 32 * c0, 32 * c1), v(hi, 32 * c0, 32 * c1))
+                distances(tb, "HU", zt, 256.0, c)
+            group_sums("B%d" % hh, v("KC", lo, lo + 64), "AB", hh)
+        tt(v("HN", 0, 128), v(hi, 0, 128), n_, OP.subtract)
+        cp(v("KS", 0, 64), v("B0", 0, 64))
+        tt(v("KN", 0, 64), v("KC2", 0, 64), v("B0", 0, 64), OP.subtract)
+        tt(v("H1", 0, 32), v("KS", 0, 32), v("KS", 32, 64), OP.max)
+        tt(v("H1", 0, 8), v("H1", 0, 8), v("DK", 8 * s, 8 * s + 8), OP.max)
+        tt(v("H1", 32, 64), v("KN", 0, 32), v("KN", 32, 64), OP.max)
+        tt(v("B7", 0, 64), v("B0", 0, 64), v("LT", 0, 64), OP.is_lt)
+        tt(v("KN", 64, 128), v("KC2", 64, 128), v("B1", 0, 64), OP.subtract)
+        for j, (b, lo) in enumerate((("B1", 0), ("KN", 64))):
+            tt(v("H2", 32 * j, 32 * j + 32), v(b, lo, lo + 32), v("H1", 32 * j, 32 * j + 32), OP.max)
+            tt(v3("TR", 32, j, j + 1, 0, 32), v(b, lo + 32, lo + 64), v("H2", 32 * j, 32 * j + 32), OP.max)
+        tt(v3("TR2", 16, 0, 2, 0, 16), v3("TR", 32, 0, 2, 0, 16), v3("TR", 32, 0, 2, 16, 32), OP.max)
+        tt(v3("MM", 8, 0, 2, 0, 8), v3("TR2", 16, 0, 2, 0, 8), v3("TR2", 16, 0, 2, 8, 16), OP.max)
+        ts(v3("MA", 8, 0, 2, 0, 8), v3("MM", 8, 0, 2, 0, 8), 255, OP.bitwise_and)
+        ts(v3("CU", 8, 0, 2, 0, 8), v3("MA", 8, 0, 2, 0, 8), -1.0, OP.mult, 255.0, OP.add)
+        ts(v3("CU", 8, 2, 3, 0, 8), v3("MA", 8, 1, 2, 0, 8), -16.0, OP.mult, v("PF", 4, 5), OP.add)
+        tt(v("B7", 64, 128), v("B1", 0, 64), v("LT", 64, 128), OP.is_lt)
+        act(v("KS", 64, 128), v("B1", 0, 64))
+        cj, cb, jb = [v3("CU", 8, j, j + 1, 0, 8) for j in range(3)]
+        tt(v("VV", 256, 384), ind(v(ow, 0, 136), cj), v("DM2", 0, 128), OP.mult)
+        tt(v("VV", 128, 256), ind(v(hi, 0, 136), cb), v("DM2", 0, 128), OP.mult)
+        tt(v("VV", 0, 128), ind(v(hi, 0, 136), cj), v("DM2", 0, 128), OP.mult)
+        mm(v("B4", 0, 128), [(v("BD", 0, 128), v("VV", 256, 384))])
+        mm(v("B5", 0, 128), [(v("BD", 0, 128), v("VV", 128, 256))])
+        op("V", "tensor_tensor_scan", v("SC", 0, 256), v("SEG2", 0, 256), v("VV", 128, 384), 0.0, OP.mult, OP.add)
+        for j in range(2):
+            lo, b, a0 = 576 * j, "B%d" % (5 - j), EQA[s][j]
+            b2 = "B%d" % (3 - j) if 0 < a0 < 8 else b
+            if b2 != b: mm(v(b2, 0, 16 * a0), [(v("BD", 0, 128), v("VV", 128 + 128 * j, 128 + 128 * j + 16 * a0))])
+            for a in range(8):
+                c = v("SC", 128 * j + 15 + 16 * a, 128 * j + 16 + 16 * a)
+                if a >= a0: act(v("EA", lo + SEGO[a], lo + SEGO[a + 1]), v(b, 0, 16 * a + 16), AF.Abs, scale=-1.0, bias=c)
+                else: ts(v("EQ", lo + SEGO[a], lo + SEGO[a + 1]), v(b2, 0, 16 * a + 16), c, OP.is_equal, EPS, OP.mult)
+            if a0 < 8: act(v("EQ", lo + SEGO[a0], lo + 576), v("EA", lo + SEGO[a0], lo + 576), AF.Relu, scale=-EPS, bias=EPS)
+        xm = "XM%d" % s
+        for j in (1, 0):
+            lo = 576 * j
+            op("V", "tensor_tensor_scan", v("SP", lo, lo + 576), v("CS", lo, lo + 576), v("EQ", lo, lo + 576), 0.0, OP.mult, OP.max)
+            tt(v("OF", 16 * j, 16 * j + 16), ind(v("SP", lo, lo + 576), v("ENDS", 0, 1)), v("SC", 15, 256, 16), OP.max)
+            cp(v(xm, 128 + 8 * j, 136 + 8 * j), v("OF", 24 * j, 24 * j + 8))
+        if not last:
+            act(v("VHH", 0, 128), v("VV", 0, 128))
+            mm(v("B6", 0, 128), [(v("SF1", 0, 128), v("VV", 0, 128)), (v("S01", 0, 128), v("VHH", 0, 128))])
+            act(v("PV", 0, 128), v("B6", 0, 128))
+            cp(ind(v(pw, 0, 8192), v(xm, 136, 144)), v("PV", 0, 128))
+        else:
+            mm(v("B6", 0, 128), [(v("BD", 0, 128), v("VV", 0, 128))])
+            act(v("PF3", 0, 128), v("B6", 0, 128))
+            cp(ind(v(pw, 0, 8192), v(xm, 136, 144)), v("PF3", 0, 128))
+            dma("S", hbm("yp"), v(pw, 0, 4096, rows=0))
+        ts(v("ZI", 0, 128), ind(v("D", 0, 2048), jb), 0.5, OP.mult, -0.25, OP.add)
+        tt(v(zt, 0, 128), v("ZI", 0, 128), v(zt, 0, 128), OP.add)
+        if not last:
+            to, nxt = (3 if s == 2 else -1), "TB%d" % (s + 2)
+            cp(v(xm, 0, 128), v(zt, 0, 128))
+            sx = send("dx%d" % s, [(v(xm, 0, 136), v("XL%d" % s, 0, 136))], to, [2], "rest")
+            arrive("dx%d" % s, [sx])
+            stage_from(pw, tb)
+            arrive("ps%d" % s, [send("ps%d" % s, [(v(tb, 0, 512), v(nxt, 0, 512))], to, [3], "rest", after=[sx])])
+            tile_z(zt)
+        cp(ind(v(tb, X0, XD), v(xm, 128, 136)), v(zt, 0, 128))
+        if s < 2:
+            nm = "t%d" % (s + 3)
+            arrive(nm, [send(nm, [(v(tb, 512, XE), v("TB%d" % (s + 3), 512, XE))], 2 if s else -2, after=[sx])])
+        if last:
+            dma("S", hbm("yx", 0, 1024), v(tb, X0, X0 + 1024))
+            dma("A", hbm("yx", 1024, 2048), v(tb, X0 + 1024, XE))
+            dma("S", hbm("yz"), v(zt, 0, 128))
+        red = v("B7", 0, 128)
+        tt(v("NE", 0, 128), ind(v3("MM", 8, 0, 1, 0, 8), v("TILE", 0, 8)), v("KS", 0, 128), OP.not_equal)
+        for lo in (0, 64):
+            r, u, nn = v("B7", lo, lo + 64), v("B7", 256 + lo, 320 + lo), v(n_[1], n_[3] + lo, n_[3] + lo + 64)
+            tt(u, r, v("DT", lo, lo + 64), OP.mult)
+            tt(u, u, v(st, 128 + lo, 192 + lo), OP.add)
+            tn = v("B7", 128 + lo, 192 + lo) if last else v("HN", lo, lo + 64)
+            tt(tn, r, v("HN", lo, lo + 64), OP.mult)
+            tt(nn, tn, nn, OP.add)
+        tt(t_, v("B7", 256, 384), v("NE", 0, 128), OP.mult)
+        if s == S - 2: act(v(st, 0, 128), n_)
+        if last:
+            dma("S", hbm("yn"), n_)
+            act(v("YT", 0, 128), t_, AF.Identity, scale=-1.0, bias=99.0)
+            dma("A", hbm("yt"), v("YT", 0, 128))
+        else:
+            act(v("JK", 0, 128), red, accum_out=v("RS", 0, 1))
+            mm(v("B4", 256, 257), [(v("BD", 0, 128), v("RS", 0, 1))])
+            act(v("A32", 0, 1), v("B4", 256, 257), scale=32.0)
+            act(v("CA", 0, 128), v("CO", 0, 128), AF.Identity, bias=v("A32", 0, 1))
+
+    def take_x(s, tb):
+        cp(ind(v(tb, X0, XD), v("XL%d" % s, 128, 136)), v("XL%d" % s, 0, 128))
+
+    tile_z("ZT")
+    limits(3, "TB0")
+    part_a(0, "TB0", "PWa")
+    limits(0, "TB1")
+    part_c(0, "TB1", "PWb", "HI", "OW", "ST", "ZT")
+    part_a(1, "TB1", "PWb")
+    limits(1, "TB2")
+    stage_to("PWa", "TB2")
+    take_x(0, "TB2")
+    part_c(1, "TB2", "PWa", "HI", "OW", "ST", "ZT")
+    part_a(2, "TB2", "PWa")
+    limits(2, "TB3")
+    stage_to("PWb", "TB3")
+    take_x(1, "TB3")
+    part_c(2, "TB3", "PWb", "HI", "OW", "ST", "ZT")
+    arrive("z4", [send("z4", [(v("ZT", 0, 128), v("ZT4", 0, 128))], 4)])
+    arrive("s4", [send("s4", [(v("ST", 0, 256), v("ST4", 0, 256))], 4)])
+    part_a(3, "TB3", "PWb")
+    tile_z("ZT4")
+    take_x(2, "TB4")
+    mm(v("B6", 128, 384), [(v("NID", 0, 128), v("TB4", 0, 256)), (v("NID", 0, 128), v("TB4", 256, 512))])
+    act(v("PFC", 0, 256), v("B6", 128, 384), scale=-1.0)
+    dma("S", v("PWF", 0, 4096, rows=0), v("PFC", 0, 256))
+    part_c(3, "TB4", "PWF", "HI4", "OW4", "ST4", "ZT4")
+    return ops
+
+
+def analyse():
+    ops = build()
+    n = len(ops)
+    hist = {}
+    for i, o in enumerate(ops):
+        deps = set(o["after"])
+        for acc, w in [(a, False) for a in o["rd"]] + [(a, True) for a in o["wr"]]:
+            ps = SCRATCH[acc[1]][0] == "psum"
+            for (j, lo, hi, w2, rows) in hist.get(acc[1], []):
+                if j == i: continue
+                meet = lo < acc[4] and acc[3] < hi and (w or w2)
+                if meet and rows != acc[2][0] and rows != slice(None) and acc[2][0] != slice(None): meet = False
+                if meet or (ps and ops[j]["eng"] != o["eng"]): deps.add(j)
+        for acc, w in [(a, False) for a in o["rd"]] + [(a, True) for a in o["wr"]]:
+            hist.setdefault(acc[1], []).append((i, acc[3], acc[4], w, acc[2][0]))
+        o["deps"] = deps
+    succ = [[] for _ in range(n)]
+    for i, o in enumerate(ops):
+        for j in o["deps"]: succ[j].append(i)
+
+    def delay(j, i):
+        if ops[j]["kind"] == "r": return ops[j]["lat"] if ops[i]["kind"] == "a" else 0.0
+        return ops[j]["lat"] + (0.0 if ops[j]["kind"] == "a" else LAT)
+    prio = [0.0] * n
+    for i in range(n - 1, -1, -1):
+        prio[i] = ops[i]["cost"] + max([delay(i, k) + prio[k] for k in succ[i]] + [ops[i]["lat"]])
+    kin = {}
+    for i, o in enumerate(ops):
+        x = o.get("out") or ("v", o["name"], 0, 0, 0)
+        x = x[1] if x[0] == "i" else x
+        o["kin"] = kin.setdefault((o["eng"], o.get("meth"), x[1].rstrip("0123456789ab"), x[3], len(o["rd"]), o["cost"]), [])
+        o["kin"].append(i)
+    return ops, succ, prio, delay
+
+
+def schedule(ops, succ, prio, delay):
+    n, prio = len(ops), list(prio)
+    for x in NUDGE:
+        for i in (ops[x % n]["kin"] if x // (41 * n) else [x % n]):
+            prio[i] += 150.0 * (x // n % 41 - 20)
+    left = [len(o["deps"]) for o in ops]
+    ready = {i: 0.0 for i in range(n) if left[i] == 0}
+    free, end, order = {}, [0.0] * n, []
+    while ready:
+        best = None
+        for e in set(ops[i]["eng"] for i in ready):
+            mine = [i for i in ready if ops[i]["eng"] == e]
+            t = max(free.get(e, 0.0), min(ready[i] for i in mine))
+            c = max([i for i in mine if ready[i] <= t], key=lambda i: (prio[i], -i))
+            soon = [i for i in mine if prio[i] > prio[c] + 2 * ops[c]["cost"] and ready[i] < t + 0.5 * ops[c]["cost"]]
+            if soon:
+                c = min(soon, key=lambda i: ready[i]); t = max(t, ready[c])
+            if best is None or (t, e) < best[:2]: best = (t, e, c)
+        t, e, c = best
+        del ready[c]
+        end[c] = t + ops[c]["cost"]; ops[c]["t"] = t
+        if e != "X": free[e] = end[c]
+        order.append(c)
+        for k in succ[c]:
+            left[k] -= 1
+            if left[k] == 0: ready[k] = max(end[j] + delay(j, k) for j in ops[k]["deps"])
+    return order, end
+
+
+def plan():
+    ops, succ, prio, delay = analyse()
+    order, end = schedule(ops, succ, prio, delay)
+    cnt, known, sems = {}, {}, []
+    for i in order:
+        o = ops[i]
+        if o["kind"] == "a":
+            o["sig"] = ("a_" + o["name"], None); o["vc"] = {}; sems.append(o["sig"][0]); continue
+        vc = known.setdefault(o["eng"], {})
+        waits = []
+        for j in sorted(o["deps"], key=lambda j: -end[j]):
+            p = ops[j]
+            if p["kind"] == "r":
+                assert o["kind"] == "r"
+                continue
+            sem, val = p["sig"]
+            if vc.get(sem, 0) >= (val or 1): continue
+            waits.append(j)
+            vc[sem] = val or 1
+            for k2, x in p["vc"].items(): vc[k2] = max(vc.get(k2, 0), x)
+        o["waits"] = waits; o["vc"] = dict(vc)
+        if o["kind"] == "d":
+            o["sig"] = ("d%d" % i, 16); sems.append(o["sig"][0])
+        elif o["kind"] != "r":
+            cnt[o["eng"]] = cnt.get(o["eng"], 0) + 1; o["sig"] = ("q" + o["eng"], cnt[o["eng"]])
+    sems += ["q" + e for e in cnt] + ["sent"] + ["r_" + o["name"] for o in ops if o["kind"] == "r" and o["relays"] is not None]
+    return ops, order, cnt, sems
+
+
+OPS, ORDER, COUNTS, SEMAPHORES = plan()
+
+
+def _mask(es):
+    return sum(1 << e for e in es)
+
+
+def _helpers(topo, src, dst):
+    cs = [c for c in topo.cores_of(src) if c != src and topo.may_write(c, dst)]
+    return sorted(cs, key=lambda c: (topo.die(c) != topo.die(src), c))
+
+
+def rank_program(g, core, T, topo):
+    def ap(a):
+        if not _isv(a): return a
+        if a[0] == "i": return ap(a[1]).indirect(ap(a[2]))
+        if a[0] == "h": return T[a[1]][:] if a[2] is None else T[a[1]][:, a[2]:a[3]]
+        return T[a[1]][a[2]]
+
+    rank = T.rank_of(core)
+    if rank is None:
+        own = [c for c in topo.cores_of(core) if T.rank_of(c) is not None]
+        if not own: return
+        src, sent = own[0], 0
+        for i in ORDER:
+            o = OPS[i]
+            if o["kind"] != "r" or o["relays"] is None: continue
+            dst = T.cores[(T.rank_of(src) + o["to"]) % N]
+            hs = _helpers(topo, src, dst)
+            for p, r in zip(o["parts"], o["relays"]):
+                if hs[r % len(hs)] != core: continue
+                es = _first_hop(topo, src, core, dst, o)
+                g.wait_ge(T.sem["r_" + o["name"]], len(es) // len(o["parts"]))
+                rid, pid = topo.addr(dst, core)
+                g.remote_dma(ap(p[1]), ap(p[1]), T.sem["a_" + o["arr"]], T.sem.sent, pid, rid, topo.mask(core, dst))
+                sent += len(topo.engines(core, dst))
+        if sent: g.wait_ge(T.sem.sent, sent)
+        return
+
+    q = {"V": g.vector, "A": g.scalar, "P": g.tensor, "G": g, "S": g.sync}
+    sent = 0
+
+    def total(o):
+        s = OPS[o["after"][0]]
+        src = T.cores[(rank - s["to"]) % N]
+        if s["relays"] is not None: src = _helpers(topo, src, core)[0]
+        return o["n"] * len(topo.engines(src, core))
+
+    for i in ORDER:
+        o = OPS[i]
+        if o["kind"] == "a": continue
+        e = q[o["eng"]]
+        for j in o["waits"]:
+            sem, val = OPS[j]["sig"]
+            e.wait_ge(T.sem[sem], total(OPS[j]) if val is None else val)
+        if o["kind"] == "r":
+            dst = T.cores[(rank + o["to"]) % N]
+            if o["relays"] is None:
+                rid, pid = topo.addr(dst, core)
+                p = o["parts"][0]
+                g.remote_dma(ap(p[1]), ap(p[0]), T.sem["a_" + o["arr"]], T.sem.sent, pid, rid, topo.mask(core, dst))
+                sent += len(topo.engines(core, dst))
+                continue
+            hs = _helpers(topo, core, dst)
+            tr = []
+            for k, (p, r) in enumerate(zip(o["parts"], o["relays"])):
+                h = hs[r % len(hs)]
+                es = _first_hop(topo, core, h, dst, o)
+                w = len(es) // len(o["parts"])
+                rid, pid = topo.addr(h, core)
+                tr.append((rid, pid, _mask(es[k * w:k * w + w]), p))
+                sent += w
+            if len(tr) == 1:
+                rid, pid, m, p = tr[0]
+                g.remote_dma(ap(p[1]), ap(p[0]), T.sem["r_" + o["name"]], T.sem.sent, pid, rid, m)
+            else:
+                g.remote_dma_fused([RemoteDMATransfer(dst_ids=[DstId(rid=rid, pnc=pid)], dma_engine_mask=m, remote_sem=T.sem["r_" + o["name"]],
+                                                      src=ap(p[0]), dst=ap(p[1])) for rid, pid, m, p in tr], local_sem=T.sem.sent)
+            continue
+        if o["kind"] == "m":
+            k = len(o["pairs"])
+            for j, (l, r) in enumerate(o["pairs"]):
+                ins = e.matmul(ap(o["out"]), ap(l), ap(r), j == 0, j == k - 1)
+        else:
+            args = [ap(o["out"])] + [ap(a) for a in o["args"]]
+            kw = {k: ap(a) for k, a in o["kw"].items()}
+            m = o["meth"]
+            if m == "tensor_tensor": ins = e.tensor_tensor(*args)
+            elif m == "tensor_scalar": ins = e.tensor_scalar(*args)
+            elif m == "tensor_copy": ins = e.tensor_copy(*args)
+            elif m == "tensor_tensor_scan": ins = e.tensor_tensor_scan(*args)
+            elif m == "memset": ins = e.memset(*args)
+            elif m == "activation": ins = e.activation(*args, **kw)
+            elif m == "iota": ins = e.iota(*args)
+            else: ins = e.dma_start(*args, **kw)
+        ins.then_inc(T.sem[o["sig"][0]], 16 if o["kind"] == "d" else 1)
+    for o in OPS:
+        if o["kind"] == "a": g.wait_ge(T.sem[o["sig"][0]], total(o))
+    g.wait_ge(T.sem.sent, sent)
+    for k, c in COUNTS.items():
+        g.wait_ge(T.sem["q" + k], c)
+    for i in ORDER:
+        if OPS[i]["kind"] == "d": g.wait_ge(T.sem[OPS[i]["sig"][0]], 16)
+
+
+def _first_hop(topo, src, helper, dst, o):
+    es = topo.engines(src, helper)
+    if o["sel"] == "rest":
+        off = topo.engines(helper, dst)
+        es = [e for e in es if e not in off]
+    return es

@@ -29,25 +29,28 @@ SCRATCH = {
     "D1": _sb(128, BF), "NM": _sb(128, F), "KS": _sb(128, F), "H1": _sb(64, F), "H2": _sb(64, F),
     "TR": _sb((2, 32), F), "TR2": _sb((2, 16), F), "MM": _sb((2, 8), I), "MA": _sb((2, 8), I), "CU": _sb((3, 8), U),
     "VV": _sb(384, F), "SC": _sb(256, F), "EQ": _sb(1152, BF), "SP": _sb(1152, BF), "OF": _sb(32, F),
-    "VHH": _sb(128, BF), "ZI": _sb(128, I), "E": _sb(128, F), "LT": _sb(128, F), "DT": _sb(128, F), "HN": _sb(128, F),
+    "VHH": _sb(128, BF), "E": _sb(128, F), "LT": _sb(128, F), "DT": _sb(128, F), "HN": _sb(128, F),
     "NE": _sb(128, F), "JK": _sb(128, BF), "RS": _sb(8, F), "A32": _sb(8, F), "L1": _sb(8, F), "DK": _sb(32, F), "YT": _sb(128, F),
     "XM0": _sb(144, U), "XM1": _sb(144, U), "XM2": _sb(144, U), "XM3": _sb(144, U),
     "XL0": _sb(144, U), "XL1": _sb(144, U), "XL2": _sb(144, U),
-    "PV": _sb(128, BF), "PF3": _sb(128, F), "PFC": _sb(256, F), "EA": _sb(1152, BF),
+    "ZM": _sb(128, F), "ZS": _sb(128, F), "SZ": _sb(64, F), "NIF": _sb(128, F), "IDP": _sb(128, BF),
+    "WP0": _sb(144, BF), "WN0": _sb(144, BF), "WP1": _sb(144, BF), "WN1": _sb(144, BF), "PV": _sb(128, BF), "PF3": _sb(128, F), "PFC": _sb(256, F), "EA": _sb(1152, BF),
 }
 for _b in range(8):
     SCRATCH["B%d" % _b] = ("psum", [128, 512], F)
 
 CY = 1.0
 GA, SCA, FIX, LAT = 1.6, 3.8, 60.0, 90.0
-HOP1, HOP2 = 2600.0, 3200.0
+HOP1, HOP2 = 1700.0, 2300.0
+ZPE = (0, 0, 0, 0)
+FAR = [[(1, 0, 1, 0)] * 3 + [(0, 0, 1, 0)], [(1, 0, 1, 0)] * 4]
 PEC, BW, AFIX = 0.5, 45.0, 70.0
-EQA, PGV = [(6, 5)] * 3 + [(6, 2)], [(0, 1, 0, 0)] * 4
-CUT = ((0, 0, 0, 0), (0, 0, 0, 256))
+EQA, PGV = [(4, 6)] * 3 + [(6, 2)], [(0, 1, 0, 0)] * 4
+CUT = ((0, 0, 0, 0), (0, 0, 0, 0))
 GRP = [((0, 2), (2, 4))] * 3 + [((0, 1), (1, 2), (2, 4))]
-NUDGE = [35284, 30127, 49224, 37915, 30834, 1134, 2644, 46312, 28536, 46491, 47782, 51847, 37148, 29294, 39564, 27028, 39567, 28893,
-         3605, 5432, 6773, 32940, 22553, 43315, 45610, 44686, 18948, 16961]
-EPS = 2.0 ** -10
+NUDGE = [40821, 56740, 9499, 33621, 32834, 51856, 30244, 37080, 23082, 37357, 47541, 50887, 39423, 30987, 39387, 31646, 48917, 34712,
+         37964, 19731, 44969, 39298, 8407, 45714, 173, 9025, 30911]
+EPS, BIG = 2.0 ** -10, 1.5 * 2.0 ** 24
 
 
 def v(name, lo, hi, step=1, rows=None):
@@ -104,18 +107,18 @@ def build():
             cost = max(64, out[5] * (1 if ps else 2))
         elif meth == "activation":
             cost = AFIX + out[5]
-        elif meth == "iota":
-            cost = 150 + 2 * out[5]
+        elif meth in ("iota", "affine_select"):
+            cost = 200 + 2 * out[5]
         else:
             big = [a for a in rd + wr if a[5] > 1]
             cost = max(64, out[5] * (0.5 if all(two(a) for a in big) else 1))
         ops.append(dict(eng=eng, kind=kind, meth=meth, out=out, args=args, kw=kw, rd=rd, wr=wr, cost=cost * CY, lat=lat, after=[]))
         return len(ops) - 1
 
-    def mm(out, pairs):
-        rd = [a for p in pairs for a in p]
+    def mm(out, pairs, start=True, stop=True):
+        rd = [a for p in pairs for a in p[:2]]
         cost = sum(PEC * max(64, p[1][5]) * (1 if two(p[0]) else 4) for p in pairs)
-        ops.append(dict(eng="P", kind="m", out=out, pairs=pairs, rd=rd, wr=[out], cost=cost + 60, lat=0.0, after=[]))
+        ops.append(dict(eng="P", kind="m", out=out, pairs=[p if len(p) == 3 else p + (out,) for p in pairs], start=start, stop=stop, rd=rd, wr=[out], cost=cost + 60, lat=0.0, after=[]))
 
     def send(name, parts, to, relays=None, eng="all", after=(), arr=None):
         by = sum(p[0][5] * (2 if two(p[0]) else 4) * 128 for p in parts)
@@ -209,8 +212,11 @@ def build():
     ts(v("EN", 0, 1), p8, 1.0, OP.add, 8.0, OP.mult)
     ts(v("EN", 1, 2), p8, 2.0, OP.add, v("EN", 0, 1), OP.mult)
     ts(v("ENDS", 0, 1), v("EN", 1, 2), 1.0, OP.subtract)
-    act(v("PF", 4, 5), pm, AF.Identity, bias=4080.0)
-    act(v("CS", 0, 1152), v("TB0", X0, X0 + 1152), AF.Identity, scale=0.0, bias=1.0)
+    for nm, x in (("WP0", 2.0), ("WN0", -1.0), ("WP1", 512.0), ("WN1", -256.0)):
+        act(v(nm, 0, 144), v("ZC", 0, 144), scale=x)
+    act(v("NIF", 0, 128), v("NID", 0, 128))
+    act(v("IDP", 0, 128), v("NID", 0, 128), scale=-1.0)
+    ms(v("CS", 0, 1152), 1.0)
     for j in range(2):
         for a in range(8):
             lo = 576 * j
@@ -218,28 +224,54 @@ def build():
             act(v("CS", lo + SEGO[a], lo + SEGO[a] + 1), v("DM2", 0, 1), scale=0.0)
     ms(v("HI", 128, 136), 0)
     ms(v("HI4", 128, 136), 0)
-    ms(v("PWb", 0, 2048), 0.0)
-    ms(v("PWb", 2048, 4096), 0.0)
+    for c in range(4):
+        ms(v("PWb", 1024 * c, 1024 * c + 1024), 0.0)
     o4 = send("o4", [(v("OW", 0, 136), v("OW4", 0, 136))], 4, after=[x1])
     arrive("o4", [o4])
     arrive("t2", [send("t2", [(v("TB0", 512, XE), v("TB2", 512, XE))], -2, after=[o4])])
     stage_to("PWb", "TB1")
 
-    def tile_z(zt):
-        act(v(zt, 128, 256), v(zt, 0, 128))
-        act(v(zt, 256, 512), v(zt, 0, 256))
+    def tile_z(zt, pool=False):
+        for w in (128, 256):
+            if pool: op("G", "affine_select", v(zt, w, 2 * w), v(zt, 0, w), [[1, w]], OP.is_ge, 0.0, 0, 0)
+            else: act(v(zt, w, 2 * w), v(zt, 0, w))
 
     def limits(s, tb):
         mm(v("B5", 256, 264), [(v("BDb", 0, 128), v(tb, 512, 520)), (v("BDb", 0, 128), v(tb, 520, 528))])
         act(v("L1", s, s + 1), v("B5", 256 + s, 257 + s), AF.Identity, scale=256.0, bias=256.0)
         act(v("DK", 8 * s, 8 * s + 8), v("DK0", 0, 8), AF.Identity, bias=v("L1", s, s + 1))
 
-    def distances(tb, offs, zt, scale, c):
+    def distances(tb, offs, zt, scale, c, far):
         cut = CUT[scale > 1][c]
         for lo, hi in (((0, cut), (cut, 512)) if cut else ((0, 512),)):
             a, b = 512 * c + lo, 512 * c + hi
-            tt(v("D", a, b), ind(v(tb, X0, XE), v(offs, a // 16, b // 16)), v(zt, 0, b - a), OP.subtract)
-            act(v("AB", a, b), v("D", a, b), AF.Abs, scale=scale)
+            w = ind(v(tb, X0, XE), v(offs, a // 16, b // 16))
+            if far:
+                act(v("D", a, b), w)
+                tt(v("AB", a, b), v("D", a, b), v("B6", 0, b - a), OP.max)
+            else:
+                tt(v("D", a, b), w, v(zt, 0, b - a), OP.subtract)
+                act(v("AB", a, b), v("D", a, b), AF.Abs, scale=0.5)
+
+    def dist_sums(bank, const, k, c0, c1, far):
+        out = v(bank, 0, 32 * (c1 - c0))
+        pre = [(v("NID", 0, 128), const, out)]
+        for c in range(c0, c1):
+            if far[c]:
+                o = v(bank, 32 * (c - c0), 32 * (c - c0) + 32)
+                pre += [(v("NIF", 0, 128), v("SZ", 32 * k, 32 * k + 32), o)]
+                pre += [(v("WN%d" % k, 15 - p, 143 - p), v("D", 512 * c + p, 512 * c + 512, 16), o) for p in range(16)]
+        post = [(v("WP%d" % k, 15 - p, 143 - p), v("AB", 512 * c0 + p, 512 * c1, 16), out) for p in range(16)]
+        if len(pre) == 1: mm(out, pre + post)
+        else:
+            mm(out, pre, stop=False)
+            mm(out, post, start=False)
+
+    def spread_z(zt):
+        mm(v("B6", 0, 512), [(v("IDP", 0, 128), v(zt, 0, 512))])
+        mm(v("B5", 384, 416), [(sel(p), v(zt, p, 512, 16)) for p in range(16)])
+        act(v("SZ", 0, 32), v("B5", 384, 416))
+        act(v("SZ", 32, 64), v("B5", 384, 416), scale=256.0)
 
     def part_a(s, tb, pw):
         sends = []
@@ -257,8 +289,8 @@ def build():
         for hh, (c0, c1) in enumerate(GRP[s]):
             b, lo, hi = "B%d" % ((2 + hh) % 4), 32 * c0, 32 * c1
             for c in range(c0, c1):
-                distances(tb, "RU", "ZT", 1.0, c)
-            group_sums(b, v("M2K", 0, hi - lo), "AB", c0 / 2, c1 / 2)
+                distances(tb, "RU", "ZT", 1.0, c, FAR[0][s][c])
+            dist_sums(b, v("M2K", 0, hi - lo), 0, c0, c1, FAR[0][s])
             tt(v("B7", 384 + lo, 384 + hi), v(b, 0, hi - lo), v("O32", lo, hi), OP.mult)
             tt(v("VI", lo, hi), v("B7", 384 + lo, 384 + hi), v("CO" if s == 0 else "CA", lo, hi), OP.add)
             ts(v("HI", lo, hi), v("VI", lo, hi), 5, OP.arith_shift_right, 2047, OP.bitwise_and)
@@ -279,8 +311,8 @@ def build():
             for c in (2 * hh, 2 * hh + 1):
                 for c0, c1 in GRP[s]:
                     if c0 == c: cp(v("HU", 32 * c0, 32 * c1), v(hi, 32 * c0, 32 * c1))
-                distances(tb, "HU", zt, 256.0, c)
-            group_sums("B%d" % hh, v("KC", lo, lo + 64), "AB", hh)
+                distances(tb, "HU", zt, 256.0, c, FAR[1][s][c])
+            dist_sums("B%d" % hh, v("KC", lo, lo + 64), 1, 2 * hh, 2 * hh + 2, FAR[1][s])
         tt(v("HN", 0, 128), v(hi, 0, 128), n_, OP.subtract)
         cp(v("KS", 0, 64), v("B0", 0, 64))
         tt(v("KN", 0, 64), v("KC2", 0, 64), v("B0", 0, 64), OP.subtract)
@@ -296,7 +328,6 @@ def build():
         tt(v3("MM", 8, 0, 2, 0, 8), v3("TR2", 16, 0, 2, 0, 8), v3("TR2", 16, 0, 2, 8, 16), OP.max)
         ts(v3("MA", 8, 0, 2, 0, 8), v3("MM", 8, 0, 2, 0, 8), 255, OP.bitwise_and)
         ts(v3("CU", 8, 0, 2, 0, 8), v3("MA", 8, 0, 2, 0, 8), -1.0, OP.mult, 255.0, OP.add)
-        ts(v3("CU", 8, 2, 3, 0, 8), v3("MA", 8, 1, 2, 0, 8), -16.0, OP.mult, v("PF", 4, 5), OP.add)
         tt(v("B7", 64, 128), v("B1", 0, 64), v("LT", 64, 128), OP.is_lt)
         act(v("KS", 64, 128), v("B1", 0, 64))
         cj, cb, jb = [v3("CU", 8, j, j + 1, 0, 8) for j in range(3)]
@@ -323,16 +354,22 @@ def build():
             cp(v(xm, 128 + 8 * j, 136 + 8 * j), v("OF", 24 * j, 24 * j + 8))
         if not last:
             act(v("VHH", 0, 128), v("VV", 0, 128))
-            mm(v("B6", 0, 128), [(v("SF1", 0, 128), v("VV", 0, 128)), (v("S01", 0, 128), v("VHH", 0, 128))])
-            act(v("PV", 0, 128), v("B6", 0, 128))
+            mm(v("B0", 256, 384), [(v("SF1", 0, 128), v("VV", 0, 128)), (v("S01", 0, 128), v("VHH", 0, 128))])
+            act(v("PV", 0, 128), v("B0", 256, 384))
             cp(ind(v(pw, 0, 8192), v(xm, 136, 144)), v("PV", 0, 128))
         else:
-            mm(v("B6", 0, 128), [(v("BD", 0, 128), v("VV", 0, 128))])
-            act(v("PF3", 0, 128), v("B6", 0, 128))
+            mm(v("B0", 256, 384), [(v("BD", 0, 128), v("VV", 0, 128))])
+            act(v("PF3", 0, 128), v("B0", 256, 384))
             cp(ind(v(pw, 0, 8192), v(xm, 136, 144)), v("PF3", 0, 128))
             dma("S", hbm("yp"), v(pw, 0, 4096, rows=0))
-        ts(v("ZI", 0, 128), ind(v("D", 0, 2048), jb), 0.5, OP.mult, -0.25, OP.add)
-        tt(v(zt, 0, 128), v("ZI", 0, 128), v(zt, 0, 128), OP.add)
+        cp(jb, v("SC", 15, 128, 16))
+        tt(v("ZS", 0, 128), ind(v(tb, X0, XE), jb), v(zt, 0, 128), OP.add)
+        if ZPE[s]:
+            act(v("E2", 0, 128), v("ZS", 0, 128), AF.Identity, bias=-0.5)
+            act(v("ZM", 0, 128), v("E2", 0, 128), AF.Identity, bias=BIG)
+        else:
+            ts(v("ZM", 0, 128), v("ZS", 0, 128), -0.5, OP.add, BIG, OP.add)
+        act(v(zt, 0, 128), v("ZM", 0, 128), AF.Identity, scale=0.5, bias=-BIG / 2)
         if not last:
             to, nxt = (3 if s == 2 else -1), "TB%d" % (s + 2)
             cp(v(xm, 0, 128), v(zt, 0, 128))
@@ -340,7 +377,8 @@ def build():
             arrive("dx%d" % s, [sx])
             stage_from(pw, tb)
             arrive("ps%d" % s, [send("ps%d" % s, [(v(tb, 0, 512), v(nxt, 0, 512))], to, [3], "rest", after=[sx])])
-            tile_z(zt)
+            tile_z(zt, True)
+            spread_z(zt)
         cp(ind(v(tb, X0, XD), v(xm, 128, 136)), v(zt, 0, 128))
         if s < 2:
             nm = "t%d" % (s + 3)
@@ -375,6 +413,7 @@ def build():
 
     tile_z("ZT")
     limits(3, "TB0")
+    spread_z("ZT")
     part_a(0, "TB0", "PWa")
     limits(0, "TB1")
     part_c(0, "TB1", "PWb", "HI", "OW", "ST", "ZT")
@@ -393,8 +432,9 @@ def build():
     part_a(3, "TB3", "PWb")
     tile_z("ZT4")
     take_x(2, "TB4")
-    mm(v("B6", 128, 384), [(v("NID", 0, 128), v("TB4", 0, 256)), (v("NID", 0, 128), v("TB4", 256, 512))])
-    act(v("PFC", 0, 256), v("B6", 128, 384), scale=-1.0)
+    spread_z("ZT4")
+    mm(v("B4", 128, 384), [(v("NID", 0, 128), v("TB4", 0, 256)), (v("NID", 0, 128), v("TB4", 256, 512))])
+    act(v("PFC", 0, 256), v("B4", 128, 384), scale=-1.0)
     dma("S", v("PWF", 0, 4096, rows=0), v("PFC", 0, 256))
     part_c(3, "TB4", "PWF", "HI4", "OW4", "ST4", "ZT4")
     return ops
@@ -426,6 +466,7 @@ def analyse():
     prio = [0.0] * n
     for i in range(n - 1, -1, -1):
         prio[i] = ops[i]["cost"] + max([delay(i, k) + prio[k] for k in succ[i]] + [ops[i]["lat"]])
+    prio[0] += 1e6
     kin = {}
     for i, o in enumerate(ops):
         x = o.get("out") or ("v", o["name"], 0, 0, 0)
@@ -574,8 +615,8 @@ def rank_program(g, core, T, topo):
             continue
         if o["kind"] == "m":
             k = len(o["pairs"])
-            for j, (l, r) in enumerate(o["pairs"]):
-                ins = e.matmul(ap(o["out"]), ap(l), ap(r), j == 0, j == k - 1)
+            for j, (l, r, w) in enumerate(o["pairs"]):
+                ins = e.matmul(ap(w), ap(l), ap(r), j == 0 and o["start"], j == k - 1 and o["stop"])
         else:
             args = [ap(o["out"])] + [ap(a) for a in o["args"]]
             kw = {k: ap(a) for k, a in o["kw"].items()}
@@ -587,6 +628,7 @@ def rank_program(g, core, T, topo):
             elif m == "memset": ins = e.memset(*args)
             elif m == "activation": ins = e.activation(*args, **kw)
             elif m == "iota": ins = e.iota(*args)
+            elif m == "affine_select": ins = e.affine_select(*args)
             else: ins = e.dma_start(*args, **kw)
         ins.then_inc(T.sem[o["sig"][0]], 16 if o["kind"] == "d" else 1)
     for o in OPS:

@@ -1,10 +1,11 @@
+import math
 from concourse.bass import DstId, RemoteDMATransfer
 from concourse.mybir import AluOpType as OP, ActivationFunctionType as AF
 
-N, S = 8, 4
+N, S, WORLD = 8, 4, 256
 X0 = 528
 XE, XD = X0 + 2048, X0 + 4096
-SEGO = [8 * a * (a + 1) for a in range(9)]
+PD = 8192 + 32
 BF, F, I, U = "bfloat16", "float32", "int32", "uint16"
 
 
@@ -14,43 +15,46 @@ def _sb(cols, dt):
 
 SCRATCH = {
     "TB0": _sb(XE, BF), "TB1": _sb(XD, BF), "TB2": _sb(XD, BF), "TB3": _sb(XD, BF), "TB4": _sb(XD, BF),
-    "PWa": _sb(8192, BF), "PWb": _sb(8192, BF), "PWF": _sb(8192, F),
+    "PW": _sb(PD, BF), "PWF": _sb(PD, F),
     "D": _sb(2048, BF), "AB": _sb(2048, BF), "PG": _sb(2048, BF),
     "PXI": _sb(256, I), "OLI": _sb(128, I), "NLI": _sb(128, I), "TLI": _sb(128, I), "THI": _sb(8, I),
-    "J": _sb(144, I), "PID": _sb(8, I), "PI2": _sb(8, I), "PF": _sb(8, F), "JG": _sb(128, I), "JM": _sb(128, I),
+    "J": _sb(144, I), "PID": _sb(8, I), "PI2": _sb(8, I), "PF": _sb(8, F), "JG": _sb(128, I), "JM": _sb(144, I),
     "ZC": _sb(144, BF), "SF1": _sb(128, F), "S01": _sb(128, BF), "NID": _sb(128, BF),
-    "BD": _sb(128, F), "BDb": _sb(128, BF), "DM2": _sb(256, F), "SEG2": _sb(256, F), "KC": _sb(128, BF),
+    "BD": _sb(128, F), "BDb": _sb(128, BF), "DM": _sb(128, F), "NDM": _sb(144, F), "KC": _sb(128, BF),
     "KC2": _sb(128, F), "KN": _sb(128, F), "E2": _sb(128, F),
-    "DK0": _sb(8, F), "LN": _sb(8, F), "DU": _sb(16, F), "TILE": _sb(8, U), "ENDS": _sb(8, U), "EN": _sb(8, F),
-    "CS": _sb(1152, BF), "M2K": _sb(64, BF),
+    "LN": _sb(8, F), "DU": _sb(16, F), "TILE": _sb(8, U), "ENDS": _sb(8, U), "EN": _sb(8, F),
+    "CS": _sb(1152, BF), "M2K": _sb(128, BF),
     "OW": _sb(136, F), "OW4": _sb(136, F), "OU": _sb(128, U), "O32": _sb(128, F), "CI": _sb(128, I), "CI2": _sb(128, I),
     "CO": _sb(128, F), "CA": _sb(128, F), "ST": _sb(256, F), "ST4": _sb(256, F), "ZT": _sb(512, BF), "ZT4": _sb(512, BF),
     "HI": _sb(136, I), "HI4": _sb(136, I), "HU": _sb(128, U), "VI": _sb(128, I), "RF": _sb(128, F), "RU": _sb(128, U),
-    "D1": _sb(128, BF), "NM": _sb(128, F), "KS": _sb(128, F), "H1": _sb(64, F), "H2": _sb(64, F),
+    "D1": _sb(128, BF), "NM": _sb(128, F),
     "TR": _sb((2, 32), F), "TR2": _sb((2, 16), F), "MM": _sb((2, 8), I), "MA": _sb((2, 8), I), "CU": _sb((3, 8), U),
-    "VV": _sb(384, F), "SC": _sb(256, F), "EQ": _sb(1152, BF), "SP": _sb(1152, BF), "OF": _sb(32, F),
-    "VHH": _sb(128, BF), "E": _sb(128, F), "LT": _sb(128, F), "DT": _sb(128, F), "HN": _sb(128, F),
-    "NE": _sb(128, F), "JK": _sb(128, BF), "RS": _sb(8, F), "A32": _sb(8, F), "L1": _sb(8, F), "DK": _sb(32, F), "YT": _sb(128, F),
+    "VH": _sb(128, F), "VB": _sb(144, F), "VO": _sb(144, F), "SB": _sb(144, F), "SO": _sb(144, F),
+    "EQ": _sb(1152, BF), "SP": _sb(1152, BF), "EA": _sb(1152, BF), "OF": _sb(32, F), "XP": _sb(16, U),
+    "VHH": _sb(128, BF), "E": _sb(128, F), "LT": _sb(128, F), "HN": _sb(128, F),
+    "NE": _sb(128, F), "RR": _sb(128, F), "RS": _sb(8, F), "A32": _sb(8, F), "L1": _sb(8, F), "YT": _sb(128, F),
     "XM0": _sb(144, U), "XM1": _sb(144, U), "XM2": _sb(144, U), "XM3": _sb(144, U),
     "XL0": _sb(144, U), "XL1": _sb(144, U), "XL2": _sb(144, U),
-    "ZM": _sb(128, F), "ZS": _sb(128, F), "SZ": _sb(64, F), "NIF": _sb(128, F), "IDP": _sb(128, BF),
-    "WP0": _sb(144, BF), "WN0": _sb(144, BF), "WP1": _sb(144, BF), "WN1": _sb(144, BF), "PV": _sb(128, BF), "PF3": _sb(128, F), "PFC": _sb(256, F), "EA": _sb(1152, BF),
+    "ZS": _sb(128, F), "GB": _sb(128, BF), "MB": _sb(8, BF), "SZ": _sb(32, F), "NF0": _sb(128, F), "NF1": _sb(128, F), "IDP": _sb(128, BF),
+    "WP0": _sb(144, BF), "WN0": _sb(144, BF), "WP1": _sb(144, BF), "WN1": _sb(144, BF), "PV": _sb(128, BF), "PF3": _sb(128, F), "PFC": _sb(256, F),
 }
 for _b in range(8):
     SCRATCH["B%d" % _b] = ("psum", [128, 512], F)
 
-CY = 1.0
 GA, SCA, FIX, LAT = 1.6, 3.8, 60.0, 90.0
-HOP1, HOP2 = 1700.0, 2300.0
-ZPE = (0, 0, 0, 0)
-FAR = [[(1, 0, 1, 0)] * 3 + [(0, 0, 1, 0)], [(1, 0, 1, 0)] * 4]
+HOP1, HOP2 = 2000.0, 2700.0
 PEC, BW, AFIX = 0.5, 45.0, 70.0
-EQA, PGV = [(4, 6)] * 3 + [(6, 2)], [(0, 1, 0, 0)] * 4
-CUT = ((0, 0, 0, 0), (0, 0, 0, 0))
-GRP = [((0, 2), (2, 4))] * 3 + [((0, 1), (1, 2), (2, 4))]
-NUDGE = [40821, 56740, 9499, 33621, 32834, 51856, 30244, 37080, 23082, 37357, 47541, 50887, 39423, 30987, 39387, 31646, 48917, 34712,
-         37964, 19731, 44969, 39298, 8407, 45714, 173, 9025, 30911]
-EPS, BIG = 2.0 ** -10, 1.5 * 2.0 ** 24
+MATE, MATE2 = ("mate", 0), ("mate", 1)
+PLAN = dict(
+    pg=[[[(32, "V"), (32, "A")], [(32, "V"), (32, "A")]]] + [[[(32, "A"), (32, "V")], [(32, "A"), (32, "A")]]] * 3,
+    u=[[[(32, "c"), (32, "b")], [(32, "c"), (32, "b")]]] * 4,
+    d=[[[(32, "c"), (32, "b")], [(32, "c"), (32, "b")]]] * 4,
+    nb=(2, 2), eqa=[((0, 8), (0, 0))] * 4, zsa=[0, 0, 0, 0], nea=[0, 0, 0, 0], soft=0, tsplit=(1, 1, 1), pssplit=True, mw=128, early=1, szv=0,
+    loads=[["px", 0, 1, 2, "ol"], ["tl", "nl", "z"]], xsend=[[MATE, 2], [MATE2, 0], [3, 1]], xlat=[8000.0, 8500.0, 7300.0], tries=12000)
+SPEEDS = [(0.88, 1.56, 3.8, 110.0, 150.0, 0.8, 12.0, 80.0), (0.85, 1.2, 2.5, 150.0, 150.0, 0.9, 12.0, 50.0), (1.15, 1.9, 5.0, 70.0, 130.0, 0.8, 5.0, 100.0)]
+WEIGHTS, AMIN = [0.5, 0.25, 0.25], 40.0
+EPS = 2.0 ** -10
+CRIT, TEMP = 0.7, 50.0
 
 
 def v(name, lo, hi, step=1, rows=None):
@@ -75,8 +79,26 @@ def _isv(a):
     return isinstance(a, tuple) and len(a) > 0 and a[0] in ("v", "i", "h")
 
 
-def build():
-    ops = []
+def spans(groups):
+    out, at = [], 0
+    for grp in groups:
+        ps = []
+        for w, who in grp:
+            ps.append((at, at + w, who)); at += w
+        out.append((ps[0][0], at, ps))
+    return out
+
+
+def segments(nb):
+    out = [0]
+    for a in range(8): out.append(out[-1] + 16 * (a % (8 // nb) + 1))
+    return out
+
+
+def build(P):
+    ops, tag = [], [("load", 0)]
+    far = any(who == "c" for k in "ud" for st in P[k] for grp in st for _, who in grp)
+    dbank = ["B5" if far else "B6", "B5"]
 
     def two(a):
         return SCRATCH[a[1]][2] in (BF, U)
@@ -92,16 +114,16 @@ def build():
             wr.append(out)
         if "accum_out" in kw:
             wr.append(kw["accum_out"])
-        kind, lat = "c", 0.0
+        kind, lat, var = "c", 0.0, None
         if meth == "dma_start":
             kind = "d"
             a = out if out[0] == "v" else args[0]
             by = a[5] * (2 if two(a) else 4) * (8 if a[2][0] != slice(None) else 128)
             cost, lat = 100.0, 2000.0 + by / 180.0
         elif out[0] == "i":
-            cost = FIX + SCA * 16 * out[2][5]
+            cost, var = FIX + SCA * 16 * out[2][5], ("s", 16 * out[2][5])
         elif args and _isv(args[0]) and args[0][0] == "i":
-            cost = FIX + GA * out[5]
+            cost, var = FIX + GA * out[5], ("g", out[5])
         elif meth == "tensor_tensor":
             ps = SCRATCH[args[0][1]][0] == "psum" or SCRATCH[args[1][1]][0] == "psum"
             cost = max(64, out[5] * (1 if ps else 2))
@@ -112,24 +134,25 @@ def build():
         else:
             big = [a for a in rd + wr if a[5] > 1]
             cost = max(64, out[5] * (0.5 if all(two(a) for a in big) else 1))
-        ops.append(dict(eng=eng, kind=kind, meth=meth, out=out, args=args, kw=kw, rd=rd, wr=wr, cost=cost * CY, lat=lat, after=[]))
+        ops.append(dict(eng=eng, kind=kind, meth=meth, out=out, args=args, kw=kw, rd=rd, wr=wr, cost=cost, lat=lat, after=[], var=var, tag=tag[0]))
         return len(ops) - 1
 
     def mm(out, pairs, start=True, stop=True):
         rd = [a for p in pairs for a in p[:2]]
         cost = sum(PEC * max(64, p[1][5]) * (1 if two(p[0]) else 4) for p in pairs)
-        ops.append(dict(eng="P", kind="m", out=out, pairs=[p if len(p) == 3 else p + (out,) for p in pairs], start=start, stop=stop, rd=rd, wr=[out], cost=cost + 60, lat=0.0, after=[]))
+        ops.append(dict(eng="P", kind="m", out=out, pairs=[p if len(p) == 3 else p + (out,) for p in pairs], start=start, stop=stop, rd=rd, wr=[out], cost=cost + 60, lat=0.0, after=[], tag=tag[0]))
 
     def send(name, parts, to, relays=None, eng="all", after=(), arr=None):
+        relays = relays or [None]
         by = sum(p[0][5] * (2 if two(p[0]) else 4) * 128 for p in parts)
-        lat = HOP2 + by / BW if relays is None else HOP1 + by / 150.0 + HOP2 + by / (BW * min(2, len(parts)))
+        lat = HOP2 + by / BW if relays == [None] else HOP1 + by / 150.0 + HOP2 + by / (BW * min(2, len(parts)))
         ops.append(dict(eng="G", kind="r", name=name, parts=parts, to=to, relays=relays, sel=eng, arr=arr or name,
-                        rd=[p[0] for p in parts], wr=[], cost=900.0, lat=lat, after=list(after)))
+                        rd=[p[0] for p in parts], wr=[], cost=900.0, lat=lat, after=list(after), tag=tag[0]))
         return len(ops) - 1
 
     def arrive(name, sends):
         wr = [p[1] for s in sends for p in ops[s]["parts"]]
-        ops.append(dict(eng="X", kind="a", name=name, rd=[], wr=wr, cost=0.0, lat=0.0, after=list(sends), n=len(wr)))
+        ops.append(dict(eng="X", kind="a", name=name, rd=[], wr=wr, cost=0.0, lat=0.0, after=list(sends), n=len(wr), tag=tag[0]))
         return len(ops) - 1
 
     def tt(out, a, b, o): return op("V", "tensor_tensor", out, a, b, o)
@@ -137,43 +160,61 @@ def build():
         return op("V", "tensor_scalar", out, a, s1, s2, o0, o1) if o1 is not None else op("V", "tensor_scalar", out, a, s1, None, o0)
     def cp(out, a): return op("V", "tensor_copy", out, a)
     def ms(out, c): return op("V", "memset", out, c)
+    def scan(out, a, b, o0, o1): return op("V", "tensor_tensor_scan", out, a, b, 0.0, o0, o1)
     def act(out, a, f=AF.Copy, **kw): return op("A", "activation", out, a, f, **kw)
     def dma(q, out, a, **kw): return op(q, "dma_start", out, a, **kw)
     def sel(p): return v("ZC", 15 - p, 143 - p)
 
-    def group_sums(bank, const, src, h0, h1=None):
-        lo, hi = int(1024 * h0), int(1024 * (h0 + 1 if h1 is None else h1))
-        mm(v(bank, 0, (hi - lo) // 16), [(v("NID", 0, 128), const)] + [(sel(p), v(src, lo + p, hi, 16)) for p in range(16)])
+    def stage_to(tb):
+        dma("S", v("PW", 0, 4096, rows=0), v(tb, 0, 256))
+        dma("S", v("PW", 0, 4096, rows=1), v(tb, 256, 512))
 
-    def stage_to(pw, tb, q2="S"):
-        dma("S", v(pw, 0, 4096, rows=0), v(tb, 0, 256))
-        dma(q2, v(pw, 0, 4096, rows=1), v(tb, 256, 512))
+    def stage_from(tb):
+        dma("S", v(tb, 0, 256), v("PW", 0, 4096, rows=0))
+        dma("S", v(tb, 256, 512), v("PW", 0, 4096, rows=1))
 
-    def stage_from(pw, tb):
-        dma("S", v(tb, 0, 256), v(pw, 0, 4096, rows=0))
-        dma("S", v(tb, 256, 512), v(pw, 0, 4096, rows=1))
+    def send_table(k, src, to, after):
+        nm, dst = "t%d" % k, "TB%d" % k
+        if P["tsplit"][k - 2]:
+            m = (512 + XE) // 2
+            arrive(nm, [send(nm, [(v(src, 512, m), v(dst, 512, m)), (v(src, m, XE), v(dst, m, XE))], to, [None, 3], "rest", after=after)])
+        else:
+            arrive(nm, [send(nm, [(v(src, 512, XE), v(dst, 512, XE))], to, after=after)])
 
-    dma("S", v("PXI", 0, 256), hbm("px"))
-    dma("A", v("TB0", X0, X0 + 1024), hbm("x", 0, 1024))
-    dma("S", v("TB0", X0 + 1024, XE), hbm("x", 1024, 2048))
-    dma("A", v("OLI", 0, 128), hbm("ol"))
-    dma("A", v("TLI", 0, 128), hbm("tl"))
-    dma("S", v("NLI", 0, 128), hbm("nl"))
-    dma("A", v("ZT", 0, 128), hbm("z"))
-    ms(v("THI", 0, 8), 0)
-    dma("S", v("THI", 0, 4, rows=0), hbm("th"))
-    ms(v("PWa", 0, 4096), 0.0)
+    cut = [XE - 688 * c for c in range(4)]
+    loads = dict(px=v("PXI", 0, 256), ol=v("OLI", 0, 128), tl=v("TLI", 0, 128), nl=v("NLI", 0, 128), z=v("ZT", 0, 128))
+    was = {}
+
+    def load(names, queues, ahead):
+        for k, nm in enumerate(names):
+            q = queues[k % len(queues)]
+            lo = X0 if nm in loads else max(X0, cut[nm + 1])
+            i = dma(q, loads[nm], hbm(nm)) if nm in loads else dma(q, v("TB0", lo, cut[nm]), hbm("x", lo - X0, cut[nm] - X0))
+            ops[i]["after"], was[q] = [was[q]] if q in was else [], i
+            ops[i]["lat"], ahead = ops[i]["lat"] + ahead, ahead + ops[i]["lat"] - 2100.0
+    load(P["loads"][0], "SA", 0.0)
+    i = ms(v("THI", 0, 8), 0)
+    dma("A", v("THI", 0, 4, rows=0), hbm("th"))
+    ops[-1]["after"] = [was["A"]]
+    ms(v("PW", 0, 4096), 0.0)
+    ops[-1]["after"] = [i]
     op("G", "iota", v("J", 0, 144), [[1, 144]], 0, 0)
     op("G", "iota", v("PID", 0, 1), [[1, 1]], 0, 1)
-    xa = send("xa", [(v("TB0", X0 + 512 * c, X0 + 512 * c + 512), v("TB1", X0 + 512 * c, X0 + 512 * c + 512)) for c in (0, 1)], -1, [0, 2], arr="x1")
-    xb = send("xb", [(v("TB0", X0 + 512 * c, X0 + 512 * c + 512), v("TB1", X0 + 512 * c, X0 + 512 * c + 512)) for c in (2, 3)], -1, [1, 3], arr="x1")
-    x1 = arrive("x1", [xa, xb])
     cp(v("TB0", 0, 256), v("PXI", 0, 256))
     tt(v("TB0", 256, 512), v("PXI", 0, 256), v("TB0", 0, 256), OP.subtract)
-    stage_to("PWa", "TB0")
+    stage_to("TB0")
+    was["S"] = len(ops) - 1
+    load(P["loads"][1], "S", 500.0)
     cp(v("TB0", 512, 520), v("THI", 0, 8))
     tt(v("TB0", 520, 528), v("THI", 0, 8), v("TB0", 512, 520), OP.subtract)
-    arrive("p1", [send("p1", [(v("TB0", 0, X0), v("TB1", 0, X0))], -1, [0], after=[xb])])
+    xs = []
+    for c, ways in enumerate(P["xsend"]):
+        parts = [(v("TB0", lo, lo + 344), v("TB1", lo, lo + 344)) for lo in (cut[c + 1], cut[c + 1] + 344)]
+        xs.append(send("x" + "abcd"[c], parts, -1, ways, "rest" if MATE in ways or MATE2 in ways else "all", arr="x1", after=xs[-1:]))
+        ops[-1]["lat"] = P["xlat"][c]
+    x1 = arrive("x1", xs)
+    p1 = send("p1", [(v("TB0", 0, 512), v("TB1", 0, 512))], -1, [2], after=xs[-1:])
+    arrive("p1", [p1])
     ts(v("PI2", 0, 1), v("PID", 0, 1), 112, OP.bitwise_and)
     ts(v("PI2", 1, 2), v("PID", 0, 1), 15, OP.bitwise_and)
     ts(v("PI2", 2, 3), v("PID", 0, 1), 7, OP.bitwise_and)
@@ -182,14 +223,16 @@ def build():
     g16, pm, p8, pid = [v("PF", j, j + 1) for j in range(4)]
     ts(v("ZC", 0, 144), v("J", 0, 144), 15.0, OP.subtract, g16, OP.is_equal)
     ts(v("NID", 0, 128), v("J", 0, 128), pid, OP.is_equal, -1.0, OP.mult)
-    ms(v("M2K", 0, 64), 2048.0)
+    ms(v("M2K", 0, 128), 2048.0)
     cp(v("OU", 0, 128), v("OLI", 0, 128))
     cp(v("OW", 0, 128), v("OLI", 0, 128))
     act(v("O32", 0, 128), v("OW", 0, 128), AF.Identity, bias=32.0)
     ts(v("CI", 0, 128), v("OLI", 0, 128), 3232.0, OP.mult)
     ts(v("CI2", 0, 128), v("CI", 0, 128), 65535, OP.bitwise_and)
     cp(v("B7", 128, 256), v("NLI", 0, 128))
-    ts(v("ST", 128, 256), v("TLI", 0, 128), -1.0, OP.mult, 99.0, OP.add)
+    ts(v("B4", 128, 256), v("TLI", 0, 128), 99.0, OP.is_lt)
+    ts(v("E", 0, 128), v("TLI", 0, 128), 1.0, OP.add)
+    tt(v("B4", 128, 256), v("B4", 128, 256), v("E", 0, 128), OP.mult)
     cp(v("CO", 0, 128), v("CI2", 0, 128))
     act(v("SF1", 0, 128), sel(1))
     tt(v("S01", 0, 128), sel(0), sel(1), OP.subtract)
@@ -197,39 +240,37 @@ def build():
     ts(v("JM", 0, 128), v("J", 0, 128), 15, OP.bitwise_and)
     ts(v("BD", 0, 128), v("JG", 0, 128), g16, OP.is_equal)
     act(v("BDb", 0, 128), v("BD", 0, 128))
-    ts(v("DM2", 0, 128), v("JM", 0, 128), pm, OP.is_equal)
-    act(v("DM2", 128, 256), v("DM2", 0, 128))
-    ts(v("SEG2", 0, 128), v("JM", 0, 128), 1.0, OP.min)
-    act(v("SEG2", 128, 256), v("SEG2", 0, 128))
-    ts(v("KC", 0, 128), v("J", 0, 128), 255.0, OP.subtract)
-    act(v("KC2", 0, 128), v("KC", 0, 128), scale=-2.0)
-    ts(v("DK0", 0, 8), v("J", 0, 8), -1.0, OP.mult, 127.0, OP.add)
+    ts(v("NDM", 0, 128), v("JM", 0, 128), pm, OP.not_equal)
+    act(v("DM", 0, 128), v("NDM", 0, 128), AF.Identity, scale=-1.0, bias=1.0)
+    ts(v("KC", 0, 128), v("J", 0, 128), -1.0, OP.mult, 255.0, OP.add)
+    act(v("KC2", 0, 128), v("KC", 0, 128), scale=2.0)
     ts(v("LN", 0, 8), v("J", 0, 8), 16.0, OP.mult, pm, OP.add)
-    act(v("OW", 128, 136), v("LN", 0, 8), AF.Identity, scale=32.0, bias=4096.0)
-    act(v("DU", 0, 8), v("LN", 0, 8), AF.Identity, scale=16 / EPS, bias=2048 / EPS - 1)
-    act(v("DU", 8, 16), v("LN", 0, 8), AF.Identity, scale=32 / EPS, bias=4096 / EPS - 1)
-    ts(v("TILE", 0, 8), v("DK0", 0, 8), 0.0, OP.mult, p8, OP.add)
-    ts(v("EN", 0, 1), p8, 1.0, OP.add, 8.0, OP.mult)
-    ts(v("EN", 1, 2), p8, 2.0, OP.add, v("EN", 0, 1), OP.mult)
-    ts(v("ENDS", 0, 1), v("EN", 1, 2), 1.0, OP.subtract)
+    act(v("EN", 4, 5), pm, AF.Identity, bias=4097.0)
+    act(v("OW", 128, 136), v("LN", 0, 8), AF.Identity, scale=0.0, bias=v("EN", 4, 5))
+    ts(v("TILE", 0, 8), v("LN", 0, 8), 0.0, OP.mult, p8, OP.add)
     for nm, x in (("WP0", 2.0), ("WN0", -1.0), ("WP1", 512.0), ("WN1", -256.0)):
         act(v(nm, 0, 144), v("ZC", 0, 144), scale=x)
-    act(v("NIF", 0, 128), v("NID", 0, 128))
+    if far:
+        act(v("NF0", 0, 128), v("NID", 0, 128))
+        act(v("NF1", 0, 128), v("NID", 0, 128), scale=256.0)
     act(v("IDP", 0, 128), v("NID", 0, 128), scale=-1.0)
-    ms(v("CS", 0, 1152), 1.0)
     for j in range(2):
+        w, seg = 8 // P["nb"][j], segments(P["nb"][j])
+        act(v("DU", 8 * j, 8 * j + 8), v("LN", 0, 8), AF.Identity, scale=16 * (j + 1) / EPS, bias=(2048 * (j + 1) + 32 * j) / EPS - 1)
+        ms(v("CS", 576 * j, 576 * j + seg[8]), 1.0)
         for a in range(8):
-            lo = 576 * j
-            act(v("CS", lo + SEGO[a + 1] - 16, lo + SEGO[a + 1]), v("DM2", 0, 16), AF.Identity, scale=v("DU", 8 * j + a, 8 * j + a + 1), bias=1.0)
-            act(v("CS", lo + SEGO[a], lo + SEGO[a] + 1), v("DM2", 0, 1), scale=0.0)
+            lo, hi = 576 * j + seg[a], 576 * j + seg[a + 1]
+            act(v("CS", hi - 16, hi), v("DM", 0, 16), AF.Identity, scale=v("DU", 8 * j + a, 8 * j + a + 1), bias=1.0)
+            act(v("CS", lo, lo + 1), v("DM", 0, 1), scale=0.0)
+        if j and P["nb"][0] == P["nb"][1]: continue
+        ts(v("PI2", 4, 5), v("PID", 0, 1), 1, OP.arith_shift_right, w - 1, OP.bitwise_and)
+        ts(v("PI2", 5, 6), v("PID", 0, 1), w.bit_length(), OP.arith_shift_right, 8 // w - 1, OP.bitwise_and)
+        ts(v("EN", 0, 1), v("PI2", 4, 5), 1.0, OP.add, 8.0, OP.mult)
+        ts(v("EN", 1, 2), v("PI2", 4, 5), 2.0, OP.add, v("EN", 0, 1), OP.mult)
+        ts(v("EN", 2, 3), v("PI2", 5, 6), float(seg[w]), OP.mult, -1.0, OP.add)
+        ts(v("ENDS", 2 * j, 2 * j + 1), v("EN", 1, 2), v("EN", 2, 3), OP.add)
     ms(v("HI", 128, 136), 0)
     ms(v("HI4", 128, 136), 0)
-    for c in range(4):
-        ms(v("PWb", 1024 * c, 1024 * c + 1024), 0.0)
-    o4 = send("o4", [(v("OW", 0, 136), v("OW4", 0, 136))], 4, after=[x1])
-    arrive("o4", [o4])
-    arrive("t2", [send("t2", [(v("TB0", 512, XE), v("TB2", 512, XE))], -2, after=[o4])])
-    stage_to("PWb", "TB1")
 
     def tile_z(zt, pool=False):
         for w in (128, 256):
@@ -238,59 +279,68 @@ def build():
 
     def limits(s, tb):
         mm(v("B5", 256, 264), [(v("BDb", 0, 128), v(tb, 512, 520)), (v("BDb", 0, 128), v(tb, 520, 528))])
-        act(v("L1", s, s + 1), v("B5", 256 + s, 257 + s), AF.Identity, scale=256.0, bias=256.0)
-        act(v("DK", 8 * s, 8 * s + 8), v("DK0", 0, 8), AF.Identity, bias=v("L1", s, s + 1))
+        act(v("L1", s, s + 1), v("B5", 256 + s, 257 + s), AF.Identity, scale=256.0, bias=256.0 + 127.0)
 
-    def distances(tb, offs, zt, scale, c, far):
-        cut = CUT[scale > 1][c]
-        for lo, hi in (((0, cut), (cut, 512)) if cut else ((0, 512),)):
-            a, b = 512 * c + lo, 512 * c + hi
-            w = ind(v(tb, X0, XE), v(offs, a // 16, b // 16))
-            if far:
-                act(v("D", a, b), w)
-                tt(v("AB", a, b), v("D", a, b), v("B6", 0, b - a), OP.max)
-            else:
-                tt(v("D", a, b), w, v(zt, 0, b - a), OP.subtract)
-                act(v("AB", a, b), v("D", a, b), AF.Abs, scale=0.5)
-
-    def dist_sums(bank, const, k, c0, c1, far):
-        out = v(bank, 0, 32 * (c1 - c0))
-        pre = [(v("NID", 0, 128), const, out)]
-        for c in range(c0, c1):
-            if far[c]:
-                o = v(bank, 32 * (c - c0), 32 * (c - c0) + 32)
-                pre += [(v("NIF", 0, 128), v("SZ", 32 * k, 32 * k + 32), o)]
-                pre += [(v("WN%d" % k, 15 - p, 143 - p), v("D", 512 * c + p, 512 * c + 512, 16), o) for p in range(16)]
-        post = [(v("WP%d" % k, 15 - p, 143 - p), v("AB", 512 * c0 + p, 512 * c1, 16), out) for p in range(16)]
-        if len(pre) == 1: mm(out, pre + post)
+    def distances(tb, offs, zt, lo, hi, who):
+        a, b = 16 * lo, 16 * hi
+        w = ind(v(tb, X0, XE), v(offs, lo, hi))
+        if who == "c":
+            act(v("D", a, b), w)
+            for x in range(a, b, P["mw"]):
+                y = min(b, x + P["mw"])
+                tt(v("AB", x, y), v("D", x, y), v("B6", x - a, y - a), OP.max)
+        elif who == "d":
+            o = v(dbank[0], 0, b - a)
+            dbank.reverse()
+            mm(o, [(v("NID", 0, 128), v(zt, 0, b - a))], stop=False)
+            act(v("D", a, b), w)
+            mm(o, [(v("IDP", 0, 128), v("D", a, b))], start=False)
+            act(v("AB", a, b), o, AF.Abs, scale=0.5)
         else:
-            mm(out, pre, stop=False)
-            mm(out, post, start=False)
+            tt(v("D", a, b), w, v(zt, 0, b - a), OP.subtract)
+            if who == "a": ts(v("AB", a, b), v("D", a, b), 0.0, OP.max)
+            else: act(v("AB", a, b), v("D", a, b), AF.Abs, scale=0.5)
+
+    def dist_sums(bank, const, k, lo, hi, pieces):
+        out = v(bank, 0, hi - lo)
+        pre, runs = [const + (out,)], []
+        for a, b, who in pieces:
+            if who == "c": pre.append((v("NF%d" % k, 0, 128), v("SZ", 0, b - a), v(bank, a - lo, b - lo)))
+            if who in "bd": continue
+            if runs and runs[-1][1] == a: runs[-1][1] = b
+            else: runs.append([a, b])
+        mm(out, pre, stop=False)
+        for a, b in runs:
+            mm(v(bank, a - lo, b - lo), [(v("WN%d" % k, 15 - p, 143 - p), v("D", 16 * a + p, 16 * b, 16)) for p in range(16)], False, False)
+        mm(out, [(v("WP%d" % k, 15 - p, 143 - p), v("AB", 16 * lo + p, 16 * hi, 16)) for p in range(16)], start=False)
 
     def spread_z(zt):
+        if not far: return
         mm(v("B6", 0, 512), [(v("IDP", 0, 128), v(zt, 0, 512))])
         mm(v("B5", 384, 416), [(sel(p), v(zt, p, 512, 16)) for p in range(16)])
-        act(v("SZ", 0, 32), v("B5", 384, 416))
-        act(v("SZ", 32, 64), v("B5", 384, 416), scale=256.0)
+        (cp if P["szv"] else act)(v("SZ", 0, 32), v("B5", 384, 416))
 
-    def part_a(s, tb, pw):
-        sends = []
-        act(v("D1", 0, 128), v("ST", 128, 256), AF.Relu, scale=4096.0, bias=-4096.0 * (98 - s))
+    def part_a(s, tb):
+        sends, e_ = [], v("B4", 128, 256)
+        tag[0] = ("road", s)
+        if s == 0 or not P["early"]: road(s, e_, v("D1", 0, 128))
+        if s < S - 1: embargo(s, e_)
         tt(v("NM", 0, 128), v("B7", 128, 256), v("D1", 0, 128), OP.min)
-        for c in range(4):
-            o, w = v("PG", 512 * c, 512 * c + 512), ind(v(pw, 0, 4096), v("OU", 32 * c, 32 * c + 32))
-            if (c % 2 == 0 if s == 0 else PGV[s][c]): cp(o, w)
-            else: act(o, w)
-        for hh, (c0, c1) in enumerate(GRP[s]):
-            b, lo, hi = "B%d" % ((2 + hh) % 4), 32 * c0, 32 * c1
-            group_sums(b, v("D1", lo, hi), "PG", c0 / 2, c1 / 2)
+        for hh, (lo, hi, ps) in enumerate(spans(P["pg"][s])):
+            b, tag[0] = "B%d" % ((2 + hh) % 4), ("pg", s, hh)
+            for x, y, who in ps:
+                (cp if who == "V" else act)(v("PG", 16 * x, 16 * y), ind(v("PW", 0, 4096), v("OU", x, y)))
+            mm(v(b, 0, hi - lo), [(sel(p), v("PG", 16 * lo + p, 16 * hi, 16)) for p in range(16)], stop=False)
+            mm(v(b, 0, hi - lo), [(v("NID", 0, 128), v("D1", lo, hi))], start=False)
             tt(v("RF", lo, hi), v(b, 0, hi - lo), v("NM", lo, hi), OP.max)
-            cp(v("RU", lo, hi), v("RF", lo, hi))
-        for hh, (c0, c1) in enumerate(GRP[s]):
-            b, lo, hi = "B%d" % ((2 + hh) % 4), 32 * c0, 32 * c1
-            for c in range(c0, c1):
-                distances(tb, "RU", "ZT", 1.0, c, FAR[0][s][c])
-            dist_sums(b, v("M2K", 0, hi - lo), 0, c0, c1, FAR[0][s])
+            i = cp(v("RU", lo, hi), v("RF", lo, hi))
+            if s == 0 and hi == 128:
+                send_table(2, "TB0", -2, [i, p1])
+                arrive("o4", [send("o4", [(v("OW", 0, 136), v("OW4", 0, 136))], 4, after=[len(ops) - 2, x1])])
+        for hh, (lo, hi, ps) in enumerate(spans(P["u"][s])):
+            b, tag[0] = "B%d" % ((2 + hh) % 4), ("u", s, hh)
+            for x, y, who in ps: distances(tb, "RU", "ZT", x, y, who)
+            dist_sums(b, (v("NID", 0, 128), v("M2K", 0, hi - lo)), 0, lo, hi, ps)
             tt(v("B7", 384 + lo, 384 + hi), v(b, 0, hi - lo), v("O32", lo, hi), OP.mult)
             tt(v("VI", lo, hi), v("B7", 384 + lo, 384 + hi), v("CO" if s == 0 else "CA", lo, hi), OP.add)
             ts(v("HI", lo, hi), v("VI", lo, hi), 5, OP.arith_shift_right, 2047, OP.bitwise_and)
@@ -298,224 +348,385 @@ def build():
                 sends.append(send("h%d" % hh, [(v("HI", lo, hi), v("HI4", lo, hi))], 4, after=sends[-1:]))
                 arrive("h%d" % hh, sends[-1:])
 
-    def part_c(s, tb, pw, hi, ow, st, zt):
+    def road(s, e_, out):
+        act(v("E", 0, 128), e_, AF.Abs, bias=-(s + 2) / 2)
+        act(out, v("E", 0, 128), AF.Relu, scale=-4096.0, bias=4096.0 * (s + 2) / 2)
+
+    def embargo(s, e_):
+        act(v("E2", 0, 128), e_, AF.Relu, scale=2.0 ** 21, bias=-(s + 1) * 2.0 ** 21)
+
+    def clash(s, j, banks, vv, sc, out):
+        w, seg, (a1, a2), lo = 8 // P["nb"][j], segments(P["nb"][j]), P["eqa"][s][j], 576 * j
+        e = 2 * j if P["nb"][0] != P["nb"][1] else 0
+        for b, x in banks[:2 if 0 < a2 - a1 < 8 else 1]: mm(v(b, x, x + 128), [(v("BD", 0, 128), v(vv, 0, 128))])
+        scan(v(sc, 0, 128), v("NDM", 0, 128), v(vv, 0, 128), OP.mult, OP.add)
+        for a in range(8):
+            on = a1 <= a < a2
+            b, x = banks[1 if on and a2 - a1 < 8 else 0]
+            c, was = v(sc, 15 + 16 * a, 16 + 16 * a), v(b, x + 16 * (a - a % w), x + 16 * a + 16)
+            if on: act(v("EA", lo + seg[a], lo + seg[a + 1]), was, AF.Abs, scale=-1.0, bias=c)
+            else: ts(v("EQ", lo + seg[a], lo + seg[a + 1]), was, c, OP.is_equal, EPS, OP.mult)
+        if a2 > a1: act(v("EQ", lo + seg[a1], lo + seg[a2]), v("EA", lo + seg[a1], lo + seg[a2]), AF.Relu, scale=-EPS, bias=EPS)
+        scan(v("SP", lo, lo + seg[8]), v("CS", lo, lo + seg[8]), v("EQ", lo, lo + seg[8]), OP.mult, OP.max)
+        tt(v("OF", 16 * j, 16 * j + 16), ind(v("SP", lo, lo + seg[8]), v("ENDS", e, e + 1)), v(sc, 7, 128, 8), OP.max)
+        cp(out, v("OF", 16 * j + 1, 16 * j + 16, 2))
+
+    def scatter(j, win, offs, lo, src):
+        w = 8 // P["nb"][j]
+        for a in range(8 - w, -1, -w):
+            cp(ind(win, v(offs, lo + a, lo + a + w)), v(src, 16 * a, 16 * (a + w)))
+
+    def put_x(tb, xm):
+        scatter(0, v(tb, X0, XD), xm, 128, xm)
+
+    def part_c(s, tb, hi, ow, zt):
         last = s == S - 1
-        n_, t_ = (v(st, 0, 128) if last else v("B7", 128, 256)), v(st, 128, 256)
-        half = (99.0 - s) / 2
-        act(v("E", 0, 128), t_, AF.Abs, bias=-half)
-        act(v("DT", 0, 128), t_, AF.Identity, scale=-1.0, bias=97.0 - s)
-        act(v("E2", 0, 128), v("E", 0, 128), AF.Relu, scale=-2.0 ** 21, bias=half * 2.0 ** 21)
+        n_, e_ = (v("ST4", 0, 128), v("ST4", 128, 256)) if last else (v("B7", 128, 256), v("B4", 128, 256))
+        if last: embargo(s, e_)
         act(v("LT", 0, 128), v("E2", 0, 128), AF.Identity, scale=-1.0, bias=v("L1", s, s + 1))
-        for hh in range(2):
-            lo = 64 * hh
-            for c in (2 * hh, 2 * hh + 1):
-                for c0, c1 in GRP[s]:
-                    if c0 == c: cp(v("HU", 32 * c0, 32 * c1), v(hi, 32 * c0, 32 * c1))
-                distances(tb, "HU", zt, 256.0, c, FAR[1][s][c])
-            dist_sums("B%d" % hh, v("KC", lo, lo + 64), 1, 2 * hh, 2 * hh + 2, FAR[1][s])
+        cuts = [(lo, hi_) for lo, hi_, _ in spans(P["u"][s])]
+        groups = spans(P["d"][s])
+        banks = ["B0", "B1", "B3", "B2"]
+        for hh, (lo, up, ps) in enumerate(groups):
+            tag[0] = ("d", s, hh)
+            for x, y, who in ps:
+                while cuts and cuts[0][0] < y:
+                    cp(v("HU", *cuts[0]), v(hi, *cuts[0])); cuts.pop(0)
+                distances(tb, "HU", zt, x, y, who)
+            dist_sums(banks[hh], (v("IDP", 0, 128), v("KC", lo, up)), 1, lo, up, ps)
         tt(v("HN", 0, 128), v(hi, 0, 128), n_, OP.subtract)
-        cp(v("KS", 0, 64), v("B0", 0, 64))
-        tt(v("KN", 0, 64), v("KC2", 0, 64), v("B0", 0, 64), OP.subtract)
-        tt(v("H1", 0, 32), v("KS", 0, 32), v("KS", 32, 64), OP.max)
-        tt(v("H1", 0, 8), v("H1", 0, 8), v("DK", 8 * s, 8 * s + 8), OP.max)
-        tt(v("H1", 32, 64), v("KN", 0, 32), v("KN", 32, 64), OP.max)
-        tt(v("B7", 0, 64), v("B0", 0, 64), v("LT", 0, 64), OP.is_lt)
-        tt(v("KN", 64, 128), v("KC2", 64, 128), v("B1", 0, 64), OP.subtract)
-        for j, (b, lo) in enumerate((("B1", 0), ("KN", 64))):
-            tt(v("H2", 32 * j, 32 * j + 32), v(b, lo, lo + 32), v("H1", 32 * j, 32 * j + 32), OP.max)
-            tt(v3("TR", 32, j, j + 1, 0, 32), v(b, lo + 32, lo + 64), v("H2", 32 * j, 32 * j + 32), OP.max)
+        for hh, (lo, up, ps) in enumerate(groups):
+            b, tag[0] = banks[hh], ("tree", s, hh)
+            tt(v("KN", lo, up), v("KC2", lo, up), v(b, 0, up - lo), OP.subtract)
+            for x in range(lo, up, 32):
+                w = min(32, up - x)
+                t0, t1 = v3("TR", 32, 0, 1, 0, w), v3("TR", 32, 1, 2, 0, w)
+                if x == 0: ts(t0, v(b, 0, w), v("L1", s, s + 1), OP.max)
+                else: tt(t0, v(b, x - lo, x - lo + w), t0, OP.max)
+                if x == 32: tt(t1, v("KN", 0, 32), v("KN", 32, 64), OP.max)
+                elif x: tt(t1, v("KN", x, x + w), t1, OP.max)
+            tt(v("B7", lo, up), v(b, 0, up - lo), v("LT", lo, up), OP.is_lt)
         tt(v3("TR2", 16, 0, 2, 0, 16), v3("TR", 32, 0, 2, 0, 16), v3("TR", 32, 0, 2, 16, 32), OP.max)
         tt(v3("MM", 8, 0, 2, 0, 8), v3("TR2", 16, 0, 2, 0, 8), v3("TR2", 16, 0, 2, 8, 16), OP.max)
         ts(v3("MA", 8, 0, 2, 0, 8), v3("MM", 8, 0, 2, 0, 8), 255, OP.bitwise_and)
         ts(v3("CU", 8, 0, 2, 0, 8), v3("MA", 8, 0, 2, 0, 8), -1.0, OP.mult, 255.0, OP.add)
-        tt(v("B7", 64, 128), v("B1", 0, 64), v("LT", 64, 128), OP.is_lt)
-        act(v("KS", 64, 128), v("B1", 0, 64))
+        red, tag[0] = v("B7", 0, 128), ("count", s)
+        rr = v("B4", 256, 384) if last else v("RR", 0, 128)
+        if last: act(rr, red, scale=s + 3.0)
+        else:
+            act(rr, red, scale=s + 3.0, accum_out=v("RS", 0, 1))
+            mm(v("B5", 272, 273), [(v("BD", 0, 128), v("RS", 0, 1))])
+            act(v("A32", 0, 1), v("B5", 272, 273), scale=32.0 / (s + 3))
+            act(v("CA", 0, 128), v("CO", 0, 128), AF.Identity, bias=v("A32", 0, 1))
         cj, cb, jb = [v3("CU", 8, j, j + 1, 0, 8) for j in range(3)]
-        tt(v("VV", 256, 384), ind(v(ow, 0, 136), cj), v("DM2", 0, 128), OP.mult)
-        tt(v("VV", 128, 256), ind(v(hi, 0, 136), cb), v("DM2", 0, 128), OP.mult)
-        tt(v("VV", 0, 128), ind(v(hi, 0, 136), cj), v("DM2", 0, 128), OP.mult)
-        mm(v("B4", 0, 128), [(v("BD", 0, 128), v("VV", 256, 384))])
-        mm(v("B5", 0, 128), [(v("BD", 0, 128), v("VV", 128, 256))])
-        op("V", "tensor_tensor_scan", v("SC", 0, 256), v("SEG2", 0, 256), v("VV", 128, 384), 0.0, OP.mult, OP.add)
-        for j in range(2):
-            lo, b, a0 = 576 * j, "B%d" % (5 - j), EQA[s][j]
-            b2 = "B%d" % (3 - j) if 0 < a0 < 8 else b
-            if b2 != b: mm(v(b2, 0, 16 * a0), [(v("BD", 0, 128), v("VV", 128 + 128 * j, 128 + 128 * j + 16 * a0))])
-            for a in range(8):
-                c = v("SC", 128 * j + 15 + 16 * a, 128 * j + 16 + 16 * a)
-                if a >= a0: act(v("EA", lo + SEGO[a], lo + SEGO[a + 1]), v(b, 0, 16 * a + 16), AF.Abs, scale=-1.0, bias=c)
-                else: ts(v("EQ", lo + SEGO[a], lo + SEGO[a + 1]), v(b2, 0, 16 * a + 16), c, OP.is_equal, EPS, OP.mult)
-            if a0 < 8: act(v("EQ", lo + SEGO[a0], lo + 576), v("EA", lo + SEGO[a0], lo + 576), AF.Relu, scale=-EPS, bias=EPS)
-        xm = "XM%d" % s
-        for j in (1, 0):
-            lo = 576 * j
-            op("V", "tensor_tensor_scan", v("SP", lo, lo + 576), v("CS", lo, lo + 576), v("EQ", lo, lo + 576), 0.0, OP.mult, OP.max)
-            tt(v("OF", 16 * j, 16 * j + 16), ind(v("SP", lo, lo + 576), v("ENDS", 0, 1)), v("SC", 15, 256, 16), OP.max)
-            cp(v(xm, 128 + 8 * j, 136 + 8 * j), v("OF", 24 * j, 24 * j + 8))
+        tag[0] = ("p", s)
+        tt(v("VO", 0, 128), ind(v(ow, 0, 136), cj), v("DM", 0, 128), OP.mult)
+        clash(s, 1, [("B4", 0), ("B3", 256)], "VO", "SO", v("XP", 0, 8))
+        tag[0] = ("pv", s)
+        tt(v("VH", 0, 128), ind(v(hi, 0, 136), cj), v("DM", 0, 128), OP.mult)
         if not last:
-            act(v("VHH", 0, 128), v("VV", 0, 128))
-            mm(v("B0", 256, 384), [(v("SF1", 0, 128), v("VV", 0, 128)), (v("S01", 0, 128), v("VHH", 0, 128))])
+            act(v("VHH", 0, 128), v("VH", 0, 128))
+            mm(v("B0", 256, 384), [(v("SF1", 0, 128), v("VH", 0, 128)), (v("S01", 0, 128), v("VHH", 0, 128))])
             act(v("PV", 0, 128), v("B0", 256, 384))
-            cp(ind(v(pw, 0, 8192), v(xm, 136, 144)), v("PV", 0, 128))
+            scatter(1, v("PW", 0, PD), "XP", 0, "PV")
         else:
-            mm(v("B0", 256, 384), [(v("BD", 0, 128), v("VV", 0, 128))])
+            mm(v("B0", 256, 384), [(v("BD", 0, 128), v("VH", 0, 128))])
             act(v("PF3", 0, 128), v("B0", 256, 384))
-            cp(ind(v(pw, 0, 8192), v(xm, 136, 144)), v("PF3", 0, 128))
-            dma("S", hbm("yp"), v(pw, 0, 4096, rows=0))
-        cp(jb, v("SC", 15, 128, 16))
-        tt(v("ZS", 0, 128), ind(v(tb, X0, XE), jb), v(zt, 0, 128), OP.add)
-        if ZPE[s]:
-            act(v("E2", 0, 128), v("ZS", 0, 128), AF.Identity, bias=-0.5)
-            act(v("ZM", 0, 128), v("E2", 0, 128), AF.Identity, bias=BIG)
+            scatter(1, v("PWF", 0, PD), "XP", 0, "PF3")
+            dma("S", hbm("yp"), v("PWF", 0, 4096, rows=0))
+        xm, tag[0] = "XM%d" % s, ("x", s)
+        tt(v("VB", 0, 128), ind(v(hi, 0, 136), cb), v("DM", 0, 128), OP.mult)
+        clash(s, 0, [("B1", 256), ("B5", 0)], "VB", "SB", v(xm, 128, 136))
+        tag[0] = ("z", s)
+        cp(jb, v("SB", 15, 128, 16))
+        if P["zsa"][s]:
+            zs = v("B1", 384, 512)
+            mm(zs, [(v("IDP", 0, 128), v(zt, 0, 128))], stop=False)
+            act(v("GB", 0, 128), ind(v(tb, X0, XE), jb))
+            mm(zs, [(v("IDP", 0, 128), v("GB", 0, 128))], start=False)
         else:
-            ts(v("ZM", 0, 128), v("ZS", 0, 128), -0.5, OP.add, BIG, OP.add)
-        act(v(zt, 0, 128), v("ZM", 0, 128), AF.Identity, scale=0.5, bias=-BIG / 2)
+            zs = v("ZS", 0, 128)
+            tt(zs, ind(v(tb, X0, XE), jb), v(zt, 0, 128), OP.add)
+        ts(v(xm, 0, 128), zs, 0.5, OP.mult, -0.25, OP.add)
+        cp(v(zt, 0, 128), v(xm, 0, 128))
         if not last:
             to, nxt = (3 if s == 2 else -1), "TB%d" % (s + 2)
-            cp(v(xm, 0, 128), v(zt, 0, 128))
-            sx = send("dx%d" % s, [(v(xm, 0, 136), v("XL%d" % s, 0, 136))], to, [2], "rest")
+            w = 136
+            sx = send("dx%d" % s, [(v(xm, 0, w), v("XL%d" % s, 0, w))], to, [0])
             arrive("dx%d" % s, [sx])
-            stage_from(pw, tb)
-            arrive("ps%d" % s, [send("ps%d" % s, [(v(tb, 0, 512), v(nxt, 0, 512))], to, [3], "rest", after=[sx])])
+            stage_from(tb)
+            parts = [(v(tb, c, c + 256), v(nxt, c, c + 256)) for c in (0, 256)] if P["pssplit"] else [(v(tb, 0, 512), v(nxt, 0, 512))]
+            sp = send("ps%d" % s, parts, to, [3, 1][:len(parts)], "rest", after=[sx])
+            arrive("ps%d" % s, [sp])
             tile_z(zt, True)
             spread_z(zt)
-        cp(ind(v(tb, X0, XD), v(xm, 128, 136)), v(zt, 0, 128))
-        if s < 2:
-            nm = "t%d" % (s + 3)
-            arrive(nm, [send(nm, [(v(tb, 512, XE), v("TB%d" % (s + 3), 512, XE))], 2 if s else -2, after=[sx])])
+        put_x(tb, xm)
+        if s < 2: send_table(s + 3, tb, 2 if s else -2, [sp])
         if last:
             dma("S", hbm("yx", 0, 1024), v(tb, X0, X0 + 1024))
             dma("A", hbm("yx", 1024, 2048), v(tb, X0 + 1024, XE))
             dma("S", hbm("yz"), v(zt, 0, 128))
-        red = v("B7", 0, 128)
-        tt(v("NE", 0, 128), ind(v3("MM", 8, 0, 1, 0, 8), v("TILE", 0, 8)), v("KS", 0, 128), OP.not_equal)
-        for lo in (0, 64):
-            r, u, nn = v("B7", lo, lo + 64), v("B7", 256 + lo, 320 + lo), v(n_[1], n_[3] + lo, n_[3] + lo + 64)
-            tt(u, r, v("DT", lo, lo + 64), OP.mult)
-            tt(u, u, v(st, 128 + lo, 192 + lo), OP.add)
-            tn = v("B7", 128 + lo, 192 + lo) if last else v("HN", lo, lo + 64)
-            tt(tn, r, v("HN", lo, lo + 64), OP.mult)
-            tt(nn, tn, nn, OP.add)
-        tt(t_, v("B7", 256, 384), v("NE", 0, 128), OP.mult)
-        if s == S - 2: act(v(st, 0, 128), n_)
+        e1, tag[0] = (rr if last else e_), ("date", s)
+        tt(e1, e_, rr, OP.max)
+        if P["early"] and not last: road(s + 1, e1, v("B5", 128, 256))
+        if P["nea"][s]:
+            cp(v("MB", 0, 8), v3("MA", 8, 0, 1, 0, 8))
+            mm(v("B3", 128, 256), [(v("NID", 0, 128), v("KC", 0, 128))] + [(v("IDP", 0, 128), v("MB", 0, 8), v("B3", 128 + 8 * k, 136 + 8 * k)) for k in range(16)])
+            act(v("NE", 0, 128), v("B3", 128, 256), AF.Abs, scale=128.0)
+            tt(e_, e1, v("NE", 0, 128), OP.min)
+        else:
+            tt(v("NE", 0, 128), ind(v3("MA", 8, 0, 1, 0, 8), v("TILE", 0, 8)), v("KC", 0, 128), OP.not_equal)
+            if P["early"] and not last: tt(v("D1", 0, 128), v("B5", 128, 256), v("NE", 0, 128), OP.mult)
+            tt(e_, e1, v("NE", 0, 128), OP.mult)
+        tn, tag[0] = (red if last else v("HN", 0, 128)), ("name", s)
+        tt(tn, red, v("HN", 0, 128), OP.mult)
+        tt(n_, tn, n_, OP.add)
+        if s == S - 2:
+            act(v("ST", 0, 128), n_)
+            act(v("ST", 128, 256), e_)
         if last:
             dma("S", hbm("yn"), n_)
-            act(v("YT", 0, 128), t_, AF.Identity, scale=-1.0, bias=99.0)
+            act(rr, e_, AF.Identity, scale=-100.0, bias=99.0)
+            act(v("E", 0, 128), e_, AF.Identity, bias=-1.0)
+            tt(v("YT", 0, 128), rr, v("E", 0, 128), OP.max)
             dma("A", hbm("yt"), v("YT", 0, 128))
-        else:
-            act(v("JK", 0, 128), red, accum_out=v("RS", 0, 1))
-            mm(v("B4", 256, 257), [(v("BD", 0, 128), v("RS", 0, 1))])
-            act(v("A32", 0, 1), v("B4", 256, 257), scale=32.0)
-            act(v("CA", 0, 128), v("CO", 0, 128), AF.Identity, bias=v("A32", 0, 1))
-
-    def take_x(s, tb):
-        cp(ind(v(tb, X0, XD), v("XL%d" % s, 128, 136)), v("XL%d" % s, 0, 128))
 
     tile_z("ZT")
     limits(3, "TB0")
     spread_z("ZT")
-    part_a(0, "TB0", "PWa")
-    limits(0, "TB1")
-    part_c(0, "TB1", "PWb", "HI", "OW", "ST", "ZT")
-    part_a(1, "TB1", "PWb")
-    limits(1, "TB2")
-    stage_to("PWa", "TB2")
-    take_x(0, "TB2")
-    part_c(1, "TB2", "PWa", "HI", "OW", "ST", "ZT")
-    part_a(2, "TB2", "PWa")
-    limits(2, "TB3")
-    stage_to("PWb", "TB3")
-    take_x(1, "TB3")
-    part_c(2, "TB3", "PWb", "HI", "OW", "ST", "ZT")
+    for s in range(S - 1):
+        part_a(s, "TB%d" % s)
+        tb = "TB%d" % (s + 1)
+        limits(s, tb)
+        stage_to(tb)
+        if s: put_x(tb, "XL%d" % (s - 1))
+        part_c(s, tb, "HI", "OW", "ZT")
     arrive("z4", [send("z4", [(v("ZT", 0, 128), v("ZT4", 0, 128))], 4)])
     arrive("s4", [send("s4", [(v("ST", 0, 256), v("ST4", 0, 256))], 4)])
-    part_a(3, "TB3", "PWb")
+    part_a(3, "TB3")
+    tag[0] = ("land", 3)
     tile_z("ZT4")
-    take_x(2, "TB4")
+    put_x("TB4", "XL2")
     spread_z("ZT4")
     mm(v("B4", 128, 384), [(v("NID", 0, 128), v("TB4", 0, 256)), (v("NID", 0, 128), v("TB4", 256, 512))])
     act(v("PFC", 0, 256), v("B4", 128, 384), scale=-1.0)
     dma("S", v("PWF", 0, 4096, rows=0), v("PFC", 0, 256))
-    part_c(3, "TB4", "PWF", "HI4", "OW4", "ST4", "ZT4")
+    part_c(3, "TB4", "HI4", "OW4", "ZT4")
     return ops
 
 
-def analyse():
-    ops = build()
+def analyse(P):
+    ops = build(P)
     n = len(ops)
     hist = {}
     for i, o in enumerate(ops):
-        deps = set(o["after"])
+        deps, hard = set(o["after"]), set(j for j in o["after"] if ops[j]["kind"] != "d")
         for acc, w in [(a, False) for a in o["rd"]] + [(a, True) for a in o["wr"]]:
             ps = SCRATCH[acc[1]][0] == "psum"
             for (j, lo, hi, w2, rows) in hist.get(acc[1], []):
                 if j == i: continue
                 meet = lo < acc[4] and acc[3] < hi and (w or w2)
                 if meet and rows != acc[2][0] and rows != slice(None) and acc[2][0] != slice(None): meet = False
-                if meet or (ps and ops[j]["eng"] != o["eng"]): deps.add(j)
+                if ps and o["kind"] == "m" and ops[j]["kind"] == "m": deps.add(j)
+                elif meet:
+                    deps.add(j)
+                    same = ops[j]["eng"] == o["eng"] and o["kind"] == "c" and ops[j]["kind"] == "c"
+                    both = o["out"][0] == "i" and ops[j]["out"][0] == "i" if same else False
+                    if not (same and w and (P["soft"] == 2 or (P["soft"] == 1 and both))): hard.add(j)
         for acc, w in [(a, False) for a in o["rd"]] + [(a, True) for a in o["wr"]]:
             hist.setdefault(acc[1], []).append((i, acc[3], acc[4], w, acc[2][0]))
-        o["deps"] = deps
-    succ = [[] for _ in range(n)]
-    for i, o in enumerate(ops):
-        for j in o["deps"]: succ[j].append(i)
+        o["deps"], o["hard"] = deps, hard
+        o["far"] = set(deps).union(*[ops[j]["far"] for j in deps])
+        o["near"] = sorted(j for j in deps if ops[j]["kind"] in "rd" or not any(j in ops[k]["far"] for k in deps if ops[k]["kind"] in "cm" and k in hard))
+        o["banks"] = sorted(set(a[1] for a in o["rd"] + o["wr"] if SCRATCH[a[1]][0] == "psum"))
+    return ops
 
-    def delay(j, i):
-        if ops[j]["kind"] == "r": return ops[j]["lat"] if ops[i]["kind"] == "a" else 0.0
-        return ops[j]["lat"] + (0.0 if ops[j]["kind"] == "a" else LAT)
-    prio = [0.0] * n
-    for i in range(n - 1, -1, -1):
-        prio[i] = ops[i]["cost"] + max([delay(i, k) + prio[k] for k in succ[i]] + [ops[i]["lat"]])
-    prio[0] += 1e6
-    kin = {}
+
+def graph(ops, speed):
+    cy, ga, sca, lat, same, link, vfix, afix = speed
+    cost, pre = [], []
     for i, o in enumerate(ops):
-        x = o.get("out") or ("v", o["name"], 0, 0, 0)
+        c = o["cost"]
+        if o.get("var"): c = FIX + (ga if o["var"][0] == "g" else sca) * o["var"][1] * cy
+        elif o["kind"] == "m": c = (c - 60) * cy + 50
+        elif o["kind"] == "c": c = max(AMIN, c - AFIX) * cy + afix if o["eng"] == "A" else c * cy + vfix
+        cost.append(c)
+        e = []
+        for j in o["near"]:
+            p = ops[j]
+            if p["kind"] == "r": d = p["lat"] * link if o["kind"] == "a" else 0.0
+            elif j not in o["hard"] or p["kind"] == "a": d = 0.0
+            else: d = p["lat"] + (same if p["eng"] == o["eng"] else lat)
+            e.append((j, d))
+        pre.append(e)
+    return cost, pre, lat
+
+
+def place(ops, seq, cost, pre, lat, head):
+    st, en = [0.0] * len(ops), [0.0] * len(ops)
+    qs, bs = {e: [(-1e9, -1e9)] for e in "VAPGS"}, {"B%d" % b: [(-1e9, -1e9, "")] for b in range(8)}
+    for i in seq:
+        c, e, banks, t = cost[i], ops[i][0], ops[i][1], head[i]
+        for j, d in pre[i]:
+            if en[j] + d > t: t = en[j] + d
+        if e != "X":
+            q = qs[e]
+            n = len(q)
+            while True:
+                p = n
+                while q[p - 1][1] > t: p -= 1
+                while p < n and q[p][0] < t + c - 1e-6:
+                    t = q[p][1]; p += 1
+                t0 = t
+                for b in banks:
+                    r = bs[b]
+                    k = m = len(r)
+                    while r[k - 1][1] + lat > t: k -= 1
+                    while k < m and r[k][0] < t + c + lat:
+                        if r[k][2] != e and t < r[k][1] + lat: t = r[k][1] + lat
+                        k += 1
+                if t == t0: break
+            q.insert(p, (t, t + c))
+            for b in banks:
+                r = bs[b]
+                k = len(r)
+                while r[k - 1][0] > t: k -= 1
+                r.insert(k, (t, t + c, e))
+        st[i], en[i] = t, t + c
+    return st, en
+
+
+def in_turn(key, pre, order):
+    key = list(key)
+    for i in order:
+        for j, _ in pre[i]:
+            if key[j] >= key[i]: key[i] = key[j] + 1e-3
+    return sorted(order, key=lambda i: key[i])
+
+
+def turns(ops, order):
+    last, out = {"B%d" % b: {} for b in range(8)}, [()] * len(ops)
+    for i in order:
+        e, banks = ops[i]["eng"], ops[i]["banks"]
+        if banks:
+            out[i] = [j for b in banks for e2, j in last[b].items() if e2 != e]
+            for b in banks: last[b][e] = i
+    return out
+
+
+def replay(ops, order, turn, tail, cost, pre, lat):
+    en, free, m = [0.0] * len(ops), dict.fromkeys("VAPGSX", 0.0), 0.0
+    for i in order:
+        e = ops[i]["eng"]
+        t = free[e]
+        for j, d in pre[i]:
+            if en[j] + d > t: t = en[j] + d
+        for j in turn[i]:
+            if en[j] + lat > t: t = en[j] + lat
+        t += cost[i]
+        en[i] = t
+        if e != "X": free[e] = t
+        if t + tail[i] > m: m = t + tail[i]
+    return m
+
+
+def best_order(ops, tries, seed=1):
+    n = len(ops)
+    up, down, zero = list(range(n)), list(range(n - 1, -1, -1)), [0.0] * n
+    gs = [graph(ops, s) for s in SPEEDS]
+    cost, pre, lat = gs[0]
+    suc = [[] for _ in up]
+    for i in up:
+        for j, d in pre[i]: suc[j].append((i, d))
+    tail = [0.0 if o["kind"] == "r" else o["lat"] for o in ops]
+    kin, stage = {}, {}
+    for i, o in enumerate(ops):
+        stage.setdefault(o["tag"], []).append(i)
+        x = o.get("out") or ("v", o["name"], 0, 0)
         x = x[1] if x[0] == "i" else x
-        o["kin"] = kin.setdefault((o["eng"], o.get("meth"), x[1].rstrip("0123456789ab"), x[3], len(o["rd"]), o["cost"]), [])
+        o["kin"] = kin.setdefault((o["eng"], o.get("meth"), x[1].rstrip("0123456789"), x[3], len(o["rd"]), o["cost"]), [])
         o["kin"].append(i)
-    return ops, succ, prio, delay
+    x, bar, where = [seed], [1e9], [(o["eng"], o["banks"]) for o in ops]
+
+    def rnd():
+        x[0] = (x[0] * 6364136223846793005 + 1442695040888963407) % 2 ** 64
+        return (x[0] >> 11) / 2.0 ** 53
+
+    def forth(key):
+        st, en = place(where, in_turn(key, pre, up), cost, pre, lat, zero)
+        m = max(en[i] + tail[i] for i in up)
+        if m > bar[0]: return 2 * m, st, en
+        order = in_turn(st, pre, up)
+        turn = turns(ops, order)
+        ms = [m] + [replay(ops, order, turn, tail, *g) for g in gs[1:]]
+        return sum(m * w for m, w in zip(ms, WEIGHTS)), st, en, order, ms
+
+    def back(r):
+        en = place(where, in_turn([-(r[2][i] + tail[i]) for i in up], suc, down), cost, suc, lat, tail)[1]
+        return forth([-y for y in en])
+
+    def tight(r):
+        st, en, order = r[1:4]
+        before, last, turn = {}, {}, turns(ops, order)
+        for i in order:
+            before[i] = last.get(ops[i]["eng"]); last[ops[i]["eng"]] = i
+        i, out = max(up, key=lambda i: en[i] + tail[i]), []
+        while True:
+            c = [j for j, d in pre[i] if abs(en[j] + d - st[i]) < 0.01]
+            if not c:
+                c = [j for j in turn[i] if abs(en[j] + lat - st[i]) < 0.01]
+                j = before[i]
+                if j is not None and ops[i]["eng"] != "X" and abs(en[j] - st[i]) < 0.01: c.append(j)
+                if not c: return out or [(0, 1)]
+                out.append((c[0], i))
+            i = c[0]
+    chain = [None, None]
+    long = list(tail)
+    for i in down: long[i] = cost[i] + max([d + long[k] for k, d in suc[i]] + [tail[i]])
+    long[0] += 1e6
+    best = cur = forth([-y for y in long])
+    for it in range(tries):
+        key, u, i = list(cur[1]), rnd(), int(rnd() * n)
+        d = (1 if rnd() < 0.5 else -1) * 10 ** (1.8 + 1.6 * rnd())
+        if rnd() < CRIT:
+            if chain[0] is not cur: chain[:] = [cur, tight(cur)]
+            a, b = chain[1][int(rnd() * len(chain[1]))]
+            i, d = (b, key[a] - key[b] - 1) if rnd() < 0.5 else (a, key[b] - key[a] + 1)
+            if rnd() < 0.3: d *= 1 + 4 * rnd()
+        some = set(ops[i]["kin"] if rnd() < 0.5 else [i])
+        if u < 0.35:
+            edge = set(some)
+            for _ in range(1 + int(5 * rnd())):
+                edge = set(j for a in sorted(edge) for j, _d in (pre if d < 0 else suc)[a] if abs(key[j] - key[a]) < abs(d) + 600 and rnd() < 0.8) - some
+                some |= edge
+        elif u < 0.6:
+            for a in sorted(some):
+                some |= set(j for j in stage[ops[a]["tag"]] if (j > a) == (d > 0))
+        if u < 0.9:
+            for j in some: key[j] += d
+        else: key = [y + 120 * (rnd() - 0.5) for y in key]
+        bar[0] = cur[4][0] + 700.0
+        new = forth(key)
+        if rnd() < 0.3: new = min(new, back(new), key=lambda r: r[0])
+        if new[0] <= cur[0] + TEMP * (1 - it / tries) * -math.log(1 - rnd()): cur = new
+        if new[0] < best[0]: best = new
+    return best
 
 
-def schedule(ops, succ, prio, delay):
-    n, prio = len(ops), list(prio)
-    for x in NUDGE:
-        for i in (ops[x % n]["kin"] if x // (41 * n) else [x % n]):
-            prio[i] += 150.0 * (x // n % 41 - 20)
-    left = [len(o["deps"]) for o in ops]
-    ready = {i: 0.0 for i in range(n) if left[i] == 0}
-    free, end, order = {}, [0.0] * n, []
-    while ready:
-        best = None
-        for e in set(ops[i]["eng"] for i in ready):
-            mine = [i for i in ready if ops[i]["eng"] == e]
-            t = max(free.get(e, 0.0), min(ready[i] for i in mine))
-            c = max([i for i in mine if ready[i] <= t], key=lambda i: (prio[i], -i))
-            soon = [i for i in mine if prio[i] > prio[c] + 2 * ops[c]["cost"] and ready[i] < t + 0.5 * ops[c]["cost"]]
-            if soon:
-                c = min(soon, key=lambda i: ready[i]); t = max(t, ready[c])
-            if best is None or (t, e) < best[:2]: best = (t, e, c)
-        t, e, c = best
-        del ready[c]
-        end[c] = t + ops[c]["cost"]; ops[c]["t"] = t
-        if e != "X": free[e] = end[c]
-        order.append(c)
-        for k in succ[c]:
-            left[k] -= 1
-            if left[k] == 0: ready[k] = max(end[j] + delay(j, k) for j in ops[k]["deps"])
-    return order, end
-
-
-def plan():
-    ops, succ, prio, delay = analyse()
-    order, end = schedule(ops, succ, prio, delay)
+def plan(P):
+    ops = analyse(P)
+    _, start, end, order, ms = best_order(ops, P["tries"])
+    turn = turns(ops, order)
     cnt, known, sems = {}, {}, []
     for i in order:
         o = ops[i]
+        o["deps"], o["hard"] = o["deps"] | set(turn[i]), o["hard"] | set(turn[i])
+        o["t"] = start[i]
         if o["kind"] == "a":
             o["sig"] = ("a_" + o["name"], None); o["vc"] = {}; sems.append(o["sig"][0]); continue
         vc = known.setdefault(o["eng"], {})
         waits = []
-        for j in sorted(o["deps"], key=lambda j: -end[j]):
+        for j in sorted(o["hard"], key=lambda j: -end[j]):
             p = ops[j]
             if p["kind"] == "r":
                 assert o["kind"] == "r"
@@ -530,20 +741,48 @@ def plan():
             o["sig"] = ("d%d" % i, 16); sems.append(o["sig"][0])
         elif o["kind"] != "r":
             cnt[o["eng"]] = cnt.get(o["eng"], 0) + 1; o["sig"] = ("q" + o["eng"], cnt[o["eng"]])
-    sems += ["q" + e for e in cnt] + ["sent"] + ["r_" + o["name"] for o in ops if o["kind"] == "r" and o["relays"] is not None]
+    sems += ["q" + e for e in cnt] + ["sent"] + ["r_" + o["name"] for o in ops if o["kind"] == "r" and o["relays"] != [None]]
     return ops, order, cnt, sems
 
 
-OPS, ORDER, COUNTS, SEMAPHORES = plan()
+OPS, ORDER, COUNTS, SEMAPHORES = plan(PLAN)
 
 
 def _mask(es):
     return sum(1 << e for e in es)
 
 
-def _helpers(topo, src, dst):
+def _helpers(topo, T, src, dst):
+    nxt = T.cores[(T.rank_of(src) + 1) % N]
     cs = [c for c in topo.cores_of(src) if c != src and topo.may_write(c, dst)]
-    return sorted(cs, key=lambda c: (topo.die(c) != topo.die(src), c))
+    return sorted(cs, key=lambda c: (topo.die(c) != topo.die(src), topo.may_write(c, nxt), c))
+
+
+def _hops(topo, T, src, o):
+    if (src, o["name"]) not in _known: _known[src, o["name"]] = _find_hops(topo, T, src, o)
+    return _known[src, o["name"]]
+
+
+_known = {}
+
+
+def _find_hops(topo, T, src, o):
+    dst = T.cores[(T.rank_of(src) + o["to"]) % N]
+    hs = _helpers(topo, T, src, dst)
+    k, out = 0, []
+    nrel = sum(isinstance(r, int) for r in o["relays"])
+    for p, r in zip(o["parts"], o["relays"]):
+        if r is None:
+            out.append((p, dst, topo.engines(src, dst), False)); continue
+        if isinstance(r, tuple):
+            ms = [c for c in range(WORLD) if topo.mates(c, dst) and topo.may_write(c, dst) and topo.may_write(src, c)]
+            h = sorted(ms, key=lambda c: (topo.die(c) != topo.die(src), c))[r[1]]
+            out.append((p, h, topo.engines(src, h), True)); continue
+        es = topo.engines(src, hs[r])
+        if o["sel"] == "rest": es = [e for e in es if e not in topo.engines(hs[r], dst)]
+        w = len(es) // nrel
+        out.append((p, hs[r], es[k * w:k * w + w], True)); k += 1
+    return dst, out
 
 
 def rank_program(g, core, T, topo):
@@ -555,18 +794,11 @@ def rank_program(g, core, T, topo):
 
     rank = T.rank_of(core)
     if rank is None:
-        own = [c for c in topo.cores_of(core) if T.rank_of(c) is not None]
-        if not own: return
-        src, sent = own[0], 0
-        for i in ORDER:
-            o = OPS[i]
-            if o["kind"] != "r" or o["relays"] is None: continue
-            dst = T.cores[(T.rank_of(src) + o["to"]) % N]
-            hs = _helpers(topo, src, dst)
-            for p, r in zip(o["parts"], o["relays"]):
-                if hs[r % len(hs)] != core: continue
-                es = _first_hop(topo, src, core, dst, o)
-                g.wait_ge(T.sem["r_" + o["name"]], len(es) // len(o["parts"]))
+        sent = 0
+        for o in [OPS[i] for i in ORDER if OPS[i]["kind"] == "r"]:
+            ways = [_hops(topo, T, src, o) for src in T.cores]
+            for dst, p, es in [(dst, p, es) for dst, hops in ways for p, h, es, relayed in hops if relayed and h == core]:
+                g.wait_ge(T.sem["r_" + o["name"]], len(es))
                 rid, pid = topo.addr(dst, core)
                 g.remote_dma(ap(p[1]), ap(p[1]), T.sem["a_" + o["arr"]], T.sem.sent, pid, rid, topo.mask(core, dst))
                 sent += len(topo.engines(core, dst))
@@ -577,10 +809,11 @@ def rank_program(g, core, T, topo):
     sent = 0
 
     def total(o):
-        s = OPS[o["after"][0]]
-        src = T.cores[(rank - s["to"]) % N]
-        if s["relays"] is not None: src = _helpers(topo, src, core)[0]
-        return o["n"] * len(topo.engines(src, core))
+        n = 0
+        for s in o["after"]:
+            src = T.cores[(rank - OPS[s]["to"]) % N]
+            n += sum(len(topo.engines(h, core)) if relayed else len(es) for p, h, es, relayed in _hops(topo, T, src, OPS[s])[1])
+        return n
 
     for i in ORDER:
         o = OPS[i]
@@ -590,28 +823,16 @@ def rank_program(g, core, T, topo):
             sem, val = OPS[j]["sig"]
             e.wait_ge(T.sem[sem], total(OPS[j]) if val is None else val)
         if o["kind"] == "r":
-            dst = T.cores[(rank + o["to"]) % N]
-            if o["relays"] is None:
-                rid, pid = topo.addr(dst, core)
-                p = o["parts"][0]
-                g.remote_dma(ap(p[1]), ap(p[0]), T.sem["a_" + o["arr"]], T.sem.sent, pid, rid, topo.mask(core, dst))
-                sent += len(topo.engines(core, dst))
-                continue
-            hs = _helpers(topo, core, dst)
             tr = []
-            for k, (p, r) in enumerate(zip(o["parts"], o["relays"])):
-                h = hs[r % len(hs)]
-                es = _first_hop(topo, core, h, dst, o)
-                w = len(es) // len(o["parts"])
-                rid, pid = topo.addr(h, core)
-                tr.append((rid, pid, _mask(es[k * w:k * w + w]), p))
-                sent += w
+            for p, h, es, relayed in _hops(topo, T, core, o)[1]:
+                tr.append(topo.addr(h, core) + (_mask(es), p, T.sem["r_" + o["name"] if relayed else "a_" + o["arr"]]))
+                sent += len(es)
             if len(tr) == 1:
-                rid, pid, m, p = tr[0]
-                g.remote_dma(ap(p[1]), ap(p[0]), T.sem["r_" + o["name"]], T.sem.sent, pid, rid, m)
+                rid, pid, m, p, sem = tr[0]
+                g.remote_dma(ap(p[1]), ap(p[0]), sem, T.sem.sent, pid, rid, m)
             else:
-                g.remote_dma_fused([RemoteDMATransfer(dst_ids=[DstId(rid=rid, pnc=pid)], dma_engine_mask=m, remote_sem=T.sem["r_" + o["name"]],
-                                                      src=ap(p[0]), dst=ap(p[1])) for rid, pid, m, p in tr], local_sem=T.sem.sent)
+                g.remote_dma_fused([RemoteDMATransfer(dst_ids=[DstId(rid=rid, pnc=pid)], dma_engine_mask=m, remote_sem=sem,
+                                                      src=ap(p[0]), dst=ap(p[1])) for rid, pid, m, p, sem in tr], local_sem=T.sem.sent)
             continue
         if o["kind"] == "m":
             k = len(o["pairs"])
@@ -638,11 +859,3 @@ def rank_program(g, core, T, topo):
         g.wait_ge(T.sem["q" + k], c)
     for i in ORDER:
         if OPS[i]["kind"] == "d": g.wait_ge(T.sem[OPS[i]["sig"][0]], 16)
-
-
-def _first_hop(topo, src, helper, dst, o):
-    es = topo.engines(src, helper)
-    if o["sel"] == "rest":
-        off = topo.engines(helper, dst)
-        es = [e for e in es if e not in off]
-    return es

@@ -21,21 +21,22 @@ SCRATCH = {
     "J": _sb(144, I), "PID": _sb(8, I), "PI2": _sb(8, I), "PF": _sb(8, F), "JG": _sb(128, I), "JM": _sb(144, I),
     "ZC": _sb(144, BF), "SF1": _sb(128, F), "S01": _sb(128, BF), "NID": _sb(128, BF),
     "BD": _sb(128, F), "BDb": _sb(128, BF), "DM": _sb(128, F), "NDM": _sb(144, F), "KC": _sb(128, BF),
-    "KC2": _sb(128, F), "KN": _sb(128, F), "E2": _sb(128, F),
+    "KN": _sb(128, F), "E2": _sb(128, F),
     "LN": _sb(8, F), "DU": _sb(16, F), "TILE": _sb(8, U), "ENDS": _sb(8, U), "EN": _sb(8, F),
     "CS": _sb(1152, BF), "M2K": _sb(128, BF),
     "OW": _sb(136, F), "OW4": _sb(136, F), "OU": _sb(128, U), "O32": _sb(128, F), "CI": _sb(128, I), "CI2": _sb(128, I),
-    "CO": _sb(128, F), "CA": _sb(128, F), "ST": _sb(256, F), "ST4": _sb(256, F), "ZT": _sb(512, BF), "ZT4": _sb(512, BF),
+    "CO": _sb(128, F), "CA": _sb(128, F), "ST": _sb(256, F), "ST4": _sb(256, F), "ZT": _sb((8, 128), BF), "ZT4": _sb((8, 128), BF),
+    "Z": _sb(128, BF), "ZF": _sb(128, BF), "ZB": _sb(512, BF), "ZL": _sb(32, U), "Z4": _sb(128, U), "LI": _sb(48, I), "TURN": _sb(8, U), "SK0": _sb(64, F), "SK1": _sb(128, F), "KX": _sb(128, F), "LF": _sb(8, F),
     "HI": _sb(136, I), "HI4": _sb(136, I), "HU": _sb(128, U), "VI": _sb(128, I), "RF": _sb(128, F), "RU": _sb(128, U),
     "D1": _sb(128, BF), "NM": _sb(128, F),
-    "TR": _sb((2, 32), F), "TR2": _sb((2, 16), F), "MM": _sb((2, 8), I), "MA": _sb((2, 8), I), "CU": _sb((3, 8), U),
+    "MM": _sb(16, I), "MA": _sb(16, I), "CU": _sb(24, U),
     "VH": _sb(128, F), "VB": _sb(144, F), "VO": _sb(144, F), "SB": _sb(144, F), "SO": _sb(144, F),
     "EQ": _sb(1152, BF), "SP": _sb(1152, BF), "EA": _sb(1152, BF), "OF": _sb(32, F), "XP": _sb(16, U),
     "VHH": _sb(128, BF), "E": _sb(128, F), "LT": _sb(128, F), "HN": _sb(128, F),
     "NE": _sb(128, F), "RR": _sb(128, F), "RS": _sb(8, F), "A32": _sb(8, F), "L1": _sb(8, F), "YT": _sb(128, F),
     "XM0": _sb(144, U), "XM1": _sb(144, U), "XM2": _sb(144, U), "XM3": _sb(144, U),
     "XL0": _sb(144, U), "XL1": _sb(144, U), "XL2": _sb(144, U),
-    "ZS": _sb(128, F), "GB": _sb(128, BF), "MB": _sb(8, BF), "SZ": _sb(32, F), "NF0": _sb(128, F), "NF1": _sb(128, F), "IDP": _sb(128, BF),
+    "ZS": _sb(128, F), "GB": _sb(128, BF), "IDF": _sb(128, F), "SZ": _sb(64, F), "NF0": _sb(128, F), "NF1": _sb(128, F), "IDP": _sb(128, BF),
     "WP0": _sb(144, BF), "WN0": _sb(144, BF), "WP1": _sb(144, BF), "WN1": _sb(144, BF), "PV": _sb(128, BF), "PF3": _sb(128, F), "PFC": _sb(256, F),
 }
 for _b in range(8):
@@ -49,12 +50,13 @@ PLAN = dict(
     pg=[[[(32, "V"), (32, "A")], [(32, "V"), (32, "A")]]] + [[[(32, "A"), (32, "V")], [(32, "A"), (32, "A")]]] * 3,
     u=[[[(32, "c"), (32, "b")], [(32, "c"), (32, "b")]]] * 4,
     d=[[[(32, "c"), (32, "b")], [(32, "c"), (32, "b")]]] * 4,
-    nb=(2, 2), eqa=[((0, 8), (0, 0))] * 4, zsa=[0, 0, 0, 0], nea=[0, 0, 0, 0], soft=0, tsplit=(1, 1, 1), pssplit=True, mw=128, early=1, szv=0,
-    loads=[["px", 0, 1, 2, "ol"], ["tl", "nl", "z"]], xsend=[[MATE, 2], [MATE2, 0], [3, 1]], xlat=[8000.0, 8500.0, 7300.0], tries=12000)
-SPEEDS = [(0.88, 1.56, 3.8, 110.0, 150.0, 0.8, 12.0, 80.0), (0.85, 1.2, 2.5, 150.0, 150.0, 0.9, 12.0, 50.0), (1.15, 1.9, 5.0, 70.0, 130.0, 0.8, 5.0, 100.0)]
-WEIGHTS, AMIN = [0.5, 0.25, 0.25], 40.0
-EPS = 2.0 ** -10
-CRIT, TEMP = 0.7, 50.0
+    nb=(2, 2), eqa=[((0, 8), (0, 0))] * 3 + [((0, 0), (0, 8))], zsa=[1, 1, 1, 1], nea=[0, 0, 0, 0], soft=0, tsplit=(1, 1, 1), pssplit=True, comb=(4, 1, 4), early=1, szv=0,
+    loads=[["px", 0, "z", "tl", 1, "ol", 2], ["nl"]], xsend=[[MATE, 2], [MATE2, 0], [3, 1]], xlat=[8000.0, 8500.0, 7300.0], joint=1, first=(1, 1), tile="GVVV", tile0="VVVV", tile4="AAAA", npe=1, tries=24000)
+SPEEDS = [(0.92, 1.56, 3.8, 90.0, 180.0, 0.83, 0.0, 55.0), (0.85, 1.2, 2.5, 130.0, 180.0, 0.9, 10.0, 50.0), (1.2, 1.9, 5.0, 90.0, 200.0, 0.83, 5.0, 80.0),
+          (1.0, 1.4, 3.0, 100.0, 160.0, 1.1, 0.0, 55.0)]
+WEIGHTS, AMIN = [0.35, 0.15, 0.25, 0.25], 0.0
+EPS, BIG = 2.0 ** -10, 2.0 ** 21
+CRIT, TEMP = 0.7, 60.0
 
 
 def v(name, lo, hi, step=1, rows=None):
@@ -62,9 +64,9 @@ def v(name, lo, hi, step=1, rows=None):
     return ("v", name, (r, slice(lo, hi, step)), lo, hi, len(range(lo, hi, step)))
 
 
-def v3(name, w, j0, j1, lo, hi):
-    idx = (slice(None), j0, slice(lo, hi)) if j1 == j0 + 1 else (slice(None), slice(j0, j1), slice(lo, hi))
-    return ("v", name, idx, j0 * w + lo, (j1 - 1) * w + hi, (j1 - j0) * (hi - lo))
+def v3(name, w, j0, j1, lo, hi, step=1):
+    idx = (slice(None), slice(j0, j1), slice(lo, hi, step))
+    return ("v", name, idx, j0 * w + lo, (j1 - 1) * w + hi, (j1 - j0) * len(range(lo, hi, step)))
 
 
 def hbm(name, lo=None, hi=None):
@@ -182,7 +184,7 @@ def build(P):
             arrive(nm, [send(nm, [(v(src, 512, XE), v(dst, 512, XE))], to, after=after)])
 
     cut = [XE - 688 * c for c in range(4)]
-    loads = dict(px=v("PXI", 0, 256), ol=v("OLI", 0, 128), tl=v("TLI", 0, 128), nl=v("NLI", 0, 128), z=v("ZT", 0, 128))
+    loads = dict(px=v("PXI", 0, 256), ol=v("OLI", 0, 128), tl=v("TLI", 0, 128), nl=v("NLI", 0, 128), z=v("Z", 0, 128))
     was = {}
 
     def load(names, queues, ahead):
@@ -224,14 +226,31 @@ def build(P):
     ts(v("ZC", 0, 144), v("J", 0, 144), 15.0, OP.subtract, g16, OP.is_equal)
     ts(v("NID", 0, 128), v("J", 0, 128), pid, OP.is_equal, -1.0, OP.mult)
     ms(v("M2K", 0, 128), 2048.0)
-    cp(v("OU", 0, 128), v("OLI", 0, 128))
-    cp(v("OW", 0, 128), v("OLI", 0, 128))
+    ts(v("LN", 0, 8), v("J", 0, 8), 16.0, OP.mult, pm, OP.add)
+    cp(v("LI", 0, 8), v("LN", 0, 8))
+    ts(v("LI", 8, 16), v("LI", 0, 8), 3, OP.arith_shift_right, 7, OP.bitwise_and)
+    ts(v("LI", 16, 24), v("LI", 0, 8), 7, OP.bitwise_and)
+    cp(v("TILE", 0, 8), v("LI", 8, 16))
+    tt(v("LI", 24, 32), v("LI", 16, 24), v("LI", 8, 16), OP.subtract)
+    ts(v("LI", 32, 40), v("LI", 24, 32), 7.0, OP.mult)
+    tt(v("LI", 40, 48), v("LI", 32, 40), v("LN", 0, 8), OP.add)
+    cp(v("TURN", 0, 8), v("LI", 40, 48))
+
+    if "g" in P["tile"] + P["tile0"] + P["tile4"]:
+        ts(v("CI", 0, 32), v("J", 32, 64), 3, OP.arith_shift_right)
+        ts(v("ZL", 0, 32), v("CI", 0, 32), 16.0, OP.mult, pm, OP.add)
+
+    def turned(a): return ind(a, v("TURN", 0, 8))
+    cp(v("OW", 0, 128), turned(v("OLI", 0, 128)))
+    cp(v("OU", 0, 128), v("OW", 0, 128))
     act(v("O32", 0, 128), v("OW", 0, 128), AF.Identity, bias=32.0)
-    ts(v("CI", 0, 128), v("OLI", 0, 128), 3232.0, OP.mult)
+    ts(v("CI", 0, 128), v("OW", 0, 128), 3232.0, OP.mult)
     ts(v("CI2", 0, 128), v("CI", 0, 128), 65535, OP.bitwise_and)
-    cp(v("B7", 128, 256), v("NLI", 0, 128))
-    ts(v("B4", 128, 256), v("TLI", 0, 128), 99.0, OP.is_lt)
-    ts(v("E", 0, 128), v("TLI", 0, 128), 1.0, OP.add)
+    cp(v("ST", 0, 128), turned(v("NLI", 0, 128)))
+    act(v("B7", 128, 256), v("ST", 0, 128))
+    if P["npe"]: act(v("IDF", 0, 128), v("NID", 0, 128), scale=-1.0)
+    ts(v("E", 0, 128), turned(v("TLI", 0, 128)), 1.0, OP.add)
+    ts(v("B4", 128, 256), v("E", 0, 128), 100.0, OP.is_lt)
     tt(v("B4", 128, 256), v("B4", 128, 256), v("E", 0, 128), OP.mult)
     cp(v("CO", 0, 128), v("CI2", 0, 128))
     act(v("SF1", 0, 128), sel(1))
@@ -243,11 +262,14 @@ def build(P):
     ts(v("NDM", 0, 128), v("JM", 0, 128), pm, OP.not_equal)
     act(v("DM", 0, 128), v("NDM", 0, 128), AF.Identity, scale=-1.0, bias=1.0)
     ts(v("KC", 0, 128), v("J", 0, 128), -1.0, OP.mult, 255.0, OP.add)
-    act(v("KC2", 0, 128), v("KC", 0, 128), scale=2.0)
-    ts(v("LN", 0, 8), v("J", 0, 8), 16.0, OP.mult, pm, OP.add)
+    ts(v("JG", 0, 128), v("J", 0, 128), 7, OP.bitwise_and)
+    ts(v("SK0", 0, 64), v("JG", 0, 64), 1.0, OP.min)
+    ts(v("B5", 0, 128), v("JG", 0, 128), 7.0, OP.is_equal)
+    act(v("KN", 0, 128), v("KC", 0, 128), AF.Identity, scale=-2.0, bias=BIG + 257)
+    tt(v("KN", 0, 128), v("B5", 0, 128), v("KN", 0, 128), OP.mult)
+    act(v("SK1", 0, 128), v("KN", 0, 128), AF.Identity, bias=-2.0)
     act(v("EN", 4, 5), pm, AF.Identity, bias=4097.0)
     act(v("OW", 128, 136), v("LN", 0, 8), AF.Identity, scale=0.0, bias=v("EN", 4, 5))
-    ts(v("TILE", 0, 8), v("LN", 0, 8), 0.0, OP.mult, p8, OP.add)
     for nm, x in (("WP0", 2.0), ("WN0", -1.0), ("WP1", 512.0), ("WN1", -256.0)):
         act(v(nm, 0, 144), v("ZC", 0, 144), scale=x)
     if far:
@@ -272,10 +294,16 @@ def build(P):
     ms(v("HI", 128, 136), 0)
     ms(v("HI4", 128, 136), 0)
 
-    def tile_z(zt, pool=False):
-        for w in (128, 256):
-            if pool: op("G", "affine_select", v(zt, w, 2 * w), v(zt, 0, w), [[1, w]], OP.is_ge, 0.0, 0, 0)
-            else: act(v(zt, w, 2 * w), v(zt, 0, w))
+    def tile_z(zt, who, src, z):
+        n = 4 if who[1] == "g" else 8
+        (cp if who[3] == "V" else act)(v3(zt, 128, 0, n, 0, 16), v(src, 0, 16 * n))
+        for a, b, e in ([(0, n, who[0])] if who[0] == who[1] or n == 4 else [(0, 4, who[0]), (4, 8, who[1])]):
+            for w in (16, 32, 64):
+                o, i = v3(zt, 128, a, b, w, 2 * w), v3(zt, 128, a, b, 0, w)
+                if e == "G": op("G", "affine_select", o, i, [[1, w * (b - a)]], OP.is_ge, 0.0, 0, 0)
+                else: (cp if e == "V" else act)(o, i)
+        if who[2] == "S": dma("S", v("ZB", 0, 512), v3(zt, 128, 4, 8, 0, 128))
+        else: (cp if who[2] == "V" else act)(v("ZB", 0, 512), ind(v(z, 0, 128), v("ZL", 0, 32)) if n == 4 else v3(zt, 128, 4, 8, 0, 128))
 
     def limits(s, tb):
         mm(v("B5", 256, 264), [(v("BDb", 0, 128), v(tb, 512, 520)), (v("BDb", 0, 128), v(tb, 520, 528))])
@@ -286,39 +314,44 @@ def build(P):
         w = ind(v(tb, X0, XE), v(offs, lo, hi))
         if who == "c":
             act(v("D", a, b), w)
-            for x in range(a, b, P["mw"]):
-                y = min(b, x + P["mw"])
-                tt(v("AB", x, y), v("D", x, y), v("B6", x - a, y - a), OP.max)
+            n = P["comb"][0]
+            for r in range(n):
+                tt(v("AB", a + r, b, n), v("D", a + r, b, n), v("B6" if a % 1024 < 512 else "B1", a % 512 + r, a % 512 + b - a, n), OP.max)
         elif who == "d":
-            o = v(dbank[0], 0, b - a)
-            dbank.reverse()
-            mm(o, [(v("NID", 0, 128), v(zt, 0, b - a))], stop=False)
+            o = v("B0" if offs == "RU" else "B2", 0, b - a)
+            mm(o, [(v("NID", 0, 128), v3(zt, 128, lo % 64 // 8, lo % 64 // 8 + (hi - lo) // 8, 0, 128))], stop=False)
             act(v("D", a, b), w)
             mm(o, [(v("IDP", 0, 128), v("D", a, b))], start=False)
             act(v("AB", a, b), o, AF.Abs, scale=0.5)
         else:
-            tt(v("D", a, b), w, v(zt, 0, b - a), OP.subtract)
+            tt(v("D", a, b), w, v("ZB", a % 1024 - 512, a % 1024 - 512 + b - a), OP.subtract)
             if who == "a": ts(v("AB", a, b), v("D", a, b), 0.0, OP.max)
-            else: act(v("AB", a, b), v("D", a, b), AF.Abs, scale=0.5)
+            else:
+                n = P["comb"][1 + (hi == 128)]
+                for r in range(n): act(v("AB", a + r, b, n), v("D", a + r, b, n), AF.Abs, scale=0.5)
 
     def dist_sums(bank, const, k, lo, hi, pieces):
         out = v(bank, 0, hi - lo)
         pre, runs = [const + (out,)], []
         for a, b, who in pieces:
-            if who == "c": pre.append((v("NF%d" % k, 0, 128), v("SZ", 0, b - a), v(bank, a - lo, b - lo)))
+            if who == "c": pre.append((v("NF%d" % k, 0, 128), v("SZ", a % 64, a % 64 + b - a), v(bank, a - lo, b - lo)))
             if who in "bd": continue
             if runs and runs[-1][1] == a: runs[-1][1] = b
             else: runs.append([a, b])
         mm(out, pre, stop=False)
         for a, b in runs:
             mm(v(bank, a - lo, b - lo), [(v("WN%d" % k, 15 - p, 143 - p), v("D", 16 * a + p, 16 * b, 16)) for p in range(16)], False, False)
-        mm(out, [(v("WP%d" % k, 15 - p, 143 - p), v("AB", 16 * lo + p, 16 * hi, 16)) for p in range(16)], start=False)
+        n = max(P["comb"])
+        for r in range(n):
+            mm(out, [(v("WP%d" % k, 15 - p, 143 - p), v("AB", 16 * lo + p, 16 * hi, 16)) for p in range(r, 16, n)], False, r == n - 1)
 
-    def spread_z(zt):
+    def spread_z(zt, s):
         if not far: return
-        mm(v("B6", 0, 512), [(v("IDP", 0, 128), v(zt, 0, 512))])
-        mm(v("B5", 384, 416), [(sel(p), v(zt, p, 512, 16)) for p in range(16)])
-        (cp if P["szv"] else act)(v("SZ", 0, 32), v("B5", 384, 416))
+        mm(v("B6", 0, 512), [(v("IDP", 0, 128), v3(zt, 128, 0, 4, 0, 128))])
+        n = 8 if s < S and any(who == "c" and y % 64 != 32 for _, _, ps in spans(P["u"][s]) for x, y, who in ps if x % 64 >= 32) else 4
+        if n == 8: mm(v("B1", 0, 512), [(v("IDP", 0, 128), v3(zt, 128, 4, 8, 0, 128))])
+        mm(v("B5", 384, 384 + 8 * n), [(sel(p), v3(zt, 128, 0, n, p, 128, 16)) for p in range(16)])
+        (cp if P["szv"] else act)(v("SZ", 0, 8 * n), v("B5", 384, 384 + 8 * n))
 
     def part_a(s, tb):
         sends, e_ = [], v("B4", 128, 256)
@@ -330,8 +363,10 @@ def build(P):
             b, tag[0] = "B%d" % ((2 + hh) % 4), ("pg", s, hh)
             for x, y, who in ps:
                 (cp if who == "V" else act)(v("PG", 16 * x, 16 * y), ind(v("PW", 0, 4096), v("OU", x, y)))
-            mm(v(b, 0, hi - lo), [(sel(p), v("PG", 16 * lo + p, 16 * hi, 16)) for p in range(16)], stop=False)
-            mm(v(b, 0, hi - lo), [(v("NID", 0, 128), v("D1", lo, hi))], start=False)
+            two_ = [[(sel(p), v("PG", 16 * lo + p, 16 * hi, 16)) for p in range(16)], [(v("NID", 0, 128), v("D1", lo, hi))]]
+            if P["first"][hh]: two_.reverse()
+            mm(v(b, 0, hi - lo), two_[0], stop=False)
+            mm(v(b, 0, hi - lo), two_[1], start=False)
             tt(v("RF", lo, hi), v(b, 0, hi - lo), v("NM", lo, hi), OP.max)
             i = cp(v("RU", lo, hi), v("RF", lo, hi))
             if s == 0 and hi == 128:
@@ -396,20 +431,18 @@ def build(P):
             dist_sums(banks[hh], (v("IDP", 0, 128), v("KC", lo, up)), 1, lo, up, ps)
         tt(v("HN", 0, 128), v(hi, 0, 128), n_, OP.subtract)
         for hh, (lo, up, ps) in enumerate(groups):
-            b, tag[0] = banks[hh], ("tree", s, hh)
-            tt(v("KN", lo, up), v("KC2", lo, up), v(b, 0, up - lo), OP.subtract)
-            for x in range(lo, up, 32):
-                w = min(32, up - x)
-                t0, t1 = v3("TR", 32, 0, 1, 0, w), v3("TR", 32, 1, 2, 0, w)
-                if x == 0: ts(t0, v(b, 0, w), v("L1", s, s + 1), OP.max)
-                else: tt(t0, v(b, x - lo, x - lo + w), t0, OP.max)
-                if x == 32: tt(t1, v("KN", 0, 32), v("KN", 32, 64), OP.max)
-                elif x: tt(t1, v("KN", x, x + w), t1, OP.max)
-            tt(v("B7", lo, up), v(b, 0, up - lo), v("LT", lo, up), OP.is_lt)
-        tt(v3("TR2", 16, 0, 2, 0, 16), v3("TR", 32, 0, 2, 0, 16), v3("TR", 32, 0, 2, 16, 32), OP.max)
-        tt(v3("MM", 8, 0, 2, 0, 8), v3("TR2", 16, 0, 2, 0, 8), v3("TR2", 16, 0, 2, 8, 16), OP.max)
-        ts(v3("MA", 8, 0, 2, 0, 8), v3("MM", 8, 0, 2, 0, 8), 255, OP.bitwise_and)
-        ts(v3("CU", 8, 0, 2, 0, 8), v3("MA", 8, 0, 2, 0, 8), -1.0, OP.mult, 255.0, OP.add)
+            b, tag[0] = v(banks[hh], 0, 64), ("tree", s, hh)
+            scan(v("KX", lo, up), v("SK0", 0, 64), b, OP.mult, OP.max)
+            op("V", "tensor_tensor_scan", v("KN", lo, up), b, v("SK1", lo, up), BIG, OP.min, OP.add)
+            if hh == 0: ts(v("LF", 0, 8), v("KX", 7, 64, 8), v("L1", s, s + 1), OP.max)
+            tt(v("B7", lo, up), b, v("LT", lo, up), OP.is_lt)
+        tt(v("MM", 0, 8), v("KX", 71, 128, 8), v("LF", 0, 8), OP.max)
+        tt(v("MM", 8, 16), v("KN", 71, 128, 8), v("KN", 7, 64, 8), OP.min)
+        if P["joint"]: ts(v("MA", 0, 16), v("MM", 0, 16), 255, OP.bitwise_and)
+        else:
+            for lo in (0, 8): ts(v("MA", lo, lo + 8), v("MM", lo, lo + 8), 255, OP.bitwise_and)
+        ts(v("CU", 0, 8), v("MA", 0, 8), -1.0, OP.mult, 255.0, OP.add)
+        cp(v("CU", 8, 16), v("MA", 8, 16))
         red, tag[0] = v("B7", 0, 128), ("count", s)
         rr = v("B4", 256, 384) if last else v("RR", 0, 128)
         if last: act(rr, red, scale=s + 3.0)
@@ -418,7 +451,7 @@ def build(P):
             mm(v("B5", 272, 273), [(v("BD", 0, 128), v("RS", 0, 1))])
             act(v("A32", 0, 1), v("B5", 272, 273), scale=32.0 / (s + 3))
             act(v("CA", 0, 128), v("CO", 0, 128), AF.Identity, bias=v("A32", 0, 1))
-        cj, cb, jb = [v3("CU", 8, j, j + 1, 0, 8) for j in range(3)]
+        cj, cb, jb = [v("CU", 8 * j, 8 * j + 8) for j in range(3)]
         tag[0] = ("p", s)
         tt(v("VO", 0, 128), ind(v(ow, 0, 136), cj), v("DM", 0, 128), OP.mult)
         clash(s, 1, [("B4", 0), ("B3", 256)], "VO", "SO", v("XP", 0, 8))
@@ -439,16 +472,17 @@ def build(P):
         clash(s, 0, [("B1", 256), ("B5", 0)], "VB", "SB", v(xm, 128, 136))
         tag[0] = ("z", s)
         cp(jb, v("SB", 15, 128, 16))
+        z0 = v3(zt, 128, 0, 8, 0, 16) if P["zsa"][s] else v("ZF" if last else "Z", 0, 128)
         if P["zsa"][s]:
-            zs = v("B1", 384, 512)
-            mm(zs, [(v("IDP", 0, 128), v(zt, 0, 128))], stop=False)
+            zs = v("B2", 256, 384)
+            mm(zs, [(v("IDP", 0, 128), z0)], stop=False)
             act(v("GB", 0, 128), ind(v(tb, X0, XE), jb))
             mm(zs, [(v("IDP", 0, 128), v("GB", 0, 128))], start=False)
         else:
             zs = v("ZS", 0, 128)
-            tt(zs, ind(v(tb, X0, XE), jb), v(zt, 0, 128), OP.add)
+            tt(zs, ind(v(tb, X0, XE), jb), z0, OP.add)
         ts(v(xm, 0, 128), zs, 0.5, OP.mult, -0.25, OP.add)
-        cp(v(zt, 0, 128), v(xm, 0, 128))
+        if last or P["tile"][3] != "V" or (s < S - 2 and not P["zsa"][s + 1]): cp(v("Z", 0, 128), v(xm, 0, 128))
         if not last:
             to, nxt = (3 if s == 2 else -1), "TB%d" % (s + 2)
             w = 136
@@ -458,42 +492,39 @@ def build(P):
             parts = [(v(tb, c, c + 256), v(nxt, c, c + 256)) for c in (0, 256)] if P["pssplit"] else [(v(tb, 0, 512), v(nxt, 0, 512))]
             sp = send("ps%d" % s, parts, to, [3, 1][:len(parts)], "rest", after=[sx])
             arrive("ps%d" % s, [sp])
-            tile_z(zt, True)
-            spread_z(zt)
+            tile_z(zt, P["tile"], xm if P["tile"][3] == "V" else "Z", "Z")
+            spread_z(zt, s + 1)
         put_x(tb, xm)
         if s < 2: send_table(s + 3, tb, 2 if s else -2, [sp])
         if last:
             dma("S", hbm("yx", 0, 1024), v(tb, X0, X0 + 1024))
             dma("A", hbm("yx", 1024, 2048), v(tb, X0 + 1024, XE))
-            dma("S", hbm("yz"), v(zt, 0, 128))
+            dma("S", hbm("yz"), v("Z", 0, 128))
         e1, tag[0] = (rr if last else e_), ("date", s)
         tt(e1, e_, rr, OP.max)
         if P["early"] and not last: road(s + 1, e1, v("B5", 128, 256))
-        if P["nea"][s]:
-            cp(v("MB", 0, 8), v3("MA", 8, 0, 1, 0, 8))
-            mm(v("B3", 128, 256), [(v("NID", 0, 128), v("KC", 0, 128))] + [(v("IDP", 0, 128), v("MB", 0, 8), v("B3", 128 + 8 * k, 136 + 8 * k)) for k in range(16)])
-            act(v("NE", 0, 128), v("B3", 128, 256), AF.Abs, scale=128.0)
-            tt(e_, e1, v("NE", 0, 128), OP.min)
-        else:
-            tt(v("NE", 0, 128), ind(v3("MA", 8, 0, 1, 0, 8), v("TILE", 0, 8)), v("KC", 0, 128), OP.not_equal)
-            if P["early"] and not last: tt(v("D1", 0, 128), v("B5", 128, 256), v("NE", 0, 128), OP.mult)
-            tt(e_, e1, v("NE", 0, 128), OP.mult)
-        tn, tag[0] = (red if last else v("HN", 0, 128)), ("name", s)
-        tt(tn, red, v("HN", 0, 128), OP.mult)
-        tt(n_, tn, n_, OP.add)
-        if s == S - 2:
-            act(v("ST", 0, 128), n_)
-            act(v("ST", 128, 256), e_)
+        tt(v("NE", 0, 128), ind(v("MA", 0, 8), v("TILE", 0, 8)), v("KC", 0, 128), OP.not_equal)
+        if P["early"] and not last: tt(v("D1", 0, 128), v("B5", 128, 256), v("NE", 0, 128), OP.mult)
+        tt(e_, e1, v("NE", 0, 128), OP.mult)
+        tn, tag[0] = v("HN", 0, 128), ("name", s)
+        tt(tn, red, tn, OP.mult)
+        if not last:
+            if P["npe"]: mm(n_, [(v("IDF", 0, 128), v("ST", 0, 128)), (v("IDF", 0, 128), tn)])
+            else: tt(n_, tn, n_, OP.add)
+            if P["npe"] or s == S - 2: act(v("ST", 0, 128), n_)
+        if s == S - 2: act(v("ST", 128, 256), e_)
         if last:
-            dma("S", hbm("yn"), n_)
-            act(rr, e_, AF.Identity, scale=-100.0, bias=99.0)
-            act(v("E", 0, 128), e_, AF.Identity, bias=-1.0)
-            tt(v("YT", 0, 128), rr, v("E", 0, 128), OP.max)
+            act(v("NM", 0, 128), turned(n_))
+            tt(v("RF", 0, 128), turned(tn), v("NM", 0, 128), OP.add)
+            dma("S", hbm("yn"), v("RF", 0, 128))
+            act(v("RR", 0, 128), turned(e_), AF.Identity, scale=-100.0, bias=99.0)
+            act(v("E", 0, 128), turned(e_), AF.Identity, bias=-1.0)
+            tt(v("YT", 0, 128), v("RR", 0, 128), v("E", 0, 128), OP.max)
             dma("A", hbm("yt"), v("YT", 0, 128))
 
-    tile_z("ZT")
+    tile_z("ZT", P["tile0"], "Z", "Z")
     limits(3, "TB0")
-    spread_z("ZT")
+    spread_z("ZT", 0)
     for s in range(S - 1):
         part_a(s, "TB%d" % s)
         tb = "TB%d" % (s + 1)
@@ -501,18 +532,23 @@ def build(P):
         stage_to(tb)
         if s: put_x(tb, "XL%d" % (s - 1))
         part_c(s, tb, "HI", "OW", "ZT")
-    arrive("z4", [send("z4", [(v("ZT", 0, 128), v("ZT4", 0, 128))], 4)])
+    arrive("z4", [send("z4", [(v("XM2", 0, 128), v("Z4", 0, 128))], 4)])
     arrive("s4", [send("s4", [(v("ST", 0, 256), v("ST4", 0, 256))], 4)])
     part_a(3, "TB3")
     tag[0] = ("land", 3)
-    tile_z("ZT4")
+    cp(v("ZF", 0, 128), v("Z4", 0, 128))
+    tile_z("ZT4", P["tile4"], "ZF", "ZF")
     put_x("TB4", "XL2")
-    spread_z("ZT4")
+    spread_z("ZT4", S)
     mm(v("B4", 128, 384), [(v("NID", 0, 128), v("TB4", 0, 256)), (v("NID", 0, 128), v("TB4", 256, 512))])
     act(v("PFC", 0, 256), v("B4", 128, 384), scale=-1.0)
     dma("S", v("PWF", 0, 4096, rows=0), v("PFC", 0, 256))
     part_c(3, "TB4", "HI4", "OW4", "ZT4")
     return ops
+
+
+def _step(a):
+    return a[2][1].step if len(a[2]) == 2 and a[1] in ("AB", "D") else 1
 
 
 def analyse(P):
@@ -523,9 +559,9 @@ def analyse(P):
         deps, hard = set(o["after"]), set(j for j in o["after"] if ops[j]["kind"] != "d")
         for acc, w in [(a, False) for a in o["rd"]] + [(a, True) for a in o["wr"]]:
             ps = SCRATCH[acc[1]][0] == "psum"
-            for (j, lo, hi, w2, rows) in hist.get(acc[1], []):
+            for (j, lo, hi, w2, rows, step) in hist.get(acc[1], []):
                 if j == i: continue
-                meet = lo < acc[4] and acc[3] < hi and (w or w2)
+                meet = lo < acc[4] and acc[3] < hi and (w or w2) and (lo - acc[3]) % math.gcd(step, _step(acc)) == 0
                 if meet and rows != acc[2][0] and rows != slice(None) and acc[2][0] != slice(None): meet = False
                 if ps and o["kind"] == "m" and ops[j]["kind"] == "m": deps.add(j)
                 elif meet:
@@ -534,7 +570,7 @@ def analyse(P):
                     both = o["out"][0] == "i" and ops[j]["out"][0] == "i" if same else False
                     if not (same and w and (P["soft"] == 2 or (P["soft"] == 1 and both))): hard.add(j)
         for acc, w in [(a, False) for a in o["rd"]] + [(a, True) for a in o["wr"]]:
-            hist.setdefault(acc[1], []).append((i, acc[3], acc[4], w, acc[2][0]))
+            hist.setdefault(acc[1], []).append((i, acc[3], acc[4], w, acc[2][0], _step(acc)))
         o["deps"], o["hard"] = deps, hard
         o["far"] = set(deps).union(*[ops[j]["far"] for j in deps])
         o["near"] = sorted(j for j in deps if ops[j]["kind"] in "rd" or not any(j in ops[k]["far"] for k in deps if ops[k]["kind"] in "cm" and k in hard))
@@ -548,7 +584,7 @@ def graph(ops, speed):
     for i, o in enumerate(ops):
         c = o["cost"]
         if o.get("var"): c = FIX + (ga if o["var"][0] == "g" else sca) * o["var"][1] * cy
-        elif o["kind"] == "m": c = (c - 60) * cy + 50
+        elif o["kind"] == "m": c = (c - 60) * cy + (50 if o["stop"] else 10)
         elif o["kind"] == "c": c = max(AMIN, c - AFIX) * cy + afix if o["eng"] == "A" else c * cy + vfix
         cost.append(c)
         e = []

import math
from concourse.bass import DstId, RemoteDMATransfer
from concourse.mybir import AluOpType as OP, ActivationFunctionType as AF

N, S, WORLD = 8, 4, 256
X0 = 528
XE, XD = X0 + 2048, X0 + 4096
PD = 8192 + 32
BF, F, I, U = "bfloat16", "float32", "int32", "uint16"


def _sb(cols, dt):
    return ("sbuf", [128] + (list(cols) if isinstance(cols, tuple) else [cols]), dt)


SCRATCH = {
    "TB0": _sb(XE, BF), "TB1": _sb(XD, BF), "TB2": _sb(XD, BF), "TB3": _sb(XD, BF), "TB4": _sb(XD, BF),
    "PW": _sb(PD, BF), "PWF": _sb(PD, F),
    "D": _sb(2048, BF), "AB": _sb(2048, BF), "PG": _sb(2048, BF),
    "PXI": _sb(256, I), "OLI": _sb(128, I), "NLI": _sb(128, I), "TLI": _sb(128, I), "THI": _sb(8, I),
    "J": _sb(144, I), "PID": _sb(8, I), "PI2": _sb(8, I), "PF": _sb(8, F), "JG": _sb(128, I), "JM": _sb(144, I),
    "ZC": _sb(144, BF), "SF1": _sb(128, F), "S01": _sb(128, BF), "NID": _sb(128, BF),
    "BD": _sb(128, F), "BDb": _sb(128, BF), "DM": _sb(128, F), "NDM": _sb(144, F), "KC": _sb(128, BF),
    "KN": _sb(128, F), "E2": _sb(128, F),
    "LN": _sb(8, F), "DU": _sb(16, F), "TILE": _sb(8, U), "ENDS": _sb(8, U), "EN": _sb(8, F),
    "CS": _sb(1152, BF), "M2K": _sb(128, BF),
    "OW": _sb(136, F), "OW4": _sb(136, F), "OU": _sb(128, U), "O32": _sb(128, F), "CI": _sb(128, I), "CI2": _sb(128, I),
    "CO": _sb(128, F), "CA": _sb(128, F), "ST": _sb(256, F), "ST4": _sb(256, F), "ZT": _sb((8, 128), BF), "ZT4": _sb((8, 128), BF),
    "Z": _sb(128, BF), "ZF": _sb(128, BF), "ZB": _sb(512, BF), "ZL": _sb(32, U), "Z4": _sb(128, U), "LI": _sb(48, I), "TURN": _sb(8, U), "SK0": _sb(64, F), "SK1": _sb(128, F), "KX": _sb(128, F), "LF": _sb(8, F),
    "HI": _sb(136, I), "HI4": _sb(136, I), "HU": _sb(128, U), "VI": _sb(128, I), "RF": _sb(128, F), "RU": _sb(128, U),
    "D1": _sb(128, BF), "NM": _sb(128, F),
    "MM": _sb(16, I), "MA": _sb(16, I), "CU": _sb(24, U),
    "VH": _sb(128, F), "VB": _sb(144, F), "VO": _sb(144, F), "SB": _sb(144, F), "SO": _sb(144, F),
    "EQ": _sb(1152, BF), "SP": _sb(1152, BF), "EA": _sb(1152, BF), "OF": _sb(32, F), "XP": _sb(16, U),
    "VHH": _sb(128, BF), "E": _sb(128, F), "LT": _sb(128, F), "HN": _sb(128, F),
    "NE": _sb(128, F), "RR": _sb(128, F), "RS": _sb(8, F), "A32": _sb(8, F), "L1": _sb(8, F), "YT": _sb(128, F),
    "XM0": _sb(144, U), "XM1": _sb(144, U), "XM2": _sb(144, U), "XM3": _sb(144, U),
    "XL0": _sb(144, U), "XL1": _sb(144, U), "XL2": _sb(144, U),
    "ZS": _sb(128, F), "GB": _sb(128, BF), "IDF": _sb(128, F), "SZ": _sb(64, F), "NF0": _sb(128, F), "NF1": _sb(128, F), "IDP": _sb(128, BF),
    "WP0": _sb(144, BF), "WN0": _sb(144, BF), "WP1": _sb(144, BF), "WN1": _sb(144, BF), "PV": _sb(128, BF), "PF3": _sb(128, F), "PFC": _sb(256, F),
}
for _b in range(8):
    SCRATCH["B%d" % _b] = ("psum", [128, 512], F)

GA, SCA, FIX, LAT = 1.6, 3.8, 60.0, 90.0
HOP1, HOP2 = 2000.0, 2700.0
PEC, BW, AFIX = 0.5, 45.0, 70.0
MATE, MATE2 = ("mate", 0), ("mate", 1)
PLAN = dict(
    pg=[[[(32, "V"), (32, "A")], [(32, "V"), (32, "A")]]] + [[[(32, "A"), (32, "V")], [(32, "A"), (32, "A")]]] * 3,
    u=[[[(32, "c"), (32, "b")], [(32, "c"), (32, "b")]]] * 4,
    d=[[[(32, "c"), (32, "b")], [(32, "c"), (32, "b")]]] * 4,
    nb=(2, 2), eqa=[((0, 8), (0, 0))] * 3 + [((0, 0), (0, 8))], zsa=[1, 1, 1, 1], nea=[0, 0, 0, 0], soft=0, tsplit=(1, 1, 1), pssplit=True, comb=(4, 1, 4), early=1, szv=0,
    loads=[["px", 0, "z", "tl", 1, "ol", 2], ["nl"]], xsend=[[MATE, 2], [MATE2, 0], [3, 1]], xlat=[8000.0, 8500.0, 7300.0], joint=1, first=(1, 1), tile="GVVV", tile0="VVVV", tile4="AAAA", npe=1, tries=24000)
SPEEDS = [(0.92, 1.56, 3.8, 90.0, 180.0, 0.83, 0.0, 55.0), (0.85, 1.2, 2.5, 130.0, 180.0, 0.9, 10.0, 50.0), (1.2, 1.9, 5.0, 90.0, 200.0, 0.83, 5.0, 80.0),
          (1.0, 1.4, 3.0, 100.0, 160.0, 1.1, 0.0, 55.0)]
WEIGHTS, AMIN = [0.35, 0.15, 0.25, 0.25], 0.0
EPS, BIG = 2.0 ** -10, 2.0 ** 21
CRIT, TEMP = 0.7, 60.0


def v(name, lo, hi, step=1, rows=None):
    r = slice(None) if rows is None else slice(rows, None, 16)
    return ("v", name, (r, slice(lo, hi, step)), lo, hi, len(range(lo, hi, step)))


def v3(name, w, j0, j1, lo, hi, step=1):
    idx = (slice(None), slice(j0, j1), slice(lo, hi, step))
    return ("v", name, idx, j0 * w + lo, (j1 - 1) * w + hi, (j1 - j0) * len(range(lo, hi, step)))


def hbm(name, lo=None, hi=None):
    return ("h", name, lo, hi)


def ind(win, off):
    return ("i", win, off)


def _isv(a):
    return isinstance(a, tuple) and len(a) > 0 and a[0] in ("v", "i", "h")


def spans(groups):
    out, at = [], 0
    for grp in groups:
        ps = []
        for w, who in grp:
            ps.append((at, at + w, who)); at += w
        out.append((ps[0][0], at, ps))
    return out


def segments(nb):
    out = [0]
    for a in range(8): out.append(out[-1] + 16 * (a % (8 // nb) + 1))
    return out


def build(P):
    ops, tag = [], [("load", 0)]
    far = any(who == "c" for k in "ud" for st in P[k] for grp in st for _, who in grp)
    dbank = ["B5" if far else "B6", "B5"]

    def two(a):
        return SCRATCH[a[1]][2] in (BF, U)

    def op(eng, meth, out, *args, **kw):
        rd, wr = [], []
        for a in list(args) + [x for k, x in kw.items() if k != "accum_out"]:
            if _isv(a):
                rd += [a[1], a[2]] if a[0] == "i" else ([a] if a[0] == "v" else [])
        if out[0] == "i":
            wr.append(out[1]); rd.append(out[2])
        elif out[0] == "v":
            wr.append(out)
        if "accum_out" in kw:
            wr.append(kw["accum_out"])
        kind, lat, var = "c", 0.0, None
        if meth == "dma_start":
            kind = "d"
            a = out if out[0] == "v" else args[0]
            by = a[5] * (2 if two(a) else 4) * (8 if a[2][0] != slice(None) else 128)
            cost, lat = 100.0, 2000.0 + by / 180.0
        elif out[0] == "i":
            cost, var = FIX + SCA * 16 * out[2][5], ("s", 16 * out[2][5])
        elif args and _isv(args[0]) and args[0][0] == "i":
            cost, var = FIX + GA * out[5], ("g", out[5])
        elif meth == "tensor_tensor":
            ps = SCRATCH[args[0][1]][0] == "psum" or SCRATCH[args[1][1]][0] == "psum"
            cost = max(64, out[5] * (1 if ps else 2))
        elif meth == "activation":
            cost = AFIX + out[5]
        elif meth in ("iota", "affine_select"):
            cost = 200 + 2 * out[5]
        else:
            big = [a for a in rd + wr if a[5] > 1]
            cost = max(64, out[5] * (0.5 if all(two(a) for a in big) else 1))
        ops.append(dict(eng=eng, kind=kind, meth=meth, out=out, args=args, kw=kw, rd=rd, wr=wr, cost=cost, lat=lat, after=[], var=var, tag=tag[0]))
        return len(ops) - 1

    def mm(out, pairs, start=True, stop=True):
        rd = [a for p in pairs for a in p[:2]]
        cost = sum(PEC * max(64, p[1][5]) * (1 if two(p[0]) else 4) for p in pairs)
        ops.append(dict(eng="P", kind="m", out=out, pairs=[p if len(p) == 3 else p + (out,) for p in pairs], start=start, stop=stop, rd=rd, wr=[out], cost=cost + 60, lat=0.0, after=[], tag=tag[0]))

    def send(name, parts, to, relays=None, eng="all", after=(), arr=None):
        relays = relays or [None]
        by = sum(p[0][5] * (2 if two(p[0]) else 4) * 128 for p in parts)
        lat = HOP2 + by / BW if relays == [None] else HOP1 + by / 150.0 + HOP2 + by / (BW * min(2, len(parts)))
        ops.append(dict(eng="G", kind="r", name=name, parts=parts, to=to, relays=relays, sel=eng, arr=arr or name,
                        rd=[p[0] for p in parts], wr=[], cost=900.0, lat=lat, after=list(after), tag=tag[0]))
        return len(ops) - 1

    def arrive(name, sends):
        wr = [p[1] for s in sends for p in ops[s]["parts"]]
        ops.append(dict(eng="X", kind="a", name=name, rd=[], wr=wr, cost=0.0, lat=0.0, after=list(sends), n=len(wr), tag=tag[0]))
        return len(ops) - 1

    def tt(out, a, b, o): return op("V", "tensor_tensor", out, a, b, o)
    def ts(out, a, s1, o0, s2=None, o1=None):
        return op("V", "tensor_scalar", out, a, s1, s2, o0, o1) if o1 is not None else op("V", "tensor_scalar", out, a, s1, None, o0)
    def cp(out, a): return op("V", "tensor_copy", out, a)
    def ms(out, c): return op("V", "memset", out, c)
    def scan(out, a, b, o0, o1): return op("V", "tensor_tensor_scan", out, a, b, 0.0, o0, o1)
    def act(out, a, f=AF.Copy, **kw): return op("A", "activation", out, a, f, **kw)
    def dma(q, out, a, **kw): return op(q, "dma_start", out, a, **kw)
    def sel(p): return v("ZC", 15 - p, 143 - p)

    def stage_to(tb):
        dma("S", v("PW", 0, 4096, rows=0), v(tb, 0, 256))
        dma("S", v("PW", 0, 4096, rows=1), v(tb, 256, 512))

    def stage_from(tb):
        dma("S", v(tb, 0, 256), v("PW", 0, 4096, rows=0))
        dma("S", v(tb, 256, 512), v("PW", 0, 4096, rows=1))

    def send_table(k, src, to, after):
        nm, dst = "t%d" % k, "TB%d" % k
        if P["tsplit"][k - 2]:
            m = (512 + XE) // 2
            arrive(nm, [send(nm, [(v(src, 512, m), v(dst, 512, m)), (v(src, m, XE), v(dst, m, XE))], to, [None, 3], "rest", after=after)])
        else:
            arrive(nm, [send(nm, [(v(src, 512, XE), v(dst, 512, XE))], to, after=after)])

    cut = [XE - 688 * c for c in range(4)]
    loads = dict(px=v("PXI", 0, 256), ol=v("OLI", 0, 128), tl=v("TLI", 0, 128), nl=v("NLI", 0, 128), z=v("Z", 0, 128))
    was = {}

    def load(names, queues, ahead):
        for k, nm in enumerate(names):
            q = queues[k % len(queues)]
            lo = X0 if nm in loads else max(X0, cut[nm + 1])
            i = dma(q, loads[nm], hbm(nm)) if nm in loads else dma(q, v("TB0", lo, cut[nm]), hbm("x", lo - X0, cut[nm] - X0))
            ops[i]["after"], was[q] = [was[q]] if q in was else [], i
            ops[i]["lat"], ahead = ops[i]["lat"] + ahead, ahead + ops[i]["lat"] - 2100.0
    load(P["loads"][0], "SA", 0.0)
    i = ms(v("THI", 0, 8), 0)
    dma("A", v("THI", 0, 4, rows=0), hbm("th"))
    ops[-1]["after"] = [was["A"]]
    ms(v("PW", 0, 4096), 0.0)
    ops[-1]["after"] = [i]
    op("G", "iota", v("J", 0, 144), [[1, 144]], 0, 0)
    op("G", "iota", v("PID", 0, 1), [[1, 1]], 0, 1)
    cp(v("TB0", 0, 256), v("PXI", 0, 256))
    tt(v("TB0", 256, 512), v("PXI", 0, 256), v("TB0", 0, 256), OP.subtract)
    stage_to("TB0")
    was["S"] = len(ops) - 1
    load(P["loads"][1], "S", 500.0)
    cp(v("TB0", 512, 520), v("THI", 0, 8))
    tt(v("TB0", 520, 528), v("THI", 0, 8), v("TB0", 512, 520), OP.subtract)
    xs = []
    for c, ways in enumerate(P["xsend"]):
        parts = [(v("TB0", lo, lo + 344), v("TB1", lo, lo + 344)) for lo in (cut[c + 1], cut[c + 1] + 344)]
        xs.append(send("x" + "abcd"[c], parts, -1, ways, "rest" if MATE in ways or MATE2 in ways else "all", arr="x1", after=xs[-1:]))
        ops[-1]["lat"] = P["xlat"][c]
    x1 = arrive("x1", xs)
    p1 = send("p1", [(v("TB0", 0, 512), v("TB1", 0, 512))], -1, [2], after=xs[-1:])
    arrive("p1", [p1])
    ts(v("PI2", 0, 1), v("PID", 0, 1), 112, OP.bitwise_and)
    ts(v("PI2", 1, 2), v("PID", 0, 1), 15, OP.bitwise_and)
    ts(v("PI2", 2, 3), v("PID", 0, 1), 7, OP.bitwise_and)
    cp(v("PF", 0, 3), v("PI2", 0, 3))
    cp(v("PF", 3, 4), v("PID", 0, 1))
    g16, pm, p8, pid = [v("PF", j, j + 1) for j in range(4)]
    ts(v("ZC", 0, 144), v("J", 0, 144), 15.0, OP.subtract, g16, OP.is_equal)
    ts(v("NID", 0, 128), v("J", 0, 128), pid, OP.is_equal, -1.0, OP.mult)
    ms(v("M2K", 0, 128), 2048.0)
    ts(v("LN", 0, 8), v("J", 0, 8), 16.0, OP.mult, pm, OP.add)
    cp(v("LI", 0, 8), v("LN", 0, 8))
    ts(v("LI", 8, 16), v("LI", 0, 8), 3, OP.arith_shift_right, 7, OP.bitwise_and)
    ts(v("LI", 16, 24), v("LI", 0, 8), 7, OP.bitwise_and)
    cp(v("TILE", 0, 8), v("LI", 8, 16))
    tt(v("LI", 24, 32), v("LI", 16, 24), v("LI", 8, 16), OP.subtract)
    ts(v("LI", 32, 40), v("LI", 24, 32), 7.0, OP.mult)
    tt(v("LI", 40, 48), v("LI", 32, 40), v("LN", 0, 8), OP.add)
    cp(v("TURN", 0, 8), v("LI", 40, 48))

    if "g" in P["tile"] + P["tile0"] + P["tile4"]:
        ts(v("CI", 0, 32), v("J", 32, 64), 3, OP.arith_shift_right)
        ts(v("ZL", 0, 32), v("CI", 0, 32), 16.0, OP.mult, pm, OP.add)

    def turned(a): return ind(a, v("TURN", 0, 8))
    cp(v("OW", 0, 128), turned(v("OLI", 0, 128)))
    cp(v("OU", 0, 128), v("OW", 0, 128))
    act(v("O32", 0, 128), v("OW", 0, 128), AF.Identity, bias=32.0)
    ts(v("CI", 0, 128), v("OW", 0, 128), 3232.0, OP.mult)
    ts(v("CI2", 0, 128), v("CI", 0, 128), 65535, OP.bitwise_and)
    cp(v("ST", 0, 128), turned(v("NLI", 0, 128)))
    act(v("B7", 128, 256), v("ST", 0, 128))
    if P["npe"]: act(v("IDF", 0, 128), v("NID", 0, 128), scale=-1.0)
    ts(v("E", 0, 128), turned(v("TLI", 0, 128)), 1.0, OP.add)
    ts(v("B4", 128, 256), v("E", 0, 128), 100.0, OP.is_lt)
    tt(v("B4", 128, 256), v("B4", 128, 256), v("E", 0, 128), OP.mult)
    cp(v("CO", 0, 128), v("CI2", 0, 128))
    act(v("SF1", 0, 128), sel(1))
    tt(v("S01", 0, 128), sel(0), sel(1), OP.subtract)
    ts(v("JG", 0, 128), v("J", 0, 128), 112, OP.bitwise_and)
    ts(v("JM", 0, 128), v("J", 0, 128), 15, OP.bitwise_and)
    ts(v("BD", 0, 128), v("JG", 0, 128), g16, OP.is_equal)
    act(v("BDb", 0, 128), v("BD", 0, 128))
    ts(v("NDM", 0, 128), v("JM", 0, 128), pm, OP.not_equal)
    act(v("DM", 0, 128), v("NDM", 0, 128), AF.Identity, scale=-1.0, bias=1.0)
    ts(v("KC", 0, 128), v("J", 0, 128), -1.0, OP.mult, 255.0, OP.add)
    ts(v("JG", 0, 128), v("J", 0, 128), 7, OP.bitwise_and)
    ts(v("SK0", 0, 64), v("JG", 0, 64), 1.0, OP.min)
    ts(v("B5", 0, 128), v("JG", 0, 128), 7.0, OP.is_equal)
    act(v("KN", 0, 128), v("KC", 0, 128), AF.Identity, scale=-2.0, bias=BIG + 257)
    tt(v("KN", 0, 128), v("B5", 0, 128), v("KN", 0, 128), OP.mult)
    act(v("SK1", 0, 128), v("KN", 0, 128), AF.Identity, bias=-2.0)
    act(v("EN", 4, 5), pm, AF.Identity, bias=4097.0)
    act(v("OW", 128, 136), v("LN", 0, 8), AF.Identity, scale=0.0, bias=v("EN", 4, 5))
    for nm, x in (("WP0", 2.0), ("WN0", -1.0), ("WP1", 512.0), ("WN1", -256.0)):
        act(v(nm, 0, 144), v("ZC", 0, 144), scale=x)
    if far:
        act(v("NF0", 0, 128), v("NID", 0, 128))
        act(v("NF1", 0, 128), v("NID", 0, 128), scale=256.0)
    act(v("IDP", 0, 128), v("NID", 0, 128), scale=-1.0)
    for j in range(2):
        w, seg = 8 // P["nb"][j], segments(P["nb"][j])
        act(v("DU", 8 * j, 8 * j + 8), v("LN", 0, 8), AF.Identity, scale=16 * (j + 1) / EPS, bias=(2048 * (j + 1) + 32 * j) / EPS - 1)
        ms(v("CS", 576 * j, 576 * j + seg[8]), 1.0)
        for a in range(8):
            lo, hi = 576 * j + seg[a], 576 * j + seg[a + 1]
            act(v("CS", hi - 16, hi), v("DM", 0, 16), AF.Identity, scale=v("DU", 8 * j + a, 8 * j + a + 1), bias=1.0)
            act(v("CS", lo, lo + 1), v("DM", 0, 1), scale=0.0)
        if j and P["nb"][0] == P["nb"][1]: continue
        ts(v("PI2", 4, 5), v("PID", 0, 1), 1, OP.arith_shift_right, w - 1, OP.bitwise_and)
        ts(v("PI2", 5, 6), v("PID", 0, 1), w.bit_length(), OP.arith_shift_right, 8 // w - 1, OP.bitwise_and)
        ts(v("EN", 0, 1), v("PI2", 4, 5), 1.0, OP.add, 8.0, OP.mult)
        ts(v("EN", 1, 2), v("PI2", 4, 5), 2.0, OP.add, v("EN", 0, 1), OP.mult)
        ts(v("EN", 2, 3), v("PI2", 5, 6), float(seg[w]), OP.mult, -1.0, OP.add)
        ts(v("ENDS", 2 * j, 2 * j + 1), v("EN", 1, 2), v("EN", 2, 3), OP.add)
    ms(v("HI", 128, 136), 0)
    ms(v("HI4", 128, 136), 0)

    def tile_z(zt, who, src, z):
        n = 4 if who[1] == "g" else 8
        (cp if who[3] == "V" else act)(v3(zt, 128, 0, n, 0, 16), v(src, 0, 16 * n))
        for a, b, e in ([(0, n, who[0])] if who[0] == who[1] or n == 4 else [(0, 4, who[0]), (4, 8, who[1])]):
            for w in (16, 32, 64):
                o, i = v3(zt, 128, a, b, w, 2 * w), v3(zt, 128, a, b, 0, w)
                if e == "G": op("G", "affine_select", o, i, [[1, w * (b - a)]], OP.is_ge, 0.0, 0, 0)
                else: (cp if e == "V" else act)(o, i)
        if who[2] == "S": dma("S", v("ZB", 0, 512), v3(zt, 128, 4, 8, 0, 128))
        else: (cp if who[2] == "V" else act)(v("ZB", 0, 512), ind(v(z, 0, 128), v("ZL", 0, 32)) if n == 4 else v3(zt, 128, 4, 8, 0, 128))

    def limits(s, tb):
        mm(v("B5", 256, 264), [(v("BDb", 0, 128), v(tb, 512, 520)), (v("BDb", 0, 128), v(tb, 520, 528))])
        act(v("L1", s, s + 1), v("B5", 256 + s, 257 + s), AF.Identity, scale=256.0, bias=256.0 + 127.0)

    def distances(tb, offs, zt, lo, hi, who):
        a, b = 16 * lo, 16 * hi
        w = ind(v(tb, X0, XE), v(offs, lo, hi))
        if who == "c":
            act(v("D", a, b), w)
            n = P["comb"][0]
            for r in range(n):
                tt(v("AB", a + r, b, n), v("D", a + r, b, n), v("B6" if a % 1024 < 512 else "B1", a % 512 + r, a % 512 + b - a, n), OP.max)
        elif who == "d":
            o = v("B0" if offs == "RU" else "B2", 0, b - a)
            mm(o, [(v("NID", 0, 128), v3(zt, 128, lo % 64 // 8, lo % 64 // 8 + (hi - lo) // 8, 0, 128))], stop=False)
            act(v("D", a, b), w)
            mm(o, [(v("IDP", 0, 128), v("D", a, b))], start=False)
            act(v("AB", a, b), o, AF.Abs, scale=0.5)
        else:
            tt(v("D", a, b), w, v("ZB", a % 1024 - 512, a % 1024 - 512 + b - a), OP.subtract)
            if who == "a": ts(v("AB", a, b), v("D", a, b), 0.0, OP.max)
            else:
                n = P["comb"][1 + (hi == 128)]
                for r in range(n): act(v("AB", a + r, b, n), v("D", a + r, b, n), AF.Abs, scale=0.5)

    def dist_sums(bank, const, k, lo, hi, pieces):
        out = v(bank, 0, hi - lo)
        pre, runs = [const + (out,)], []
        for a, b, who in pieces:
            if who == "c": pre.append((v("NF%d" % k, 0, 128), v("SZ", a % 64, a % 64 + b - a), v(bank, a - lo, b - lo)))
            if who in "bd": continue
            if runs and runs[-1][1] == a: runs[-1][1] = b
            else: runs.append([a, b])
        mm(out, pre, stop=False)
        for a, b in runs:
            mm(v(bank, a - lo, b - lo), [(v("WN%d" % k, 15 - p, 143 - p), v("D", 16 * a + p, 16 * b, 16)) for p in range(16)], False, False)
        n = max(P["comb"])
        for r in range(n):
            mm(out, [(v("WP%d" % k, 15 - p, 143 - p), v("AB", 16 * lo + p, 16 * hi, 16)) for p in range(r, 16, n)], False, r == n - 1)

    def spread_z(zt, s):
        if not far: return
        mm(v("B6", 0, 512), [(v("IDP", 0, 128), v3(zt, 128, 0, 4, 0, 128))])
        n = 8 if s < S and any(who == "c" and y % 64 != 32 for _, _, ps in spans(P["u"][s]) for x, y, who in ps if x % 64 >= 32) else 4
        if n == 8: mm(v("B1", 0, 512), [(v("IDP", 0, 128), v3(zt, 128, 4, 8, 0, 128))])
        mm(v("B5", 384, 384 + 8 * n), [(sel(p), v3(zt, 128, 0, n, p, 128, 16)) for p in range(16)])
        (cp if P["szv"] else act)(v("SZ", 0, 8 * n), v("B5", 384, 384 + 8 * n))

    def part_a(s, tb):
        sends, e_ = [], v("B4", 128, 256)
        tag[0] = ("road", s)
        if s == 0 or not P["early"]: road(s, e_, v("D1", 0, 128))
        if s < S - 1: embargo(s, e_)
        tt(v("NM", 0, 128), v("B7", 128, 256), v("D1", 0, 128), OP.min)
        for hh, (lo, hi, ps) in enumerate(spans(P["pg"][s])):
            b, tag[0] = "B%d" % ((2 + hh) % 4), ("pg", s, hh)
            for x, y, who in ps:
                (cp if who == "V" else act)(v("PG", 16 * x, 16 * y), ind(v("PW", 0, 4096), v("OU", x, y)))
            two_ = [[(sel(p), v("PG", 16 * lo + p, 16 * hi, 16)) for p in range(16)], [(v("NID", 0, 128), v("D1", lo, hi))]]
            if P["first"][hh]: two_.reverse()
            mm(v(b, 0, hi - lo), two_[0], stop=False)
            mm(v(b, 0, hi - lo), two_[1], start=False)
            tt(v("RF", lo, hi), v(b, 0, hi - lo), v("NM", lo, hi), OP.max)
            i = cp(v("RU", lo, hi), v("RF", lo, hi))
            if s == 0 and hi == 128:
                send_table(2, "TB0", -2, [i, p1])
                arrive("o4", [send("o4", [(v("OW", 0, 136), v("OW4", 0, 136))], 4, after=[len(ops) - 2, x1])])
        for hh, (lo, hi, ps) in enumerate(spans(P["u"][s])):
            b, tag[0] = "B%d" % ((2 + hh) % 4), ("u", s, hh)
            for x, y, who in ps: distances(tb, "RU", "ZT", x, y, who)
            dist_sums(b, (v("NID", 0, 128), v("M2K", 0, hi - lo)), 0, lo, hi, ps)
            tt(v("B7", 384 + lo, 384 + hi), v(b, 0, hi - lo), v("O32", lo, hi), OP.mult)
            tt(v("VI", lo, hi), v("B7", 384 + lo, 384 + hi), v("CO" if s == 0 else "CA", lo, hi), OP.add)
            ts(v("HI", lo, hi), v("VI", lo, hi), 5, OP.arith_shift_right, 2047, OP.bitwise_and)
            if s == S - 1:
                sends.append(send("h%d" % hh, [(v("HI", lo, hi), v("HI4", lo, hi))], 4, after=sends[-1:]))
                arrive("h%d" % hh, sends[-1:])

    def road(s, e_, out):
        act(v("E", 0, 128), e_, AF.Abs, bias=-(s + 2) / 2)
        act(out, v("E", 0, 128), AF.Relu, scale=-4096.0, bias=4096.0 * (s + 2) / 2)

    def embargo(s, e_):
        act(v("E2", 0, 128), e_, AF.Relu, scale=2.0 ** 21, bias=-(s + 1) * 2.0 ** 21)

    def clash(s, j, banks, vv, sc, out):
        w, seg, (a1, a2), lo = 8 // P["nb"][j], segments(P["nb"][j]), P["eqa"][s][j], 576 * j
        e = 2 * j if P["nb"][0] != P["nb"][1] else 0
        for b, x in banks[:2 if 0 < a2 - a1 < 8 else 1]: mm(v(b, x, x + 128), [(v("BD", 0, 128), v(vv, 0, 128))])
        scan(v(sc, 0, 128), v("NDM", 0, 128), v(vv, 0, 128), OP.mult, OP.add)
        for a in range(8):
            on = a1 <= a < a2
            b, x = banks[1 if on and a2 - a1 < 8 else 0]
            c, was = v(sc, 15 + 16 * a, 16 + 16 * a), v(b, x + 16 * (a - a % w), x + 16 * a + 16)
            if on: act(v("EA", lo + seg[a], lo + seg[a + 1]), was, AF.Abs, scale=-1.0, bias=c)
            else: ts(v("EQ", lo + seg[a], lo + seg[a + 1]), was, c, OP.is_equal, EPS, OP.mult)
        if a2 > a1: act(v("EQ", lo + seg[a1], lo + seg[a2]), v("EA", lo + seg[a1], lo + seg[a2]), AF.Relu, scale=-EPS, bias=EPS)
        scan(v("SP", lo, lo + seg[8]), v("CS", lo, lo + seg[8]), v("EQ", lo, lo + seg[8]), OP.mult, OP.max)
        tt(v("OF", 16 * j, 16 * j + 16), ind(v("SP", lo, lo + seg[8]), v("ENDS", e, e + 1)), v(sc, 7, 128, 8), OP.max)
        cp(out, v("OF", 16 * j + 1, 16 * j + 16, 2))

    def scatter(j, win, offs, lo, src):
        w = 8 // P["nb"][j]
        for a in range(8 - w, -1, -w):
            cp(ind(win, v(offs, lo + a, lo + a + w)), v(src, 16 * a, 16 * (a + w)))

    def put_x(tb, xm):
        scatter(0, v(tb, X0, XD), xm, 128, xm)

    def part_c(s, tb, hi, ow, zt):
        last = s == S - 1
        n_, e_ = (v("ST4", 0, 128), v("ST4", 128, 256)) if last else (v("B7", 128, 256), v("B4", 128, 256))
        if last: embargo(s, e_)
        act(v("LT", 0, 128), v("E2", 0, 128), AF.Identity, scale=-1.0, bias=v("L1", s, s + 1))
        cuts = [(lo, hi_) for lo, hi_, _ in spans(P["u"][s])]
        groups = spans(P["d"][s])
        banks = ["B0", "B1", "B3", "B2"]
        for hh, (lo, up, ps) in enumerate(groups):
            tag[0] = ("d", s, hh)
            for x, y, who in ps:
                while cuts and cuts[0][0] < y:
                    cp(v("HU", *cuts[0]), v(hi, *cuts[0])); cuts.pop(0)
                distances(tb, "HU", zt, x, y, who)
            dist_sums(banks[hh], (v("IDP", 0, 128), v("KC", lo, up)), 1, lo, up, ps)
        tt(v("HN", 0, 128), v(hi, 0, 128), n_, OP.subtract)
        for hh, (lo, up, ps) in enumerate(groups):
            b, tag[0] = v(banks[hh], 0, 64), ("tree", s, hh)
            scan(v("KX", lo, up), v("SK0", 0, 64), b, OP.mult, OP.max)
            op("V", "tensor_tensor_scan", v("KN", lo, up), b, v("SK1", lo, up), BIG, OP.min, OP.add)
            if hh == 0: ts(v("LF", 0, 8), v("KX", 7, 64, 8), v("L1", s, s + 1), OP.max)
            tt(v("B7", lo, up), b, v("LT", lo, up), OP.is_lt)
        tt(v("MM", 0, 8), v("KX", 71, 128, 8), v("LF", 0, 8), OP.max)
        tt(v("MM", 8, 16), v("KN", 71, 128, 8), v("KN", 7, 64, 8), OP.min)
        if P["joint"]: ts(v("MA", 0, 16), v("MM", 0, 16), 255, OP.bitwise_and)
        else:
            for lo in (0, 8): ts(v("MA", lo, lo + 8), v("MM", lo, lo + 8), 255, OP.bitwise_and)
        ts(v("CU", 0, 8), v("MA", 0, 8), -1.0, OP.mult, 255.0, OP.add)
        cp(v("CU", 8, 16), v("MA", 8, 16))
        red, tag[0] = v("B7", 0, 128), ("count", s)
        rr = v("B4", 256, 384) if last else v("RR", 0, 128)
        if last: act(rr, red, scale=s + 3.0)
        else:
            act(rr, red, scale=s + 3.0, accum_out=v("RS", 0, 1))
            mm(v("B5", 272, 273), [(v("BD", 0, 128), v("RS", 0, 1))])
            act(v("A32", 0, 1), v("B5", 272, 273), scale=32.0 / (s + 3))
            act(v("CA", 0, 128), v("CO", 0, 128), AF.Identity, bias=v("A32", 0, 1))
        cj, cb, jb = [v("CU", 8 * j, 8 * j + 8) for j in range(3)]
        tag[0] = ("p", s)
        tt(v("VO", 0, 128), ind(v(ow, 0, 136), cj), v("DM", 0, 128), OP.mult)
        clash(s, 1, [("B4", 0), ("B3", 256)], "VO", "SO", v("XP", 0, 8))
        tag[0] = ("pv", s)
        tt(v("VH", 0, 128), ind(v(hi, 0, 136), cj), v("DM", 0, 128), OP.mult)
        if not last:
            act(v("VHH", 0, 128), v("VH", 0, 128))
            mm(v("B0", 256, 384), [(v("SF1", 0, 128), v("VH", 0, 128)), (v("S01", 0, 128), v("VHH", 0, 128))])
            act(v("PV", 0, 128), v("B0", 256, 384))
            scatter(1, v("PW", 0, PD), "XP", 0, "PV")
        else:
            mm(v("B0", 256, 384), [(v("BD", 0, 128), v("VH", 0, 128))])
            act(v("PF3", 0, 128), v("B0", 256, 384))
            scatter(1, v("PWF", 0, PD), "XP", 0, "PF3")
            dma("S", hbm("yp"), v("PWF", 0, 4096, rows=0))
        xm, tag[0] = "XM%d" % s, ("x", s)
        tt(v("VB", 0, 128), ind(v(hi, 0, 136), cb), v("DM", 0, 128), OP.mult)
        clash(s, 0, [("B1", 256), ("B5", 0)], "VB", "SB", v(xm, 128, 136))
        tag[0] = ("z", s)
        cp(jb, v("SB", 15, 128, 16))
        z0 = v3(zt, 128, 0, 8, 0, 16) if P["zsa"][s] else v("ZF" if last else "Z", 0, 128)
        if P["zsa"][s]:
            zs = v("B2", 256, 384)
            mm(zs, [(v("IDP", 0, 128), z0)], stop=False)
            act(v("GB", 0, 128), ind(v(tb, X0, XE), jb))
            mm(zs, [(v("IDP", 0, 128), v("GB", 0, 128))], start=False)
        else:
            zs = v("ZS", 0, 128)
            tt(zs, ind(v(tb, X0, XE), jb), z0, OP.add)
        ts(v(xm, 0, 128), zs, 0.5, OP.mult, -0.25, OP.add)
        if last or P["tile"][3] != "V" or (s < S - 2 and not P["zsa"][s + 1]): cp(v("Z", 0, 128), v(xm, 0, 128))
        if not last:
            to, nxt = (3 if s == 2 else -1), "TB%d" % (s + 2)
            w = 136
            sx = send("dx%d" % s, [(v(xm, 0, w), v("XL%d" % s, 0, w))], to, [0])
            arrive("dx%d" % s, [sx])
            stage_from(tb)
            parts = [(v(tb, c, c + 256), v(nxt, c, c + 256)) for c in (0, 256)] if P["pssplit"] else [(v(tb, 0, 512), v(nxt, 0, 512))]
            sp = send("ps%d" % s, parts, to, [3, 1][:len(parts)], "rest", after=[sx])
            arrive("ps%d" % s, [sp])
            tile_z(zt, P["tile"], xm if P["tile"][3] == "V" else "Z", "Z")
            spread_z(zt, s + 1)
        put_x(tb, xm)
        if s < 2: send_table(s + 3, tb, 2 if s else -2, [sp])
        if last:
            dma("S", hbm("yx", 0, 1024), v(tb, X0, X0 + 1024))
            dma("A", hbm("yx", 1024, 2048), v(tb, X0 + 1024, XE))
            dma("S", hbm("yz"), v("Z", 0, 128))
        e1, tag[0] = (rr if last else e_), ("date", s)
        tt(e1, e_, rr, OP.max)
        if P["early"] and not last: road(s + 1, e1, v("B5", 128, 256))
        tt(v("NE", 0, 128), ind(v("MA", 0, 8), v("TILE", 0, 8)), v("KC", 0, 128), OP.not_equal)
        if P["early"] and not last: tt(v("D1", 0, 128), v("B5", 128, 256), v("NE", 0, 128), OP.mult)
        tt(e_, e1, v("NE", 0, 128), OP.mult)
        tn, tag[0] = v("HN", 0, 128), ("name", s)
        tt(tn, red, tn, OP.mult)
        if not last:
            if P["npe"]: mm(n_, [(v("IDF", 0, 128), v("ST", 0, 128)), (v("IDF", 0, 128), tn)])
            else: tt(n_, tn, n_, OP.add)
            if P["npe"] or s == S - 2: act(v("ST", 0, 128), n_)
        if s == S - 2: act(v("ST", 128, 256), e_)
        if last:
            act(v("NM", 0, 128), turned(n_))
            tt(v("RF", 0, 128), turned(tn), v("NM", 0, 128), OP.add)
            dma("S", hbm("yn"), v("RF", 0, 128))
            act(v("RR", 0, 128), turned(e_), AF.Identity, scale=-100.0, bias=99.0)
            act(v("E", 0, 128), turned(e_), AF.Identity, bias=-1.0)
            tt(v("YT", 0, 128), v("RR", 0, 128), v("E", 0, 128), OP.max)
            dma("A", hbm("yt"), v("YT", 0, 128))

    tile_z("ZT", P["tile0"], "Z", "Z")
    limits(3, "TB0")
    spread_z("ZT", 0)
    for s in range(S - 1):
        part_a(s, "TB%d" % s)
        tb = "TB%d" % (s + 1)
        limits(s, tb)
        stage_to(tb)
        if s: put_x(tb, "XL%d" % (s - 1))
        part_c(s, tb, "HI", "OW", "ZT")
    arrive("z4", [send("z4", [(v("XM2", 0, 128), v("Z4", 0, 128))], 4)])
    arrive("s4", [send("s4", [(v("ST", 0, 256), v("ST4", 0, 256))], 4)])
    part_a(3, "TB3")
    tag[0] = ("land", 3)
    cp(v("ZF", 0, 128), v("Z4", 0, 128))
    tile_z("ZT4", P["tile4"], "ZF", "ZF")
    put_x("TB4", "XL2")
    spread_z("ZT4", S)
    mm(v("B4", 128, 384), [(v("NID", 0, 128), v("TB4", 0, 256)), (v("NID", 0, 128), v("TB4", 256, 512))])
    act(v("PFC", 0, 256), v("B4", 128, 384), scale=-1.0)
    dma("S", v("PWF", 0, 4096, rows=0), v("PFC", 0, 256))
    part_c(3, "TB4", "HI4", "OW4", "ZT4")
    return ops


def _step(a):
    return a[2][1].step if len(a[2]) == 2 and a[1] in ("AB", "D") else 1


def analyse(P):
    ops = build(P)
    n = len(ops)
    hist = {}
    for i, o in enumerate(ops):
        deps, hard = set(o["after"]), set(j for j in o["after"] if ops[j]["kind"] != "d")
        for acc, w in [(a, False) for a in o["rd"]] + [(a, True) for a in o["wr"]]:
            ps = SCRATCH[acc[1]][0] == "psum"
            for (j, lo, hi, w2, rows, step) in hist.get(acc[1], []):
                if j == i: continue
                meet = lo < acc[4] and acc[3] < hi and (w or w2) and (lo - acc[3]) % math.gcd(step, _step(acc)) == 0
                if meet and rows != acc[2][0] and rows != slice(None) and acc[2][0] != slice(None): meet = False
                if ps and o["kind"] == "m" and ops[j]["kind"] == "m": deps.add(j)
                elif meet:
                    deps.add(j)
                    same = ops[j]["eng"] == o["eng"] and o["kind"] == "c" and ops[j]["kind"] == "c"
                    both = o["out"][0] == "i" and ops[j]["out"][0] == "i" if same else False
                    if not (same and w and (P["soft"] == 2 or (P["soft"] == 1 and both))): hard.add(j)
        for acc, w in [(a, False) for a in o["rd"]] + [(a, True) for a in o["wr"]]:
            hist.setdefault(acc[1], []).append((i, acc[3], acc[4], w, acc[2][0], _step(acc)))
        o["deps"], o["hard"] = deps, hard
        o["far"] = set(deps).union(*[ops[j]["far"] for j in deps])
        o["near"] = sorted(j for j in deps if ops[j]["kind"] in "rd" or not any(j in ops[k]["far"] for k in deps if ops[k]["kind"] in "cm" and k in hard))
        o["banks"] = sorted(set(a[1] for a in o["rd"] + o["wr"] if SCRATCH[a[1]][0] == "psum"))
    return ops


def graph(ops, speed):
    cy, ga, sca, lat, same, link, vfix, afix = speed
    cost, pre = [], []
    for i, o in enumerate(ops):
        c = o["cost"]
        if o.get("var"): c = FIX + (ga if o["var"][0] == "g" else sca) * o["var"][1] * cy
        elif o["kind"] == "m": c = (c - 60) * cy + (50 if o["stop"] else 10)
        elif o["kind"] == "c": c = max(AMIN, c - AFIX) * cy + afix if o["eng"] == "A" else c * cy + vfix
        cost.append(c)
        e = []
        for j in o["near"]:
            p = ops[j]
            if p["kind"] == "r": d = p["lat"] * link if o["kind"] == "a" else 0.0
            elif j not in o["hard"] or p["kind"] == "a": d = 0.0
            else: d = p["lat"] + (same if p["eng"] == o["eng"] else lat)
            e.append((j, d))
        pre.append(e)
    return cost, pre, lat


def place(ops, seq, cost, pre, lat, head):
    st, en = [0.0] * len(ops), [0.0] * len(ops)
    qs, bs = {e: [(-1e9, -1e9)] for e in "VAPGS"}, {"B%d" % b: [(-1e9, -1e9, "")] for b in range(8)}
    for i in seq:
        c, e, banks, t = cost[i], ops[i][0], ops[i][1], head[i]
        for j, d in pre[i]:
            if en[j] + d > t: t = en[j] + d
        if e != "X":
            q = qs[e]
            n = len(q)
            while True:
                p = n
                while q[p - 1][1] > t: p -= 1
                while p < n and q[p][0] < t + c - 1e-6:
                    t = q[p][1]; p += 1
                t0 = t
                for b in banks:
                    r = bs[b]
                    k = m = len(r)
                    while r[k - 1][1] + lat > t: k -= 1
                    while k < m and r[k][0] < t + c + lat:
                        if r[k][2] != e and t < r[k][1] + lat: t = r[k][1] + lat
                        k += 1
                if t == t0: break
            q.insert(p, (t, t + c))
            for b in banks:
                r = bs[b]
                k = len(r)
                while r[k - 1][0] > t: k -= 1
                r.insert(k, (t, t + c, e))
        st[i], en[i] = t, t + c
    return st, en


def in_turn(key, pre, order):
    key = list(key)
    for i in order:
        for j, _ in pre[i]:
            if key[j] >= key[i]: key[i] = key[j] + 1e-3
    return sorted(order, key=lambda i: key[i])


def turns(ops, order):
    last, out = {"B%d" % b: {} for b in range(8)}, [()] * len(ops)
    for i in order:
        e, banks = ops[i]["eng"], ops[i]["banks"]
        if banks:
            out[i] = [j for b in banks for e2, j in last[b].items() if e2 != e]
            for b in banks: last[b][e] = i
    return out


def replay(ops, order, turn, tail, cost, pre, lat):
    en, free, m = [0.0] * len(ops), dict.fromkeys("VAPGSX", 0.0), 0.0
    for i in order:
        e = ops[i]["eng"]
        t = free[e]
        for j, d in pre[i]:
            if en[j] + d > t: t = en[j] + d
        for j in turn[i]:
            if en[j] + lat > t: t = en[j] + lat
        t += cost[i]
        en[i] = t
        if e != "X": free[e] = t
        if t + tail[i] > m: m = t + tail[i]
    return m


def best_order(ops, tries, seed=1):
    n = len(ops)
    up, down, zero = list(range(n)), list(range(n - 1, -1, -1)), [0.0] * n
    gs = [graph(ops, s) for s in SPEEDS]
    cost, pre, lat = gs[0]
    suc = [[] for _ in up]
    for i in up:
        for j, d in pre[i]: suc[j].append((i, d))
    tail = [0.0 if o["kind"] == "r" else o["lat"] for o in ops]
    kin, stage = {}, {}
    for i, o in enumerate(ops):
        stage.setdefault(o["tag"], []).append(i)
        x = o.get("out") or ("v", o["name"], 0, 0)
        x = x[1] if x[0] == "i" else x
        o["kin"] = kin.setdefault((o["eng"], o.get("meth"), x[1].rstrip("0123456789"), x[3], len(o["rd"]), o["cost"]), [])
        o["kin"].append(i)
    x, bar, where = [seed], [1e9], [(o["eng"], o["banks"]) for o in ops]

    def rnd():
        x[0] = (x[0] * 6364136223846793005 + 1442695040888963407) % 2 ** 64
        return (x[0] >> 11) / 2.0 ** 53

    def forth(key):
        st, en = place(where, in_turn(key, pre, up), cost, pre, lat, zero)
        m = max(en[i] + tail[i] for i in up)
        if m > bar[0]: return 2 * m, st, en
        order = in_turn(st, pre, up)
        turn = turns(ops, order)
        ms = [m] + [replay(ops, order, turn, tail, *g) for g in gs[1:]]
        return sum(m * w for m, w in zip(ms, WEIGHTS)), st, en, order, ms

    def back(r):
        en = place(where, in_turn([-(r[2][i] + tail[i]) for i in up], suc, down), cost, suc, lat, tail)[1]
        return forth([-y for y in en])

    def tight(r):
        st, en, order = r[1:4]
        before, last, turn = {}, {}, turns(ops, order)
        for i in order:
            before[i] = last.get(ops[i]["eng"]); last[ops[i]["eng"]] = i
        i, out = max(up, key=lambda i: en[i] + tail[i]), []
        while True:
            c = [j for j, d in pre[i] if abs(en[j] + d - st[i]) < 0.01]
            if not c:
                c = [j for j in turn[i] if abs(en[j] + lat - st[i]) < 0.01]
                j = before[i]
                if j is not None and ops[i]["eng"] != "X" and abs(en[j] - st[i]) < 0.01: c.append(j)
                if not c: return out or [(0, 1)]
                out.append((c[0], i))
            i = c[0]
    chain = [None, None]
    long = list(tail)
    for i in down: long[i] = cost[i] + max([d + long[k] for k, d in suc[i]] + [tail[i]])
    long[0] += 1e6
    best = cur = forth([-y for y in long])
    for it in range(tries):
        key, u, i = list(cur[1]), rnd(), int(rnd() * n)
        d = (1 if rnd() < 0.5 else -1) * 10 ** (1.8 + 1.6 * rnd())
        if rnd() < CRIT:
            if chain[0] is not cur: chain[:] = [cur, tight(cur)]
            a, b = chain[1][int(rnd() * len(chain[1]))]
            i, d = (b, key[a] - key[b] - 1) if rnd() < 0.5 else (a, key[b] - key[a] + 1)
            if rnd() < 0.3: d *= 1 + 4 * rnd()
        some = set(ops[i]["kin"] if rnd() < 0.5 else [i])
        if u < 0.35:
            edge = set(some)
            for _ in range(1 + int(5 * rnd())):
                edge = set(j for a in sorted(edge) for j, _d in (pre if d < 0 else suc)[a] if abs(key[j] - key[a]) < abs(d) + 600 and rnd() < 0.8) - some
                some |= edge
        elif u < 0.6:
            for a in sorted(some):
                some |= set(j for j in stage[ops[a]["tag"]] if (j > a) == (d > 0))
        if u < 0.9:
            for j in some: key[j] += d
        else: key = [y + 120 * (rnd() - 0.5) for y in key]
        bar[0] = cur[4][0] + 700.0
        new = forth(key)
        if rnd() < 0.3: new = min(new, back(new), key=lambda r: r[0])
        if new[0] <= cur[0] + TEMP * (1 - it / tries) * -math.log(1 - rnd()): cur = new
        if new[0] < best[0]: best = new
    return best


def plan(P):
    ops = analyse(P)
    _, start, end, order, ms = best_order(ops, P["tries"])
    turn = turns(ops, order)
    cnt, known, sems = {}, {}, []
    for i in order:
        o = ops[i]
        o["deps"], o["hard"] = o["deps"] | set(turn[i]), o["hard"] | set(turn[i])
        o["t"] = start[i]
        if o["kind"] == "a":
            o["sig"] = ("a_" + o["name"], None); o["vc"] = {}; sems.append(o["sig"][0]); continue
        vc = known.setdefault(o["eng"], {})
        waits = []
        for j in sorted(o["hard"], key=lambda j: -end[j]):
            p = ops[j]
            if p["kind"] == "r":
                assert o["kind"] == "r"
                continue
            sem, val = p["sig"]
            if vc.get(sem, 0) >= (val or 1): continue
            waits.append(j)
            vc[sem] = val or 1
            for k2, x in p["vc"].items(): vc[k2] = max(vc.get(k2, 0), x)
        o["waits"] = waits; o["vc"] = dict(vc)
        if o["kind"] == "d":
            o["sig"] = ("d%d" % i, 16); sems.append(o["sig"][0])
        elif o["kind"] != "r":
            cnt[o["eng"]] = cnt.get(o["eng"], 0) + 1; o["sig"] = ("q" + o["eng"], cnt[o["eng"]])
    sems += ["q" + e for e in cnt] + ["sent"] + ["r_" + o["name"] for o in ops if o["kind"] == "r" and o["relays"] != [None]]
    return ops, order, cnt, sems


OPS, ORDER, COUNTS, SEMAPHORES = plan(PLAN)


def _mask(es):
    return sum(1 << e for e in es)


def _helpers(topo, T, src, dst):
    nxt = T.cores[(T.rank_of(src) + 1) % N]
    cs = [c for c in topo.cores_of(src) if c != src and topo.may_write(c, dst)]
    return sorted(cs, key=lambda c: (topo.die(c) != topo.die(src), topo.may_write(c, nxt), c))


def _hops(topo, T, src, o):
    if (src, o["name"]) not in _known: _known[src, o["name"]] = _find_hops(topo, T, src, o)
    return _known[src, o["name"]]


_known = {}


def _find_hops(topo, T, src, o):
    dst = T.cores[(T.rank_of(src) + o["to"]) % N]
    hs = _helpers(topo, T, src, dst)
    k, out = 0, []
    nrel = sum(isinstance(r, int) for r in o["relays"])
    for p, r in zip(o["parts"], o["relays"]):
        if r is None:
            out.append((p, dst, topo.engines(src, dst), False)); continue
        if isinstance(r, tuple):
            ms = [c for c in range(WORLD) if topo.mates(c, dst) and topo.may_write(c, dst) and topo.may_write(src, c)]
            h = sorted(ms, key=lambda c: (topo.die(c) != topo.die(src), c))[r[1]]
            out.append((p, h, topo.engines(src, h), True)); continue
        es = topo.engines(src, hs[r])
        if o["sel"] == "rest": es = [e for e in es if e not in topo.engines(hs[r], dst)]
        w = len(es) // nrel
        out.append((p, hs[r], es[k * w:k * w + w], True)); k += 1
    return dst, out


def rank_program(g, core, T, topo):
    def ap(a):
        if not _isv(a): return a
        if a[0] == "i": return ap(a[1]).indirect(ap(a[2]))
        if a[0] == "h": return T[a[1]][:] if a[2] is None else T[a[1]][:, a[2]:a[3]]
        return T[a[1]][a[2]]

    rank = T.rank_of(core)
    if rank is None:
        sent = 0
        for o in [OPS[i] for i in ORDER if OPS[i]["kind"] == "r"]:
            ways = [_hops(topo, T, src, o) for src in T.cores]
            for dst, p, es in [(dst, p, es) for dst, hops in ways for p, h, es, relayed in hops if relayed and h == core]:
                g.wait_ge(T.sem["r_" + o["name"]], len(es))
                rid, pid = topo.addr(dst, core)
                g.remote_dma(ap(p[1]), ap(p[1]), T.sem["a_" + o["arr"]], T.sem.sent, pid, rid, topo.mask(core, dst))
                sent += len(topo.engines(core, dst))
        if sent: g.wait_ge(T.sem.sent, sent)
        return

    q = {"V": g.vector, "A": g.scalar, "P": g.tensor, "G": g, "S": g.sync}
    sent = 0

    def total(o):
        n = 0
        for s in o["after"]:
            src = T.cores[(rank - OPS[s]["to"]) % N]
            n += sum(len(topo.engines(h, core)) if relayed else len(es) for p, h, es, relayed in _hops(topo, T, src, OPS[s])[1])
        return n

    for i in ORDER:
        o = OPS[i]
        if o["kind"] == "a": continue
        e = q[o["eng"]]
        for j in o["waits"]:
            sem, val = OPS[j]["sig"]
            e.wait_ge(T.sem[sem], total(OPS[j]) if val is None else val)
        if o["kind"] == "r":
            tr = []
            for p, h, es, relayed in _hops(topo, T, core, o)[1]:
                tr.append(topo.addr(h, core) + (_mask(es), p, T.sem["r_" + o["name"] if relayed else "a_" + o["arr"]]))
                sent += len(es)
            if len(tr) == 1:
                rid, pid, m, p, sem = tr[0]
                g.remote_dma(ap(p[1]), ap(p[0]), sem, T.sem.sent, pid, rid, m)
            else:
                g.remote_dma_fused([RemoteDMATransfer(dst_ids=[DstId(rid=rid, pnc=pid)], dma_engine_mask=m, remote_sem=sem,
                                                      src=ap(p[0]), dst=ap(p[1])) for rid, pid, m, p, sem in tr], local_sem=T.sem.sent)
            continue
        if o["kind"] == "m":
            k = len(o["pairs"])
            for j, (l, r, w) in enumerate(o["pairs"]):
                ins = e.matmul(ap(w), ap(l), ap(r), j == 0 and o["start"], j == k - 1 and o["stop"])
        else:
            args = [ap(o["out"])] + [ap(a) for a in o["args"]]
            kw = {k: ap(a) for k, a in o["kw"].items()}
            m = o["meth"]
            if m == "tensor_tensor": ins = e.tensor_tensor(*args)
            elif m == "tensor_scalar": ins = e.tensor_scalar(*args)
            elif m == "tensor_copy": ins = e.tensor_copy(*args)
            elif m == "tensor_tensor_scan": ins = e.tensor_tensor_scan(*args)
            elif m == "memset": ins = e.memset(*args)
            elif m == "activation": ins = e.activation(*args, **kw)
            elif m == "iota": ins = e.iota(*args)
            elif m == "affine_select": ins = e.affine_select(*args)
            else: ins = e.dma_start(*args, **kw)
        ins.then_inc(T.sem[o["sig"][0]], 16 if o["kind"] == "d" else 1)
    for o in OPS:
        if o["kind"] == "a": g.wait_ge(T.sem[o["sig"][0]], total(o))
    g.wait_ge(T.sem.sent, sent)
    for k, c in COUNTS.items():
        g.wait_ge(T.sem["q" + k], c)
    for i in ORDER:
        if OPS[i]["kind"] == "d": g.wait_ge(T.sem[OPS[i]["sig"][0]], 16)
